import numpy as np, ml_dtypes
CORES = [9,25,41,57]
N = 4
BF = ml_dtypes.bfloat16
C, WS, WE, CAP, RO = 256, 4096, 4096, 64, 4
M, H = 16 * C, 8 * C
PL = np.arange(16)[:, None]
def tables(rng):
    amp = rng.choice(np.array([30, 100, 255]), (N, 8, 1, 1))
    e = np.floor((2 * rng.random((N, 8, 16, WS)) - 1) * amp).astype(np.int64)
    return np.clip(rng.integers(0, 256, (N, 8, 1, WS)) + e, 0, 255), rng.integers(0, 64, (N, 8, 16, WE)), rng.integers(0, 16, (N, 8, 16, 2))
def still(rng):
    return rng.integers(0, 41, (N, 8, 16, WS)), rng.integers(41, 64, (N, 8, 16, WE)), rng.integers(0, 16, (N, 8, 16, 2))
def chains(rng, K, keys, td):
    L = np.full((N, 8, 16, C), -1, np.int64); n = np.zeros((N, 8, C), np.int64)
    for g in range(8):
        low = [rng.permutation(H)[:int(K[g, r])] for r in range(N)]
        for r in range(N):
            lo = low[r]; hi = rng.permutation(low[(r - 1) % N]) + H
            o = np.argsort(keys[r, g].reshape(-1))[:len(lo) + len(hi) - 4 * C]
            m = 4 + np.bincount(o // 12, minlength=C)
            c0 = np.flatnonzero(td[r, g] == 0); c1 = np.flatnonzero(td[r, g] == 1)
            A = np.full((16, C), -1, np.int64)
            A[m[c0] - 1, c0] = lo[:len(c0)]; A[m[c1] - 1, c1] = hi[:len(c1)]
            A[(PL < m) & (A < 0)] = rng.permutation(np.concatenate([lo[len(c0):], hi[len(c1):]]))
            L[r, g] = A; n[r, g] = m
    return L, n
def monos(rng, n, low):
    z = rng.integers(0, 64, (N, 8, 16, C)); t = np.where(low, rng.integers(0, 8, low.shape), rng.integers(8, 64, low.shape))
    return np.where(PL == n[:, :, None, :] - 1, t[:, :, None, :], z)
def pack(tb, L, n, z):
    z = np.where(PL < n[:, :, None, :], z, 0); b = [np.ascontiguousarray(v.reshape(N, 128, -1)).astype(np.float32).astype(BF) for v in tb]
    return {"spr": b[0], "bar": b[1], "wt": b[2], "lam": np.ascontiguousarray(L.reshape(N, 128, C)).astype(np.int32), "mon": np.ascontiguousarray(z.reshape(N, 128, C)).astype(np.int32), "cnt": n.astype(np.int32)}
def anyway():
    return np.full((N, 8, C), -1)
def bring(A, v, k, c):
    i, j = np.nonzero(A == v); i, j = int(i[0]), int(j[0])
    A[i, j] = A[k, c]; A[k, c] = v
def crowd(rng, spr, wt, L, n, z):
    spr[:, 4, 0] = rng.integers(0, 256, (N, WS)); spr[:, 4, 1] = 32
    wt[:, 4] = 0; wt[:, 4, 0, 0] = 1; wt[:, 4, 1, 1] = 1
    for r in range(0, N, 2):
        A, A1 = L[r, 4], L[r + 1, 4]; v = int(np.min(A[A >= 0])); A1[A1 == v + H] = H; A[A == v] = 0
    tails = {}
    for s in range(1, N, 2):
        A = L[s, 4]; x = rng.permutation(A[A >= 0]); x = rng.permutation(x[np.unique(x >> 3, return_index=True)[1]])
        lo = x[x < H][:CAP]; hi = np.concatenate([np.array([H]), x[(x >= H) & ((x >> 3) != C)]])[:CAP]; tails[s] = (lo, hi)
        for v, c in zip(np.concatenate([lo, hi]), rng.permutation(C)):
            k = int(n[s, 4, c]) - 1; bring(L[s, 4], v, k, c); z[s, 4, k, c] = 0
    for r in range(0, N, 2):
        s0, s1 = (r - 1) % N, r + 1; lo, hi = tails[s0][0], tails[s1][1]
        o = 1 + rng.permutation(C - 2); a = np.concatenate([np.array([C - 1]), o[:2 * CAP - 1]]); q = np.insert(o[2 * CAP - 1:4 * CAP - 2], CAP, 0)
        for m, v in enumerate(np.concatenate([lo + H, hi - H])):
            bring(L[r, 4], v, 15 if m == 0 else int(rng.integers(0, n[r, 4, a[m]])), a[m])
        spr[s0, 4, 0, lo >> 3] = q[:CAP]; spr[s1, 4, 0, hi >> 3] = q[CAP:]; spr[s1, 4, :, C] = 0
def setup_inputs(rng):
    L, n = chains(rng, rng.integers(3 * C, 6 * C + 1, (8, N)), rng.random((N, 8, C, 12)) + 0.4 * rng.random((N, 8, C, 1)), anyway())
    low = rng.random((N, 8, C)) < rng.choice(np.array([0.1, 0.3, 0.5, 0.8]), (N, 8, 1))
    return pack(tables(rng), L, n, monos(rng, n, low))
def setup_inputs_room(rng):
    ch = np.array([0, 1, CAP - 1, CAP, CAP + 1, C // 2]); td = anyway(); low = np.zeros((N, 8, C), bool)
    for r in range(N):
        for g in range(8):
            a, b = int(rng.choice(ch)), int(rng.choice(ch))
            if r == 0: a, b = (CAP, CAP + 1, CAP - 1, 1, 0, C // 2, CAP, CAP + 1)[g], (CAP + 1, CAP, C // 2, 0, 1, CAP - 1, CAP + 1, CAP)[g]
            o = rng.permutation(C); td[r, g, o[:a]] = 0; td[r, g, o[a:a + b]] = 1; low[r, g, o[:a + b]] = True
    L, n = chains(rng, rng.integers(3 * C, 6 * C + 1, (8, N)), rng.random((N, 8, C, 12)), td)
    return pack(still(rng), L, n, monos(rng, n, low))
def setup_inputs_ties(rng):
    spr, bar, wt = tables(rng)
    for r in range(N):
        for g in range(8):
            P = int(rng.choice(np.array([4, 16, 64])))
            if r == 0: P = (4, 16, 64, 4, 16, 64, 16, 4)[g]
            top = np.argsort(np.argsort(rng.random((16, P)), axis=0), axis=0) < rng.integers(7, 11, (1, P))
            pat = rng.integers(0, 101, (16, 1)) + np.where(top, rng.choice(np.array([20, 21, 40]), (1, P)), 0)
            pat[:, 0] = pat[:, 0] - np.where(top[:, 0], pat[:, 0] - np.min(pat, axis=1), 0)
            spr[r, g] = pat[:, np.where(rng.random(WS) < 0.4, 0, rng.integers(0, P, WS))]
    bar = np.broadcast_to(rng.choice(np.array([0, 19, 20, 21, 40]), (N, 8, 1, WE)), bar.shape)
    L, n = chains(rng, rng.integers(3 * C, 6 * C + 1, (8, N)), rng.random((N, 8, C, 12)), anyway())
    return pack((spr, bar, wt), L, n, rng.choice(np.array([0, 1, 7, 8, 9, 15, 16, 56, 60, 63]), (N, 8, 16, C)))
def setup_inputs_clash(rng):
    spr, bar, wt = still(rng); wt[:, :3, :, 0] = 0; wt[:, 3] = 0; wt[:, 3, 0] = 1; wt[:, 3, 1] = rng.integers(0, 3, (N, 2))
    spr[::2, 5] = rng.integers(0, 2, (N // 2, 16, WS)); spr[1::2, 5] = rng.integers(245, 256, (N // 2, 16, WS))
    wt[1::2, 5, :, 0] = np.where(np.arange(16) < 12, 15, 10); wt[1::2, 5, 0, 1] = 15
    keys = rng.random((N, 8, C, 12)) + 2 * rng.integers(0, 2, (N, 8, C, 1))
    keys[:, 0:3:2, 0, :6] = -1; keys[:, 0:3:2, 0, 6:] = 9; keys[:, 1, 0] = -1
    keys[:, 4:6] = rng.random((N, 2, C, 12)); keys[:, 4:6, :, 0] = -1; keys[:, 4:6, :, 11] = 9
    keys[::2, 4, C - 1] = -1
    L, n = chains(rng, rng.integers(3 * C, 6 * C + 1, (8, N)), keys, anyway())
    for r in range(N):
        kk, cc = np.nonzero(L[r, 0] >= H); i = int(rng.integers(0, len(kk))); v = int(L[r, 0, kk[i], cc[i]])
        L[r, 0, kk[i], cc[i]] = L[r, 0, 0, 0]; L[r, 0, 0, 0] = v
    for r in range(N):
        v = int(L[(r + 1) % N, 0, 0, 0]) - H; kk, cc = np.nonzero(L[r, 0] == v); t = int(n[r, 0, 1]) - 1
        L[r, 0, kk[0], cc[0]] = L[r, 0, t, 1]; L[r, 0, t, 1] = v
    low = rng.random((N, 8, C)) < 0.3; low[:, :3, 0] = False; low[:, :3, 1] = True
    low[:, 4] = False; low[::2, 5] = False; low[1::2, 5] = rng.random((N // 2, C)) < 0.5
    z = monos(rng, n, low); crowd(rng, spr, wt, L, n, z)
    return pack((spr, bar, wt), L, n, z)
def setup_inputs_full(rng):
    K = rng.integers(2 * C, 8 * C + 1, (8, N)); o = rng.permutation(8)
    K[o[0]] = 8 * C; K[o[1]] = 2 * C; K[o[2]] = np.where(np.arange(N) % 2 == 0, 2 * C, 8 * C)
    L, n = chains(rng, K, rng.random((N, 8, C, 12)), anyway())
    low = rng.random((N, 8, C)) < rng.choice(np.array([0.0, 0.05, 0.2, 1.0]), (N, 8, 1))
    return pack(tables(rng), L, n, monos(rng, n, low))
def setup_inputs_spread(rng):
    spr = np.minimum(np.exp2(8 * rng.random((N, 8, 1, WS))) * (0.25 + rng.random((N, 8, 16, WS))), 255).astype(np.int64)
    bar = (np.exp2(6 * rng.random((N, 8, 16, WE))) - 1).astype(np.int64); wt = (np.exp2(4 * rng.random((N, 8, 16, 2))) - 1).astype(np.int64)
    L, n = chains(rng, rng.integers(2 * C, 8 * C + 1, (8, N)), rng.random((N, 8, C, 12)) + 1.5 * rng.random((N, 8, C, 1)), anyway())
    z = np.where(rng.random((N, 8, 1, C)) < 0.5, (64 * rng.random((N, 8, 16, C)) ** 4).astype(np.int64), 63 - (64 * rng.random((N, 8, 16, C)) ** 4).astype(np.int64))
    return pack((spr, bar, wt), L, n, z)
def check_inputs(d):
    bad = []
    for k, lo, hi in (("spr", 0, 255), ("bar", 0, 63), ("wt", 0, 15), ("lam", -1, M - 1), ("mon", 0, 63), ("cnt", 4, 16)):
        v = np.asarray(d[k]).astype(np.float64)
        if not np.all((v >= lo) & (v <= hi) & (v == np.floor(v))): bad.append("range of " + k)
    L = np.asarray(d["lam"]).astype(np.int64).reshape(N, 8, 16, C); z = np.asarray(d["mon"]).reshape(N, 8, 16, C); ok = PL < np.asarray(d["cnt"])[:, :, None, :]
    if np.any((L >= 0) != ok) or np.any((L != -1) & ~ok): bad.append("places of lam")
    if np.any((z != 0) & ~ok): bad.append("empty places of mon")
    have = np.zeros((N, 8, M), np.int64); r, g, k, c = np.nonzero(ok); np.add.at(have, (r, g, np.clip(L[r, g, k, c], 0, M - 1)), 1)
    if np.any(have > 1): bad.append("a name stands twice")
    if np.any(have[:, :, :H] != np.roll(have[:, :, H:], -1, axis=0)): bad.append("twins")
    return bad
def reference(spr, bar, wt, lam, mon, cnt):
    S, B, w = [v.astype(np.float32).astype(np.int64).reshape(N, 8, 16, -1) for v in (spr, bar, wt)]
    L = lam.astype(np.int64).reshape(N, 8, 16, C); z = mon.astype(np.int64).reshape(N, 8, 16, C); n = cnt.astype(np.int64)
    for t in range(RO):
        ok = PL < n[:, :, None, :]; x = np.where(ok, L, 0)
        i = ((((x + 77 * t) & (M - 1)) * (2 * z + 1)) >> 3) & (WS - 1)
        j = (((x[:, :, 1:] * (z[:, :, :-1] + 64)) >> 5) + 811 * z[:, :, 1:]) & (WE - 1)
        F = np.take_along_axis(S, i.reshape(N, 8, 1, 16 * C), 3).reshape(N, 8, 16, 16, C)
        E = np.take_along_axis(B, j.reshape(N, 8, 1, 15 * C), 3).reshape(N, 8, 16, 15, C)
        D = F[:, :, :, 1:] - F[:, :, :, :-1]
        up = np.add.reduce((D > E).astype(np.int64), axis=2) >= 9; down = np.add.reduce((-D > E).astype(np.int64), axis=2) >= 9
        s = np.zeros((N, 8, 17, C), np.int64); s[:, :, 1:16] = np.where(ok[:, :, 1:], 8 * up.astype(np.int64) - 8 * down.astype(np.int64), 0)
        z = np.where(ok, np.clip(z + s[:, :, :16] - s[:, :, 1:], 0, 63), 0)
        last = n - 1; zl = np.take_along_axis(z, last[:, :, None, :], 2)[:, :, 0]; ll = np.take_along_axis(L, last[:, :, None, :], 2)[:, :, 0]
        f = np.take_along_axis(F, last[:, :, None, None, :], 3)[:, :, :, 0]
        u1 = np.add.reduce(w[..., 0:1] * f, axis=2); u2 = np.add.reduce(w[..., 1:2] * f, axis=2)
        qn = (((u1 & 4095) * (u2 & 4095)) >> 5) & (C - 1)
        ev = [(zl < 8) & (ll < H), (zl < 8) & (ll >= H)]
        ev = [e & (np.add.accumulate(e.astype(np.int64), axis=2) <= CAP) for e in ev]
        sends = ev[0] | ev[1]
        moved = np.zeros((N, 8, C), bool); src = np.broadcast_to(PL, L.shape).copy(); grow = np.zeros((N, 8, C), np.int64); put = []
        for r in range(N):
            for g in range(8):
                p0, p1 = (r - 1) % N, (r + 1) % N
                a0 = np.flatnonzero(ev[0][p0, g]); a1 = np.flatnonzero(ev[1][p1, g])
                home = np.concatenate([np.full(len(a0), p0), np.full(len(a1), p1)]); hc = np.concatenate([a0, a1])
                name = np.concatenate([ll[p0, g, a0] + H, ll[p1, g, a1] - H]); q = qn[home, g, hc]; fm = f[home, g, :, hc].T
                kk, cc = np.nonzero(ok[r, g]); inv = np.zeros(M, np.int64); inv[L[r, g, kk, cc]] = 16 * cc + kk
                a = inv[name] >> 4; p = inv[name] & 15; m = np.arange(len(a))
                first = np.full(C, len(a)); np.minimum.at(first, a, m); np.minimum.at(first, q, m)
                good = (n[r, g, a] > 4) & (a != q) & (n[r, g, q] < 16) & ~sends[r, g, a] & ~sends[r, g, q] & (first[a] == m) & (first[q] == m)
                a, p, q, name, fm, home, hc = a[good], p[good], q[good], name[good], fm[:, good], home[good], hc[good]
                dist = np.add.reduce(np.abs(F[r, g][:, :, q] - fm[:, None, :]), axis=0)
                b = np.argmin(np.where(PL < n[r, g, q], dist, 2 ** 20), axis=0)
                moved[home, g, hc] = True
                src[r, g][:, a] = PL + (PL >= p); src[r, g][:, q] = PL - (PL > b)
                grow[r, g, a] = -1; grow[r, g, q] = 1; put.append((r, g, b, q, name))
        src = np.minimum(np.where(moved[:, :, None, :], np.where(PL == 0, last[:, :, None, :], PL - 1), src), 15)
        L = np.take_along_axis(L, src, 2); z = np.take_along_axis(z, src, 2)
        z[:, :, 0] = np.where(moved, 16, z[:, :, 0])
        for r, g, b, q, name in put:
            L[r, g, b, q] = name; z[r, g, b, q] = 16
        n = n + grow; ok = PL < n[:, :, None, :]; L = np.where(ok, L, -1); z = np.where(ok, z, 0)
    return {"yl": L.reshape(N, 128, C).astype(np.float32), "yz": z.reshape(N, 128, C).astype(np.float32), "yn": n.astype(np.float32)}

@@ -1,0 +1,649 @@
+import math
+from concourse.bass import DstId, RemoteDMATransfer
+from concourse.mybir import AluOpType as A, ActivationFunctionType as AF
+
+RO = 4
+CEN = 256
+MAGIC = 12582912.0
+BF, F32, I32, U16 = "bfloat16", "float32", "int32", "uint16"
+P = {"it": 6000, "rnd": 200.0, "tol": 60.0, "NS": 6, "VF0": 2, "cyc": 1.0, "pe": 0.52, "g": 1.56, "sc": 3.8, "hop": 110.0, "self": 70.0, "net": 2600.0,
+     "CH": [(32 * c, 32 * c + 32) for c in range(7)] + [(224, 240), (240, 256)], "FA": (0, 0, 2, 4), "TA": 4, "SL": 224,
+     "tw": 4, "u1": 1000.0, "u2": 500.0, "u3": 500.0}
+
+SB = {}
+for _d, _l in ((BF, "spr_s 4096 bar_s 4096 wt_s 2 wB 256 vB 256 Fb 4128 E 4096 nE 4096 UD 8192 tmB 256 thi 256 fT 256 qrow 256 hiB 256 su 512 "
+                    "dany 256 dhi 256 cum 256 key 256 w1B 256 ovB 256 ST 528 tabB 272 AW 784 metaB 128 R 256 OH 4096 SG 256 eqB 128 Fq 2048 Mx 2048 "
+                    "tq 128 mT 128 CB 4608 ZB 1008 G8 24 ONES 256 KEEP 256 C1 16 CN 128 TABq 256 GB0 128 GB1 128 GB2 128 GB3 128"),
+               (F32, "Y 520 P2f 256 xs 256 pack 256 Wf 24 Dif 24 L3f 24 nmS 128 Yaq 256 Dd 128 ta 128 Dq 128 pm 128 Aq 128 Yn 128 tm2 256 qF 128 "
+                     "inv 8320 cval 4096 o1 256 o2 256 o3 256 o4 256 mg 128 jj 144 col 40 wtf 2 CF 896 tA 256 tB 256 RST 128 ordr 128 thr 128 "
+                     "ordc 8 wc 8 DUM 24 SW0 776 SW1 776 SW2 776 SW3 776 LB0 128 LB1 128 LB2 128 LB3 128"),
+               (I32, "lam_s 256 mon_s 256 Yi 256 xt 256 w 256 P1 256 x 264 P2 256 uI 32 uP 16 Jt 256 pI 2"),
+               (U16, "iF 256 iE 256 tlW 16 qS 16 offW 16 lq 128 nmW 8 AQ 16 L3 24 offI 256")):
+    _w = _l.split()
+    for _i in range(0, len(_w), 2):
+        SB[_w[_i]] = (int(_w[_i + 1]), _d)
+SCRATCH = {k: ("sbuf", [128, n], d) for k, (n, d) in SB.items()}
+for _b in range(8):
+    SCRATCH["PS%d" % _b] = ("psum", [128, 512], F32)
+SEMAPHORES = ["cV", "cS", "cP", "cG", "ls", "m0", "m1", "k0", "k1", "d0", "d1", "d2", "d3", "d4", "d5", "d6", "d7"]
+PLAN = {}
+
+
+def build(g, core, T, topo):
+    rank = T.rank_of(core)
+    n = len(T.cores)
+    nxt, prv = T.cores[(rank + 1) % n], T.cores[(rank - 1) % n]
+    ops = []
+    acc = {}
+    fixed = set()
+    now = [0]
+
+    def v(name, lo=0, hi=None, st=1, p=128):
+        if hi is None:
+            hi = SB[name][0]
+        t = T[name]
+        ap = t[0:p, lo:hi] if st == 1 else t[0:p, lo:hi:st]
+        dtp = SB[name][1] if name in SB else F32
+        return {"ap": ap, "r": [(name, lo, hi, lo % 2 if st % 2 == 0 else None)], "n": len(range(lo, hi, st)), "two": dtp in (BF, U16),
+                "ps": name not in SB, "ind": False, "f32": dtp == F32}
+
+    def ind(win, off):
+        return {"ap": win["ap"].indirect(off["ap"]), "r": win["r"], "o": off["r"], "n": 16 * off["n"], "two": win["two"], "ps": False, "ind": True}
+
+    def add(eng, fn, rd, wr, cost, sig=None, lat=0.0, extra=()):
+        i = len(ops)
+        deps = {}
+        rr, ww = [], []
+        for a in rd:
+            rr += a["r"] + a.get("o", [])
+        for a in wr:
+            ww += a["r"]
+            rr += a.get("o", [])
+        for lst, isw in ((rr, False), (ww, True)):
+            for (nm, lo, hi, pa) in lst:
+                for (j, l2, h2, w2, e2, p2) in acc.get(nm, []):
+                    ov = l2 < hi and lo < h2 and (pa is None or p2 is None or pa == p2)
+                    if nm not in SB and e2 != eng:
+                        deps[j] = True
+                    elif ov and (w2 or isw):
+                        deps[j] = deps.get(j, False) or e2 != eng or eng != "P"
+        for j in extra:
+            deps[j] = True
+        for lst, isw in ((rr, False), (ww, True)):
+            for (nm, lo, hi, pa) in lst:
+                old = acc.get(nm, [])
+                if isw and nm in SB and pa is None:
+                    old = [e for e in old if not (lo <= e[1] and e[2] <= hi)]
+                if isw or nm not in fixed:
+                    acc[nm] = (old if nm in SB else old[-150:]) + [(i, lo, hi, isw, eng, pa)]
+        ops.append({"eng": eng, "fn": fn, "deps": deps, "cost": cost, "sig": sig, "lat": lat, "up": 0.0, "t": now[0],
+                    "tag": (eng == "N", tuple((r[0][:2] if r[0][:2] in ("SW", "LB", "GB") else r[0], r[1]) for r in ww + rr))})
+        return i
+
+    def vcost(out, ins, two=1.0):
+        nn = max(a["n"] for a in ins + [out])
+        if out["ind"]:
+            return 50 + nn * P["sc"] * P["cyc"]
+        if any(a["ind"] for a in ins):
+            return 50 + nn * P["g"] * P["cyc"]
+        if two == 1.0 and out["two"] and all(a["two"] for a in ins):
+            two = 0.5
+        return max(64, nn * two) * P["cyc"]
+
+    def sc(s):
+        return s["ap"] if isinstance(s, dict) else s
+
+    def cols(*s):
+        return [a for a in s if isinstance(a, dict)]
+
+    def ts(out, in0, s1, op0, s2=None, op1=None):
+        if op1 is None:
+            fn = lambda: g.vector.tensor_scalar(out["ap"], in0["ap"], sc(s1), None, op0)
+        else:
+            fn = lambda: g.vector.tensor_scalar(out["ap"], in0["ap"], sc(s1), sc(s2), op0, op1)
+        return add("V", fn, [in0] + cols(s1, s2), [out], vcost(out, [in0]))
+
+    def tt(out, a, b, op):
+        return add("V", lambda: g.vector.tensor_tensor(out["ap"], a["ap"], b["ap"], op), [a, b], [out],
+                   vcost(out, [a, b], 1.01 if a["ps"] or b["ps"] else 2.0))
+
+    def cp(out, a):
+        return add("V", lambda: g.vector.tensor_copy(out["ap"], a["ap"]), [a], [out], vcost(out, [a]))
+
+    def ms(out, c):
+        return add("V", lambda: g.vector.memset(out["ap"], c), [], [out], vcost(out, []))
+
+    def scan(out, d0, d1, op0, op1, ini=0.0):
+        return add("V", lambda: g.vector.tensor_tensor_scan(out["ap"], d0["ap"], d1["ap"], sc(ini), op0, op1), [d0, d1] + cols(ini), [out],
+                   vcost(out, [d0, d1]))
+
+    def act(out, a, func=AF.Identity, bias=None, scale=None, more=0.0):
+        kw = {}
+        if bias is not None:
+            kw["bias"] = sc(bias)
+        if scale is not None:
+            kw["scale"] = sc(scale)
+        c = 65 + a["n"] * P["cyc"] * (P["sc"] if out["ind"] else P["g"] if a["ind"] else 1.0) + more
+        return add("S", lambda: g.scalar.activation(out["ap"], a["ap"], func, **kw), [a] + cols(bias, scale), [out], c)
+
+    def mm(items, first=True, last=True):
+        def fn():
+            r = None
+            for i, (o, l, x) in enumerate(items):
+                r = g.tensor.matmul(o["ap"], l["ap"], x["ap"], first and i == 0, last and i == len(items) - 1)
+            return r
+        c = sum(max(min(64, l["n"]), x["n"]) * (4 if x["f32"] else 1) for (o, l, x) in items) * P["pe"]
+        return add("P", fn, [a for it in items for a in it[1:]], [it[0] for it in items], c, lat=60.0)
+
+    def iota(out, pat, base, cm):
+        if out["f32"]:
+            fn = lambda: g.iota(out["ap"], pat, base, cm, allow_small_or_imprecise_dtypes=True)
+        else:
+            fn = lambda: g.iota(out["ap"], pat, base, cm)
+        return add("G", fn, [], [out], 160 + 2 * out["n"] * P["cyc"])
+
+    def sel(out, a, pat, op, fill, base, cm):
+        return add("G", lambda: g.affine_select(out["ap"], a["ap"], pat, op, fill, base, cm), [a], [out], 200 + 2 * out["n"] * P["cyc"])
+
+    def dma(q, out, in_, rd, wr, sem, lat):
+        e = g.sync if q == "Y" else g.scalar
+        return add(q, lambda: e.dma_start(out, in_).then_inc(T.sem[sem], 16), rd, wr, 60, sig=(sem, 16), lat=lat)
+
+    col = lambda j: v("col", j, j + 1)
+    cb = lambda j: v("CB", 128 * j, 128 * j + 128)
+    cf = lambda j: v("CF", 128 * j, 128 * j + 128)
+    zb = lambda j, k: v("ZB", 144 * j + 15 - k, 144 * j + 143 - k)
+    ps = lambda b, lo=0, hi=256, st=1: v("PS%d" % b, lo, hi, st)
+
+    d0 = dma("Y", T.lam_s[:], T.lam[:], [], [v("lam_s")], "d0", 2200)
+    dma("S", T.mon_s[:], T.mon[:], [], [v("mon_s")], "d1", 2200)
+    dma("S", T.wt_s[:], T.wt[:], [], [v("wt_s")], "d2", 2200)
+    d3 = dma("Y", T.spr_s[:], T.spr[:], [], [v("spr_s")], "d3", 6500)
+    d4 = dma("Y", T.bar_s[:], T.bar[:], [], [v("bar_s")], "d4", 11000)
+    ops[d3]["deps"][d0] = False
+    ops[d4]["deps"][d3] = False
+
+    Y = v("Y", 0, 256)
+    X = v("x", 0, 256)
+    iota(v("Jt"), [[16, 256]], 4112, 1)
+    ts(X, v("lam_s"), 16383, A.bitwise_and)
+    tt(v("Jt"), v("Jt"), X, A.min)
+    cp(v("offI"), v("Jt"))
+    ts(v("o1"), v("mon_s"), 2.0, A.mult, 1.0, A.add)
+    ts(v("o2"), X, 128.0, A.mult)
+    tt(Y, v("o1"), v("o2"), A.add)
+
+    iota(v("pI", 0, 1), [[0, 1]], 0, 1)
+    iota(v("mg"), [[1, 8], [0, 16]], 0, 0)
+    iota(v("jj"), [[1, 144]], 0, 0)
+    iota(v("tA"), [[1, 16], [0, 16]], 0, 0)
+    iota(v("tB"), [[0, 16], [1, 16]], 0, 0)
+    iota(v("ordr", 0, 64), [[1, 64]], 0, 0)
+    iota(v("ordr", 64, 128), [[-1, 64]], 127, 0)
+    K, GR, GE, TL, KV, M0, M2, M3, M4, M15, RO_, RN, RQ, ROV, KP, BPK, B15, DLO, DHI, T2, QK, T1 = range(22)
+    ts(v("pI", 1, 2), v("pI", 0, 1), 15, A.bitwise_and)
+    cp(col(K), v("pI", 1, 2))
+    ts(v("pI", 1, 2), v("pI", 0, 1), 4, A.logical_shift_right)
+    cp(col(GR), v("pI", 1, 2))
+    ts(col(GE), col(GR), 16.0, A.mult, 15.0, A.add)
+    ts(col(TL), col(K), 16.0, A.mult, -1.0, A.add)
+    ts(col(KV), col(K), 1048576.0, A.add)
+    ts(col(QK), col(K), -16.0 * 2448, A.add)
+    for j, k in ((M0, 0), (M2, 2), (M3, 3), (M15, 15)):
+        ts(col(j), col(K), float(k), A.is_equal)
+    tmp = [T1]
+
+    def lin(dst, terms):
+        ts(col(dst), col(K), float(terms[0][0]), A.is_equal, float(terms[0][1]), A.mult)
+        for k, wgt in terms[1:]:
+            ts(col(tmp[0]), col(K), float(k), A.is_equal, float(wgt), A.mult)
+            ts(col(dst), col(dst), col(tmp[0]), A.add)
+            tmp[0] += 1
+    lin(M4, [(4, -1)])
+    lin(RO_, [(0, 1), (4, -1), (8, 1), (12, 256)])
+    lin(RN, [(0, 64), (1, 1)])
+    lin(RQ, [(2, 16), (3, 1)])
+    lin(ROV, [(0, -1), (4, -1)])
+    ts(col(KP), col(K), 12.0, A.is_lt)
+    lin(BPK, [(0, -40960), (1, 2621440)])
+    lin(B15, [(15, 524289)])
+    lin(DLO, [(0, 256 * 32), (2, 256 * 16)])
+    lin(DHI, [(0, 256 * 96), (2, 256 * 16)])
+    cp(v("wtf"), v("wt_s"))
+    (BO, ID, NI, H100, SUPH, C40, K1, K2, C2032, T64, W16, W16N, MA, MB, MC, MH, I256, SUPT, LT, RSA, RQB, RNB, R15, ROVB, NI256, C2304, B16,
+     SUP, SDN, BSI, BDI, C8, C4, E0, E1, TM) = range(36)
+    (FI, FBO, FMX, FSI, FXS, FDI, FN128) = range(7)
+    dif, pl = [[1, 128]], [[0, 8], [1, 16]]
+    ts(cb(BO), v("mg"), col(GR), A.is_equal)
+    sel(cb(ID), cb(BO), dif, A.is_equal, 0.0, 0, -1)
+    sel(cb(SUP), cb(BO), dif, A.is_equal, 0.0, -1, -1)
+    sel(cb(SDN), cb(BO), dif, A.is_equal, 0.0, 1, -1)
+    sel(cb(BSI), cb(SUP), dif, A.not_equal, -1.0, 0, -1)
+    sel(cb(BDI), cb(SDN), dif, A.not_equal, -1.0, 0, -1)
+    sel(cb(LT), cb(BO), dif, A.is_ge, 0.0, 0, -1)
+    sel(cb(C8), cb(BO), pl, A.is_ge, 0.0, -8, 0)
+    sel(cb(C4), cb(BO), [[0, 8], [-1, 16]], A.is_ge, 0.0, 3, 0)
+    sel(cb(E0), cb(BO), pl, A.is_equal, 0.0, 0, 0)
+    sel(cb(E1), cb(BO), pl, A.is_equal, 0.0, -1, 0)
+    for d, s, c in ((NI, ID, -1.0), (H100, ID, 100.0), (K1, ID, 12288.0), (K2, ID, 688.0), (I256, ID, 256.0), (C40, BO, 2.5), (C2032, BO, 2032.0),
+                    (SUPH, SUP, 0.5), (T64, BDI, -64.0), (W16, BDI, -16.0), (W16N, BDI, 16.0), (MC, C8, 1.0 / 16), (NI256, ID, -256.0),
+                    (C2304, BO, 2304.0), (B16, BO, 1.0 / 16), (RSA, BO, col(M4)), (RQB, BO, col(RQ)), (RNB, BO, col(RN)), (R15, BO, col(M15)),
+                    (ROVB, BO, col(ROV))):
+        ts(cb(d), cb(s), c, A.mult)
+    for d, s, c in ((FI, ID, 1.0), (FN128, ID, -128.0), (FBO, BO, 1.0 / 64), (FSI, BSI, 1.0), (FDI, BDI, 1.0), (FMX, E1, 4.0)):
+        act(cf(d), cb(s), scale=c)
+    tt(cb(MA), cb(C4), cb(C8), A.subtract)
+    ts(cb(TM), cb(C4), -2.0, A.mult)
+    tt(cb(TM), cb(TM), cb(BO), A.add)
+    tt(cb(MB), cb(TM), cb(C8), A.subtract)
+    tt(cb(TM), cb(E0), cb(SUP), A.subtract)
+    act(cf(FXS), cb(TM), scale=2.0)
+    ms(cb(TM), 0.0)
+    ts(cb(C4), cb(E0), 33.0 / 64, A.mult)
+    ts(cb(SUPT), cb(SUP), 8192.0, A.mult)
+    tt(cb(SUPT), cb(SUPT), cb(C4), A.add)
+    ts(cb(E1), cb(E1), -64.0, A.mult)
+    tt(cb(E1), cb(E1), cb(E0), A.add)
+    ts(cb(MH), cb(E1), col(M0), A.mult, 256.0, A.mult)
+    Z1, ZW1, ZW2, ZO, ZN, ZQ, Z0 = range(7)
+    zf = lambda j: v("ZB", 144 * j, 144 * j + 144)
+    ts(zf(Z1), v("jj"), col(GE), A.is_equal)
+    for j, s in ((ZW1, v("wtf", 0, 1)), (ZW2, v("wtf", 1, 2)), (ZO, col(RO_)), (ZN, col(RN)), (ZQ, col(RQ)), (Z0, col(M0))):
+        ts(zf(j), zf(Z1), s, A.mult)
+    ts(v("G8", 0, 8), v("jj", 0, 8), col(GR), A.is_equal)
+    ts(v("G8", 8, 16), v("G8", 0, 8), -16.0, A.mult)
+    ts(v("G8", 16, 24), v("G8", 0, 8), 32.0, A.mult)
+    ms(v("ONES"), 1.0)
+    act(v("KEEP"), v("ONES"), scale=col(KP))
+    ts(v("C1"), v("jj", 0, 16), 16.0, A.mult)
+    ms(v("CN", 0, 64), 128.0)
+    ms(v("CN", 64, 128), -128.0)
+    act(v("tA"), v("tA"), scale=col(M2))
+    act(v("tB"), v("tB"), scale=col(M3))
+    tt(v("TABq"), v("tA"), v("tB"), A.add)
+    iota(v("RST"), pl, 0, 0)
+    ts(v("RST"), v("RST"), 0.0, A.is_equal, 4194304.0, A.mult)
+    ts(v("ordc", 0, 4), v("jj", 0, 4), 16.0, A.mult, col(K), A.add)
+    ts(v("ordc", 4, 8), v("ordc", 0, 4), -1.0, A.mult, 127.0, A.add)
+    l3 = math.log(3.0)
+    ms(col(T2), 52 * l3)
+    ex = act(v("wc"), v("ordc"), AF.Exp, bias=col(T2), scale=-l3, more=1500)
+    ex2 = act(v("thr"), v("ordr"), AF.Exp, bias=col(T2), scale=-l3)
+    act(v("thr"), v("thr"), scale=3.5)
+    ts(v("DUM", 0, 8), v("jj", 0, 8), 16.0, A.mult, col(K), A.add)
+    ts(v("DUM", 8, 16), v("DUM", 0, 8), 385.0, A.add)
+    ts(v("DUM", 16, 24), v("DUM", 0, 8), 4097.0, A.add)
+    ts(v("DUM", 0, 8), v("DUM", 0, 8), 257.0, A.add)
+    ms(v("Fb", 0, 16), 0.0)
+    ms(v("Fb", 4112, 4128), 0.0)
+    ms(v("Y", 256, 520), 0.0)
+    ms(v("x", 256, 264), 0)
+    ms(v("ST", 512, 528), 0.0)
+    ms(v("tabB", 256, 272), 0.0)
+    awz = ms(v("AW"), 0.0)
+    for t in range(RO):
+        act(v("SW%d" % t, CEN + 1, CEN + 65), v("ONES", 0, 64), scale=col(DLO))
+        act(v("SW%d" % t, CEN - 64, CEN), v("ONES", 0, 64), scale=col(DHI))
+    for c in range(P["NS"]):
+        iota(v("cval", 512 * c, 512 * c + 512), [[1, 32], [0, 16]], 64 + 32 * c, 0)
+        j = act(ind(v("inv"), v("offI", 32 * c, 32 * c + 32)), v("cval", 512 * c, 512 * c + 512), AF.Silu, more=1500 if c == 0 else 0)
+        if c == 0:
+            ops[j]["deps"].update({ex: False, ex2: False})
+
+    fixed.update(("CB", "CF", "ZB", "col", "ONES", "G8"))
+    e1 = topo.engines(core, nxt)
+    e2 = topo.engines(core, prv)
+    h = len(e1) // 2
+    mk1 = sum(1 << i for i in e1[:h])
+    mk2 = sum(1 << i for i in e2[h:])
+    did = lambda c: DstId(rid=topo.addr(c)[0], pnc=topo.addr(c)[1])
+    Fw = v("Fb", 16, 4128)
+
+    for t in range(RO):
+        now[0] = t
+
+        def index1(lo, hi):
+            s = lambda nm: v(nm, lo, hi)
+            ts(s("Yi"), s("Y"), float(128 * 77 * t), A.add)
+            ts(s("xt"), s("Yi"), 7, A.logical_shift_right, 4095, A.bitwise_and)
+            ts(s("w"), s("Yi"), 127, A.bitwise_and)
+            tt(s("P1"), s("xt"), s("w"), A.mult)
+            ts(s("P1"), s("P1"), 3, A.logical_shift_right, 4095, A.bitwise_and)
+            cp(s("iF"), s("P1"))
+
+        def pickF(c):
+            o = v("Fb", 16 + 1024 * c, 16 + 1024 * c + 1024)
+            gi = ind(v("spr_s"), v("iF", 64 * c, 64 * c + 64))
+            if t == 0 and c < P["VF0"]:
+                cp(o, gi)
+            else:
+                act(o, gi)
+
+        def tails():
+            act(v("fT"), ind(Fw, v("tlW")))
+            mm([(ps(4, 0, 16), zb(ZW1, c), v("fT", c, 256, 16)) for c in range(16)])
+            mm([(ps(4, 16, 32), zb(ZW2, c), v("fT", c, 256, 16)) for c in range(16)])
+            cp(v("uI"), ps(4, 0, 32))
+            ts(v("uI"), v("uI"), 4095, A.bitwise_and)
+            tt(v("uP"), v("uI", 0, 16), v("uI", 16, 32), A.mult)
+            ts(v("uP"), v("uP"), 5, A.logical_shift_right, 255, A.bitwise_and)
+            cp(v("qS"), v("uP"))
+            act(v("hiB"), ps(6), bias=159.508, scale=1.0 / 64)
+            mm([(ps(6), cf(FMX), v("xs")), (ps(6), cb(MH), v("hiB"))], True, False)
+            mm([(ps(6), cb(ID), v("fT"))], False, False)
+            act(v("qrow"), ind(v("TABq"), v("qS")))
+            mm([(ps(6), cb(I256), v("qrow"))], False, True)
+            act(v("pack"), ps(6), bias=col(BPK))
+
+        def slots(lo, hi):
+            s = lambda nm: v(nm, lo, hi)
+            o = ps(4, 256 + lo, 256 + hi)
+            tt(s("dany"), ps(5, lo, hi), s("tmB"), A.is_lt)
+            tt(s("dhi"), ps(5, lo, hi), s("thi"), A.is_lt)
+            mm([(o, cb(MC), s("ONES")), (o, cb(MA), s("dany")), (o, cb(MB), s("dhi"))])
+            scan(s("cum"), s("KEEP"), o, A.mult, A.add, v("cum", lo - 1, lo) if lo else 0.0)
+            tt(s("key"), s("cum"), o, A.mult)
+        index1(0, 64)
+        index1(64, 256)
+        ts(v("wB"), v("w"), 47.0, A.add)
+        mm([(ps(4), cb(SUPH), v("wB")), (ps(4), cb(C40), v("ONES"))])
+        mm([(ps(4, 256, 512), cb(K1), v("wB")), (ps(4, 256, 512), cb(K2), v("wB")), (ps(4, 256, 512), cb(C2032), v("ONES"))])
+        if t:
+            ts(X, Y, 1.0 / 128, A.mult, -0.496, A.add)
+        tt(v("P2f"), X, ps(4), A.mult)
+        tt(v("P2"), v("P2f"), ps(4, 256, 512), A.add)
+        ts(v("P2"), v("P2"), 5, A.logical_shift_right, 4095, A.bitwise_and)
+        cp(v("iE"), v("P2"))
+        ts(v("vB"), Y, 524288.0, A.is_lt)
+        mm([(ps(6, 256, 512), cb(T64), v("vB"))])
+        mm([(ps(2, 256, 272), zb(Z1, c), v("vB", c, 256, 16)) for c in range(16)] + [(ps(2, 256, 272), cb(BO), v("C1"))])
+        tt(v("xs"), X, ps(6, 256, 512), A.mult)
+        ts(v("tlW"), ps(2, 256, 272), col(TL), A.add)
+        mm([(ps(6), cf(FBO), v("xs"))])
+        ts(v("thi"), v("xs"), 131072.0, A.is_ge, 64.0, A.mult)
+        act(v("tmB"), ps(6, 256, 512))
+        for c, (lo, hi) in enumerate(P["CH"]):
+            for f in range(4):
+                if P["FA"][f] == c:
+                    pickF(f)
+            s = lambda nm: v(nm, 16 * lo, 16 * hi)
+            wd = hi - lo
+            act(s("E"), ind(v("bar_s"), v("iE", lo, hi)))
+            d = ps((0, 1, 7)[c % 3], 0, 16 * wd)
+            mm([(d, cb(ID), v("Fb", 16 + 16 * lo, 16 + 16 * hi)), (d, cb(NI), v("Fb", 15 + 16 * lo, 15 + 16 * hi))])
+            tt(v("UD", 32 * lo, 32 * lo + 16 * wd), d, s("E"), A.is_gt)
+            ts(s("nE"), s("E"), -1.0, A.mult)
+            tt(v("UD", 32 * lo + 16 * wd, 32 * hi), d, s("nE"), A.is_lt)
+            o = ps(2 + c % 2, 0, 2 * wd)
+            mm([(o, zb(Z1, k), v("UD", 32 * lo + k, 32 * hi, 16)) for k in range(1, 16)] +
+               [(ps(2 + c % 2, i * wd, i * wd + wd), cb(H100), v("vB", lo, hi)) for i in range(2)])
+            ts(v("su", 2 * lo, 2 * hi), o, 108.5, A.is_ge, 0.5, A.subtract)
+            o = ps(5, lo, hi)
+            mm([(o, cb(ID), v("wB", lo, hi)), (o, cb(W16), v("su", 2 * lo, 2 * lo + wd)), (o, cb(W16N), v("su", 2 * lo + wd, 2 * hi))])
+            if c == P["TA"]:
+                tails()
+            if hi == P["SL"]:
+                slots(0, hi)
+        slots(P["SL"], 256)
+        mm([(ps(0, 0, 16), zb(ZO, c), v("key", c, 256, 16)) for c in range(16)])
+        ts(v("offW"), ps(0, 0, 16), float(CEN), A.add)
+        sw, lb, gb = "SW%d" % t, "LB%d" % t, "GB%d" % t
+        cp(ind(v(sw), v("offW")), v("pack"))
+
+        def send(sw=sw, lb=lb):
+            return g.remote_dma_fused([
+                RemoteDMATransfer(dst_ids=[did(nxt)], dma_engine_mask=mk1, remote_sem=T.sem.m0, src=T[sw][:, CEN + 1:CEN + 65], dst=T[lb][:, 0:64]),
+                RemoteDMATransfer(dst_ids=[did(prv)], dma_engine_mask=mk2, remote_sem=T.sem.m1, src=T[sw][:, CEN - 64:CEN], dst=T[lb][:, 64:128])],
+                local_sem=T.sem.ls)
+        sn = add("G", send, [v(sw)], [], 300, sig="none", extra=[awz])
+        add("N", None, [], [v(lb, 0, 64)], 0, sig=("m0", h * (t + 1)), lat=P["net"], extra=[sn])
+        add("N", None, [], [v(lb, 64, 128)], 0, sig=("m1", (len(e2) - h) * (t + 1)), lat=P["net"], extra=[sn])
+        if t == 0:
+            for c in range(2 * P["NS"], 16):
+                ts(ind(v("inv"), v("offI", 16 * c, 16 * c + 16)), v("cval", 0, 256), 1.0, A.mult, float(16 * c), A.add)
+            ms(v("inv", 4096, 4097), 320.0)
+        ts(v("w1B"), ps(5), 48.0, A.max, 174.0, A.min)
+        ts(v("ovB"), v("key"), 65.0, A.is_ge)
+        mm([(ps(2), cf(FI), Y), (ps(2), cb(NI), v("wB")), (ps(2), cb(ID), v("w1B"))])
+        act(Y, ps(2))
+        mm([(ps(5), cb(B16), v("ONES")), (ps(5), cb(RSA), v("vB")), (ps(5), cb(BO), v("dany")), (ps(5), cb(ROVB), v("ovB"))])
+        o = ps(5, 256, 512)
+        mm([(o, cb(R15), v("vB")), (o, cb(BO), v("dany")), (o, cb(ROVB), v("ovB"))])
+        act(v("ST", 0, 512), ps(5, 0, 512), scale=1e27)
+        act(v("tabB", 0, 256), v("vB"), bias=col(KV), scale=-1048576.0)
+        dm = ps(7, 256, 512)
+        mm([(dm, cf(FXS), v("xs")), (dm, cb(SUPT), v("tmB")), (dm, cf(FSI), Y)])
+        L = v(lb)
+        ts(v("metaB"), L, 1.0 / 256, A.mult, 143.502, A.add)
+        mm([(ps(0, 0, 128), cb(RQB), v("metaB"))])
+        mm([(ps(3, 0, 128), cb(RQB), v("metaB"))])
+        ts(v("lq"), ps(0, 0, 128), 16.0, A.mult, col(QK), A.add)
+        act(v("R", 1, 256, 2), ps(3, 0, 128), bias=-2448.0)
+        ops[act(v("Fq", 0, 1024), ind(Fw, v("lq", 0, 64)))]["up"] = P["u1"]
+        ops[act(v("Fq", 1024, 2048), ind(Fw, v("lq", 64, 128)))]["up"] = P["u1"]
+        mm([(ps(1, 0, 8), zb(ZN, c), v("metaB", c, 128, 16)) for c in range(16)] + [(ps(1, 0, 8), cb(BO), v("CN", 0, 128, 16))])
+        ts(v("nmW"), ps(1, 0, 8), -9360.0, A.add)
+        ts(v("R", 0, 256, 2), ind(v("inv", 0, 4104), v("nmW")), MAGIC, A.add, MAGIC + 64, A.subtract)
+        ts(v("Wf", 16, 24), ps(1, 0, 8), -9360.0, A.add)
+        mm([(ps(4, 0, 8), zb(ZQ, c), v("metaB", c, 128, 16)) for c in range(16)])
+        ts(v("Wf", 8, 16), ps(4, 0, 8), -2448.0, A.add)
+        mm([(ps(1, 0, 8), zb(Z0, c), v("R", 2 * c, 256, 32)) for c in range(16)])
+        rng = [(16 * u, 128) for u in range(4)] + [(64, 16 * u + 16) for u in range(4, 8)]
+
+        def clash(j, u, first):
+            lo, hi = rng[u]
+            b = 256 * (8 * j + u)
+            ts(v("OH", b, b + 2 * (hi - lo)), v("R", 2 * lo, 2 * hi), v("Wf", 8 * j + u, 8 * j + u + 1), A.is_equal, v("wc", u, u + 1), A.mult)
+            mm([(ps(6, lo, hi), cb(BO), v("OH", b + i, b + 2 * (hi - lo), 2)) for i in range(2)], first, False)
+        for u in range(8):
+            clash(1, u, u == 0)
+        cp(v("Wf", 0, 8), ps(1, 0, 8))
+        for u in range(8):
+            clash(0, u, False)
+        cp(v("AQ"), v("Wf", 0, 16))
+        cp(v("SG", 128, 256), ind(v("ST", 256, 528), v("AQ", 8, 16)))
+        cp(v("SG", 0, 128), ind(v("ST", 0, 272), v("AQ", 0, 8)))
+        mm([(ps(6, 0, 128), cb(BO), v("SG", 128, 256)), (ps(6, 0, 128), cb(BO), v("SG", 0, 128))], False, True)
+        ops[tt(v(gb), ps(6, 0, 128), v("thr"), A.is_lt)]["up"] = P["u3"]
+
+        def ack(gb=gb):
+            return g.remote_dma_fused([
+                RemoteDMATransfer(dst_ids=[did(nxt)], dma_engine_mask=mk1, remote_sem=T.sem.k0, src=T[gb][:, 64:128], dst=T.AW[:, CEN - 64:CEN]),
+                RemoteDMATransfer(dst_ids=[did(prv)], dma_engine_mask=mk2, remote_sem=T.sem.k1, src=T[gb][:, 0:64], dst=T.AW[:, CEN + 1:CEN + 65])],
+                local_sem=T.sem.ls)
+        an = add("G", ack, [v(gb)], [], 300, sig="none")
+        add("N", None, [], [v("AW", CEN - 64, CEN)], 0, sig=("k0", h * (t + 1)), lat=P["net"], extra=[an])
+        add("N", None, [], [v("AW", CEN + 1, CEN + 65)], 0, sig=("k1", (len(e2) - h) * (t + 1)), lat=P["net"], extra=[an])
+        o = ps(0, 128, 256)
+        mm([(o, cf(FI), L), (o, cb(NI256), v("metaB")), (o, cb(C2304), v("ONES", 0, 128))])
+        mm([(ps(3, 0, 128), cb(TM), cb(ID))] + [(ps(3, k, 128, 16), v("Fq", k, 2048, 16), v("G8", 8, 16)) for k in range(16)], True, False)
+        for k in range(16):
+            tt(v("Mx", 128 * k, 128 * k + 64), v("Fq", k, 1024, 16), ps(0, 128, 192), A.max)
+        for k in range(16):
+            tt(v("Mx", 128 * k + 64, 128 * k + 128), v("Fq", 1024 + k, 2048, 16), ps(0, 192, 256), A.max)
+            mm([(ps(3, k, 128, 16), v("Mx", 128 * k, 128 * k + 128), v("G8", 16, 24))], False, False)
+        act(v("tq"), ind(v("tabB"), v("AQ", 8, 16)))
+        mm([(ps(3, 0, 128), v("tq"), cb(ID))], False, True)
+        mm([(ps(2, 0, 128), cb(RNB), v("metaB")), (ps(2, 0, 128), cb(BO), v("CN"))])
+        act(v("nmS"), ps(2, 0, 128), bias=-9360.0)
+        ops[act(v("Yaq"), ind(v("Y"), v("AQ")))]["up"] = P["u2"]
+        mm([(ps(5, 0, 128), cf(FI), v("Yaq", 128, 256)), (ps(5, 0, 128), cf(FN128), v("nmS"))])
+        act(v("Dq"), ps(5, 0, 128), bias=-33.0)
+        scan(v("pm"), v("RST"), ps(3, 0, 128), A.add, A.min)
+        for j in range(8):
+            ts(v("mT", 16 * j, 16 * j + 16), v("pm", 16 * j, 16 * j + 16), v("pm", 16 * j + 15, 16 * j + 16), A.is_equal)
+        mm([(ps(6, 0, 128), v("mT"), cb(ID))])
+        mm([(ps(2, 0, 128), cf(FI), v("Yaq", 128, 256))], True, False)
+        tt(v("Aq"), ps(6, 0, 128), v("Dq"), A.mult)
+        mm([(ps(2, 0, 128), cf(FSI), v("Aq"))], False, True)
+        act(v("Yn"), ps(2, 0, 128))
+        mm([(ps(1, 0, 8), zb(Z0, c), v(gb, c, 128, 16)) for c in range(16)])
+        tt(v("Dif"), v("Wf"), v("DUM"), A.subtract)
+        nl = 3 if t < RO - 1 else 2
+        for j in range(nl):
+            tt(v("L3f", 8 * j, 8 * j + 8), v("Dif", 8 * j, 8 * j + 8), ps(1, 0, 8), A.mult)
+        tt(v("L3f", 0, 8 * nl), v("L3f", 0, 8 * nl), v("DUM", 0, 8 * nl), A.add)
+        cp(v("L3", 0, 8 * nl), v("L3f", 0, 8 * nl))
+        tt(v("eqB"), ind(v("x"), v("AQ", 0, 8)), v("nmS"), A.is_equal)
+        mm([(ps(4, 0, 128), cf(FDI), v("Yaq", 0, 128))])
+        act(v("Dd"), ps(4, 0, 128), bias=col(B15))
+        mm([(ps(4, 128, 256), cb(LT), v("eqB"))])
+        tt(v("ta"), ps(4, 128, 256), v("Dd"), A.mult)
+        tt(ind(v("Y"), v("L3", 0, 8)), v("ta"), v("Yaq", 0, 128), A.add)
+        act(v("tm2"), ind(v("AW"), v("offW")))
+        tt(dm, v("tm2"), dm, A.mult)
+        tt(Y, Y, dm, A.add)
+        cp(ind(v("Y"), v("L3", 8, 16)), v("Yn"))
+        if t < RO - 1:
+            act(v("qF"), v("R", 1, 256, 2), bias=64.0)
+            cp(ind(v("inv", 0, 4232), v("L3", 16, 24)), v("qF"))
+
+    now[0] = RO
+    ts(X, Y, 1.0 / 128, A.mult, 0.504, A.add)
+    ts(v("vB"), Y, 524288.0, A.is_lt)
+    tt(v("o1"), X, v("vB"), A.mult)
+    act(v("o2"), v("o1"), bias=-1.0)
+    dma("S", T.yl[:], T.o2[:], [v("o2")], [], "d6", 2200)
+    cp(v("Yi"), Y)
+    ts(v("Yi"), v("Yi"), 1, A.logical_shift_right, 63, A.bitwise_and)
+    tt(v("o3"), v("Yi"), v("vB"), A.mult)
+    dma("Y", T.yz[:], T.o3[:], [v("o3")], [], "d7", 2200)
+    mm([(v("PS0", 0, 256, 1, 8), v("G8", 0, 8), v("vB"))])
+    act(v("o4", 0, 256, 1, 8), v("PS0", 0, 256, 1, 8))
+    dma("S", T.yn[:], T.o4[0:8, :], [v("o4")], [], "d5", 2000)
+    return ops, 2 * RO * len(e2)
+
+
+def schedule(ops):
+    n = len(ops)
+    cost = [o["cost"] for o in ops]
+    eng = [o["eng"] for o in ops]
+    pre = [[(j, cost[j] + (ops[j]["lat"] + (P["self"] if eng[j] == eng[i] else P["hop"]) if w else 0.0)) for j, w in ops[i]["deps"].items()] for i in range(n)]
+    for i in range(n):
+        far = set()
+        for j, d in pre[i]:
+            if d > cost[j]:
+                far.update(ops[j]["deps"])
+        pre[i] = [(j, d) for j, d in pre[i] if j not in far or ops[j]["lat"] > 100]
+    suc = [[] for _ in range(n)]
+    for i in range(n):
+        for j, d in pre[i]:
+            suc[j].append(i)
+
+    def place(key):
+        st = [0.0] * n
+        why = [-1] * n
+        busy = {e: [] for e in set(eng)}
+        for i in sorted(range(n), key=lambda i: (-key[i], i)):
+            s, y = 0.0, -1
+            for j, d in pre[i]:
+                if st[j] + d > s:
+                    s, y = st[j] + d, j
+            if eng[i] != "N":
+                b = busy[eng[i]]
+                k = len(b)
+                while k > 0 and b[k - 1][1] > s:
+                    k -= 1
+                while k < len(b) and b[k][0] < s + cost[i]:
+                    if b[k][1] > s:
+                        s, y = b[k][1], -2 - b[k][2]
+                    k += 1
+                b.insert(k, (s, s + cost[i], i))
+            st[i], why[i] = s, y
+        z = max(range(n), key=lambda i: st[i] + cost[i] + ops[i]["lat"])
+        return st, why, z, st[z] + cost[z] + ops[z]["lat"]
+    key = [0.0] * n
+    for more in (1.0, 0.0):
+        for i in range(n - 1, -1, -1):
+            for j, d in pre[i]:
+                key[j] = max(key[j], key[i] + d * more + 1e-3)
+        key = [key[i] + ops[i]["up"] * more for i in range(n)]
+    twin = {(o["t"], o["tag"]): i for i, o in enumerate(ops)}
+    cur = place(key)
+    best = cur
+    seed = 12345
+    for it in range(P["it"]):
+        held, i = [], cur[2]
+        while i != -1:
+            y = cur[1][i]
+            if y < -1:
+                y = -2 - y
+                held.append((i, y))
+            i = y
+        seed = (seed * 1103515245 + 12345) % 2147483648
+        i, y = held[(seed >> 8) % len(held)]
+        k2 = list(key)
+        todo = []
+        dt = ops[y]["t"] - ops[i]["t"]
+        pairs = [(i, y)]
+        if seed % 5 < P["tw"]:
+            pairs = [(twin[r, ops[i]["tag"]], twin[r + dt, ops[y]["tag"]]) for r in range(RO + 1)
+                     if (r, ops[i]["tag"]) in twin and (r + dt, ops[y]["tag"]) in twin]
+        for i, y in pairs:
+            if seed % 3:
+                k2[i] = max(k2[i], k2[y] + 1e-3 + (seed % 7) * P["rnd"])
+                todo.append(i)
+            else:
+                k2[y] = min(k2[y], k2[i] - 1e-3 - (seed % 7) * P["rnd"])
+                todo.append(y)
+        while todo:
+            a = todo.pop()
+            for j, d in pre[a]:
+                if k2[j] <= k2[a]:
+                    k2[j] = k2[a] + 1e-3
+                    todo.append(j)
+            for j in suc[a]:
+                if k2[j] >= k2[a]:
+                    k2[j] = k2[a] - 1e-3
+                    todo.append(j)
+        new = place(k2)
+        if new[3] <= cur[3] + P["tol"] * (1.0 - it / P["it"]):
+            cur, key = new, k2
+            if new[3] < best[3]:
+                best = new
+    st = best[0]
+    return [(i, st[i]) for i in sorted(range(n), key=lambda i: (st[i], i))], best[3]
+
+
+def rank_program(g, core, T, topo):
+    if T.rank_of(core) is None:
+        return
+    ops, nls = build(g, core, T, topo)
+    if "order" not in PLAN:
+        PLAN["order"] = schedule(ops)[0]
+    q = {"V": g.vector, "S": g.scalar, "P": g.tensor, "G": g, "Y": g.sync}
+    cnt = {"V": 0, "S": 0, "P": 0, "G": 0}
+    known = {k: {} for k in q}
+    clock = {}
+    sig = {}
+    for i, _ in PLAN["order"]:
+        o = ops[i]
+        e = o["eng"]
+        if e == "N":
+            sig[i] = o["sig"]
+            clock[i] = {}
+            continue
+        kn = known[e]
+        need = {}
+        for j, w in o["deps"].items():
+            if w and sig[j] != "none":
+                need[sig[j][0]] = max(need.get(sig[j][0], (0, 0)), (sig[j][1], j))
+        for s, (val, j) in sorted(need.items(), key=lambda z: -z[1][1]):
+            if kn.get(s, 0) < val:
+                q[e].wait_ge(T.sem[s], val)
+                kn[s] = val
+                for s2, v2 in clock[j].items():
+                    kn[s2] = max(kn.get(s2, 0), v2)
+        r = o["fn"]()
+        if o["sig"] is None:
+            cnt[e] += 1
+            r.then_inc(T.sem["c" + e], 1)
+            sig[i] = ("c" + e, cnt[e])
+        else:
+            sig[i] = o["sig"]
+        clock[i] = dict(kn)
+    for e in cnt:
+        g.wait_ge(T.sem["c" + e], cnt[e])
+    g.wait_ge(T.sem.ls, nls)
+    for s in ("d5", "d6", "d7"):
+        g.wait_ge(T.sem[s], 16)

@@ -3,25 +3,35 @@ from concourse.bass import DstId, RemoteDMATransfer
 from concourse.mybir import AluOpType as A, ActivationFunctionType as AF
 
 RO = 4
-CEN = 256
+LO, HI = 256, 512
 MAGIC = 12582912.0
 BF, F32, I32, U16 = "bfloat16", "float32", "int32", "uint16"
-P = {"it": 6000, "rnd": 200.0, "tol": 60.0, "NS": 6, "VF0": 2, "cyc": 1.0, "pe": 0.52, "g": 1.56, "sc": 3.8, "hop": 110.0, "self": 70.0, "net": 2600.0,
-     "CH": [(32 * c, 32 * c + 32) for c in range(7)] + [(224, 240), (240, 256)], "FA": (0, 0, 2, 4), "TA": 4, "SL": 224,
-     "tw": 4, "u1": 1000.0, "u2": 500.0, "u3": 500.0}
+P = {"it": 9000, "rnd": 5000, "tol": 250.0, "shake": 1, "jb": 2, "INV": "SSSSSSSSSSVVVVVV", "cyc": 0.87, "pe": 0.44, "g": 1.56, "sc": 3.8, "hop": 110.0, "self": 110.0, "net": 2700.0,
+     "CH": [(32 * c, 32 * c + 32) for c in range(8)], "YQ": (64, 128, 192, 256), "VF": ((), (), (), ()), "VE": ((), (), (), ()),
+     "IX": ((0, 64), (64, 128), (128, 256)), "IE": ((0, 128), (128, 256)), "SD": (), "ND": (), "FTV": 0, "ETV": 0, "UTV": 0, "suS": 0, "RS": 1, "ivS": 0, "mTS": 0,
+     "cut": 256, "VS": 1, "YV": 1, "DQ": 1, "MH": 8, "Y1": 1, "GF": [(64 * c, 64 * c + 64) for c in range(4)], "GE": [(32 * c, 32 * c + 32) for c in range(8)], "GQ": 64, "rl": 0,
+     "o1": (-1, -1), "o2": -1, "SN": (), "CS": 4, "sfix": 170.0, "EV": "",
+     "cases": ((1.4, 1.9, 5.6, 1.0, 0.0, 110.0, 1.0), (1.0, 1.15, 2.0, 1.1, 25.0, 190.0, 1.3), (1.15, 1.95, 2.2, 1.1, 25.0, 80.0, 0.8))}
 
-SB = {}
-for _d, _l in ((BF, "spr_s 4096 bar_s 4096 wt_s 2 wB 256 vB 256 Fb 4128 E 4096 nE 4096 UD 8192 tmB 256 thi 256 fT 256 qrow 256 hiB 256 su 512 "
-                    "dany 256 dhi 256 cum 256 key 256 w1B 256 ovB 256 ST 528 tabB 272 AW 784 metaB 128 R 256 OH 4096 SG 256 eqB 128 Fq 2048 Mx 2048 "
-                    "tq 128 mT 128 CB 4608 ZB 1008 G8 24 ONES 256 KEEP 256 C1 16 CN 128 TABq 256 GB0 128 GB1 128 GB2 128 GB3 128"),
-               (F32, "Y 520 P2f 256 xs 256 pack 256 Wf 24 Dif 24 L3f 24 nmS 128 Yaq 256 Dd 128 ta 128 Dq 128 pm 128 Aq 128 Yn 128 tm2 256 qF 128 "
-                     "inv 8320 cval 4096 o1 256 o2 256 o3 256 o4 256 mg 128 jj 144 col 40 wtf 2 CF 896 tA 256 tB 256 RST 128 ordr 128 thr 128 "
-                     "ordc 8 wc 8 DUM 24 SW0 776 SW1 776 SW2 776 SW3 776 LB0 128 LB1 128 LB2 128 LB3 128"),
-               (I32, "lam_s 256 mon_s 256 Yi 256 xt 256 w 256 P1 256 x 264 P2 256 uI 32 uP 16 Jt 256 pI 2"),
-               (U16, "iF 256 iE 256 tlW 16 qS 16 offW 16 lq 128 nmW 8 AQ 16 L3 24 offI 256")):
-    _w = _l.split()
+SB, POOL = {}, {}
+for _d, _l in ((BF, "spr_s 4096 bar_s 4096 wt_s 2 Fb 4128 E 4096 nE 4096 UD 8192 STv 272 SENT 768 AW 768 OH 4096 Fq 2048 Mx 2048 CB 6144 ZB 1008 "
+                    "TABq 256 GB0 128 GB1 128 GB2 128 GB3 128 FT 512 ET 256 UT 512 tmB 256 qrow 256 SG 256 G8 24 ONES 256 | wB 256 vB 256 hiB 256 su 512 w1B 256 "
+                    "metaB 128 R 256 eqB 128 mT 128 CN 128 OD 256 ODq 256 KT 128 mA 128 mQ 128 cc 32 FL 64 cs 36 DW3 48"),
+               (F32, "Y 520 Yaq 256 ta 128 Yn 128 tm2 256 qF 128 pack 256 nmS 128 inv 8320 cval 4096 o2 256 o3 256 o4 256 CF 1152 col 48 "
+                     "SW0 768 SW1 768 SW2 768 SW3 768 LB0 128 LB1 128 LB2 128 LB3 128 | P2f 256 xs 256 A1 512 Tw 512 RS 256 W2 32 Wf 384 gw 128 Dif 24 L3f 24 "
+                     "pm 128 Aq 128 Dq 128 o1 256 mg 128 jj 144 wtf 2 tA 256 tB 256 RST 128 thr 128 ordc 8 wc 128 DUM 24 tE 32 ab 32 TH 64 "
+                     "RS3 48 ow 48"),
+               (I32, "lam_s 256 mon_s 256 x 264 | Yi 256 xt 256 w 256 P1 256 P2 256 uI 32 uP 16 Jt 256 pI 2 tY 32 txt 32 tw 32 tP 32 tX 16 tP2 16"),
+               (U16, "iF 256 iE 256 lF 32 lE 16 qS 16 offW 16 lq 128 AQ 24 L3 24 offI 256 |")):
+    _w, _p = _l.split("|")
+    _w, _p, _o = _w.split(), _p.split(), 0
     for _i in range(0, len(_w), 2):
         SB[_w[_i]] = (int(_w[_i + 1]), _d)
+    for _i in range(0, len(_p), 2):
+        POOL[_p[_i]] = ("pool_" + _d, _o, int(_p[_i + 1]))
+        _o += (int(_p[_i + 1]) + 15) // 16 * 16
+    if _o:
+        SB["pool_" + _d] = (_o, _d)
 SCRATCH = {k: ("sbuf", [128, n], d) for k, (n, d) in SB.items()}
 for _b in range(8):
     SCRATCH["PS%d" % _b] = ("psum", [128, 512], F32)
@@ -39,16 +49,21 @@ def build(g, core, T, topo):
     now = [0]
 
     def v(name, lo=0, hi=None, st=1, p=128):
+        nm = name
+        if name in POOL:
+            name, o, w = POOL[name]
+            lo, hi = o + lo, o + (w if hi is None else hi)
         if hi is None:
             hi = SB[name][0]
         t = T[name]
         ap = t[0:p, lo:hi] if st == 1 else t[0:p, lo:hi:st]
         dtp = SB[name][1] if name in SB else F32
         return {"ap": ap, "r": [(name, lo, hi, lo % 2 if st % 2 == 0 else None)], "n": len(range(lo, hi, st)), "two": dtp in (BF, U16),
-                "ps": name not in SB, "ind": False, "f32": dtp == F32}
+                "ps": name not in SB, "ind": False, "f32": dtp == F32, "nm": nm}
 
     def ind(win, off):
-        return {"ap": win["ap"].indirect(off["ap"]), "r": win["r"], "o": off["r"], "n": 16 * off["n"], "two": win["two"], "ps": False, "ind": True}
+        return {"ap": win["ap"].indirect(off["ap"]), "r": win["r"], "o": off["r"], "n": 16 * off["n"], "two": win["two"], "ps": False, "ind": True,
+                "nm": win["nm"]}
 
     def add(eng, fn, rd, wr, cost, sig=None, lat=0.0, extra=()):
         i = len(ops)
@@ -65,6 +80,8 @@ def build(g, core, T, topo):
                     ov = l2 < hi and lo < h2 and (pa is None or p2 is None or pa == p2)
                     if nm not in SB and e2 != eng:
                         deps[j] = True
+                    elif nm not in SB and eng == "P":
+                        deps[j] = deps.get(j, False)
                     elif ov and (w2 or isw):
                         deps[j] = deps.get(j, False) or e2 != eng or eng != "P"
         for j in extra:
@@ -77,6 +94,7 @@ def build(g, core, T, topo):
                 if isw or nm not in fixed:
                     acc[nm] = (old if nm in SB else old[-150:]) + [(i, lo, hi, isw, eng, pa)]
         ops.append({"eng": eng, "fn": fn, "deps": deps, "cost": cost, "sig": sig, "lat": lat, "up": 0.0, "t": now[0],
+                    "g": sum(a["n"] for a in rd if a["ind"]), "sc": sum(a["n"] for a in wr if a["ind"]),
                     "tag": (eng == "N", tuple((r[0][:2] if r[0][:2] in ("SW", "LB", "GB") else r[0], r[1]) for r in ww + rr))})
         return i
 
@@ -118,15 +136,25 @@ def build(g, core, T, topo):
                    vcost(out, [d0, d1]))
 
     def act(out, a, func=AF.Identity, bias=None, scale=None, more=0.0):
+        if out["nm"] in P["EV"].split() and func == AF.Identity and not a["ind"]:
+            return ts(out, a, 1.0 if scale is None else scale, A.mult, 0.0 if bias is None else bias, A.add)
         kw = {}
         if bias is not None:
             kw["bias"] = sc(bias)
         if scale is not None:
             kw["scale"] = sc(scale)
-        c = 65 + a["n"] * P["cyc"] * (P["sc"] if out["ind"] else P["g"] if a["ind"] else 1.0) + more
+        c = (65 if out["ind"] or a["ind"] else P["sfix"]) + a["n"] * P["cyc"] * (P["sc"] if out["ind"] else P["g"] if a["ind"] else 1.0) + more
         return add("S", lambda: g.scalar.activation(out["ap"], a["ap"], func, **kw), [a] + cols(bias, scale), [out], c)
 
     def mm(items, first=True, last=True):
+        c, k = 0, 0
+        while k < len(items) - 1 and c < P["cut"]:
+            c += max(min(64, items[k][1]["n"]), items[k][2]["n"]) * (4 if items[k][2]["f32"] else 1)
+            k += 1
+        if c >= P["cut"]:
+            mm(items[:k], first, False)
+            return mm(items[k:], False, last)
+
         def fn():
             r = None
             for i, (o, l, x) in enumerate(items):
@@ -136,7 +164,7 @@ def build(g, core, T, topo):
         return add("P", fn, [a for it in items for a in it[1:]], [it[0] for it in items], c, lat=60.0)
 
     def iota(out, pat, base, cm):
-        if out["f32"]:
+        if out["f32"] or out["two"]:
             fn = lambda: g.iota(out["ap"], pat, base, cm, allow_small_or_imprecise_dtypes=True)
         else:
             fn = lambda: g.iota(out["ap"], pat, base, cm)
@@ -178,41 +206,36 @@ def build(g, core, T, topo):
     iota(v("jj"), [[1, 144]], 0, 0)
     iota(v("tA"), [[1, 16], [0, 16]], 0, 0)
     iota(v("tB"), [[0, 16], [1, 16]], 0, 0)
-    iota(v("ordr", 0, 64), [[1, 64]], 0, 0)
-    iota(v("ordr", 64, 128), [[-1, 64]], 127, 0)
-    K, GR, GE, TL, KV, M0, M2, M3, M4, M15, RO_, RN, RQ, ROV, KP, BPK, B15, DLO, DHI, T2, QK, T1 = range(22)
+    K, GR, GE, N0, M1, G4, RN, RQ, BPK, DLO, DHI, QK, CA, CQ, CT = range(15)
     ts(v("pI", 1, 2), v("pI", 0, 1), 15, A.bitwise_and)
     cp(col(K), v("pI", 1, 2))
     ts(v("pI", 1, 2), v("pI", 0, 1), 4, A.logical_shift_right)
     cp(col(GR), v("pI", 1, 2))
     ts(col(GE), col(GR), 16.0, A.mult, 15.0, A.add)
-    ts(col(TL), col(K), 16.0, A.mult, -1.0, A.add)
-    ts(col(KV), col(K), 1048576.0, A.add)
-    ts(col(QK), col(K), -16.0 * 2448, A.add)
-    for j, k in ((M0, 0), (M2, 2), (M3, 3), (M15, 15)):
-        ts(col(j), col(K), float(k), A.is_equal)
-    tmp = [T1]
+    ts(col(QK), col(K), -16.0 * 3264, A.add)
+    ts(v("col", 32, 48), v("jj", 0, 16), col(K), A.is_equal)
+    M2, M3 = 34, 35
+    ts(col(N0), col(K), 0.0, A.not_equal)
+    ts(col(M1), col(K), 1.0, A.is_equal, 1048576.0, A.mult)
+    ts(col(G4), col(K), 4.0, A.is_ge, -1048576.0, A.mult)
 
     def lin(dst, terms):
         ts(col(dst), col(K), float(terms[0][0]), A.is_equal, float(terms[0][1]), A.mult)
         for k, wgt in terms[1:]:
-            ts(col(tmp[0]), col(K), float(k), A.is_equal, float(wgt), A.mult)
-            ts(col(dst), col(dst), col(tmp[0]), A.add)
-            tmp[0] += 1
-    lin(M4, [(4, -1)])
-    lin(RO_, [(0, 1), (4, -1), (8, 1), (12, 256)])
-    lin(RN, [(0, 64), (1, 1)])
+            ts(col(dst), col(32 + k), float(wgt), A.mult, col(dst), A.add)
+    big = 2.0 ** 90
+    lin(RN, [(0, 64), (1, 1), (4, 2048)])
     lin(RQ, [(2, 16), (3, 1)])
-    lin(ROV, [(0, -1), (4, -1)])
-    ts(col(KP), col(K), 12.0, A.is_lt)
     lin(BPK, [(0, -40960), (1, 2621440)])
-    lin(B15, [(15, 524289)])
-    lin(DLO, [(0, 256 * 32), (2, 256 * 16)])
-    lin(DHI, [(0, 256 * 96), (2, 256 * 16)])
+    lin(DLO, [(4, 256), (2, 256 * 16)])
+    lin(DHI, [(4, 256 * 3), (2, 256 * 16)])
+    lin(CA, [(0, big), (1, big), (4, -big)])
+    lin(CQ, [(0, big), (15, big)])
+    lin(CT, [(0, 128 * 12480), (1, -33)])
     cp(v("wtf"), v("wt_s"))
-    (BO, ID, NI, H100, SUPH, C40, K1, K2, C2032, T64, W16, W16N, MA, MB, MC, MH, I256, SUPT, LT, RSA, RQB, RNB, R15, ROVB, NI256, C2304, B16,
-     SUP, SDN, BSI, BDI, C8, C4, E0, E1, TM) = range(36)
-    (FI, FBO, FMX, FSI, FXS, FDI, FN128) = range(7)
+    (BO, ID, NI, H100, H107, SUPH, C40, K1, K2, C2032, T64, T64P, W16, W16N, MH, I256, SUPT, LT, RQB, RNB, RN128, B128, NI256, C2304,
+     SUP, SDN, BSI, BDI, E0, E1, E15, FA, FQ, CTB, NDG, L1, L0, TN) = range(38)
+    (FI, FBO, FMX, FSI, FXS, FDI) = range(6)
     dif, pl = [[1, 128]], [[0, 8], [1, 16]]
     ts(cb(BO), v("mg"), col(GR), A.is_equal)
     sel(cb(ID), cb(BO), dif, A.is_equal, 0.0, 0, -1)
@@ -221,74 +244,98 @@ def build(g, core, T, topo):
     sel(cb(BSI), cb(SUP), dif, A.not_equal, -1.0, 0, -1)
     sel(cb(BDI), cb(SDN), dif, A.not_equal, -1.0, 0, -1)
     sel(cb(LT), cb(BO), dif, A.is_ge, 0.0, 0, -1)
-    sel(cb(C8), cb(BO), pl, A.is_ge, 0.0, -8, 0)
-    sel(cb(C4), cb(BO), [[0, 8], [-1, 16]], A.is_ge, 0.0, 3, 0)
     sel(cb(E0), cb(BO), pl, A.is_equal, 0.0, 0, 0)
     sel(cb(E1), cb(BO), pl, A.is_equal, 0.0, -1, 0)
+    sel(cb(TN), cb(BO), dif, A.is_equal, 0.0, 2, -1)
+    tt(cb(TN), cb(SDN), cb(TN), A.subtract)
+    ts(cb(T64P), cb(TN), 64.0, A.mult)
+    sel(cb(TN), cb(BO), pl, A.is_equal, 0.0, -15, 0)
+    ts(cb(E15), cb(TN), 32768.0, A.mult)
     for d, s, c in ((NI, ID, -1.0), (H100, ID, 100.0), (K1, ID, 12288.0), (K2, ID, 688.0), (I256, ID, 256.0), (C40, BO, 2.5), (C2032, BO, 2032.0),
-                    (SUPH, SUP, 0.5), (T64, BDI, -64.0), (W16, BDI, -16.0), (W16N, BDI, 16.0), (MC, C8, 1.0 / 16), (NI256, ID, -256.0),
-                    (C2304, BO, 2304.0), (B16, BO, 1.0 / 16), (RSA, BO, col(M4)), (RQB, BO, col(RQ)), (RNB, BO, col(RN)), (R15, BO, col(M15)),
-                    (ROVB, BO, col(ROV))):
-        ts(cb(d), cb(s), c, A.mult)
-    for d, s, c in ((FI, ID, 1.0), (FN128, ID, -128.0), (FBO, BO, 1.0 / 64), (FSI, BSI, 1.0), (FDI, BDI, 1.0), (FMX, E1, 4.0)):
+                    (SUPH, SUP, 0.5), (T64, BDI, -64.0), (W16, BDI, -8.0 if P["suS"] else -16.0), (W16N, BDI, 8.0 if P["suS"] else 16.0), (NI256, ID, -256.0),
+                    (C2304, BO, 3072.0), (RQB, BO, col(RQ)), (RNB, BO, col(RN)), (RN128, RNB, -128.0), (B128, BO, -128.0),
+                    (FA, BO, col(CA)), (FQ, BO, col(CQ)), (CTB, BO, col(CT))) + ((H107, ID, 107.0),) * (len(P["SD"]) > 0):
+        if d in (C40, C2032, C2304, B128, NI, H100, K1, K2, I256, NI256)[:P["CS"]]:
+            act(cb(d), cb(s), scale=c)
+        else:
+            ts(cb(d), cb(s), c, A.mult)
+    for d, s, c in ((FI, ID, 1.0), (FBO, BO, 1.0 / 64), (FSI, BSI, 1.0), (FDI, BDI, 1.0), (FMX, E1, 4.0)):
         act(cf(d), cb(s), scale=c)
-    tt(cb(MA), cb(C4), cb(C8), A.subtract)
-    ts(cb(TM), cb(C4), -2.0, A.mult)
-    tt(cb(TM), cb(TM), cb(BO), A.add)
-    tt(cb(MB), cb(TM), cb(C8), A.subtract)
-    tt(cb(TM), cb(E0), cb(SUP), A.subtract)
-    act(cf(FXS), cb(TM), scale=2.0)
-    ms(cb(TM), 0.0)
-    ts(cb(C4), cb(E0), 33.0 / 64, A.mult)
-    ts(cb(SUPT), cb(SUP), 8192.0, A.mult)
-    tt(cb(SUPT), cb(SUPT), cb(C4), A.add)
+    tt(cb(TN), cb(E0), cb(SUP), A.subtract)
+    act(cf(FXS), cb(TN), scale=2.0)
+    ts(cb(SUPT), cb(BSI), 524288.0, A.mult)
+    for i in range(1, 2):
+        ts(v("CB", 128 * SUPT, 128 * SUPT + 128, 16), v("CB", 128 * ID, 128 * ID + 128, 16), 33.0, A.mult)
     ts(cb(E1), cb(E1), -64.0, A.mult)
     tt(cb(E1), cb(E1), cb(E0), A.add)
-    ts(cb(MH), cb(E1), col(M0), A.mult, 256.0, A.mult)
-    Z1, ZW1, ZW2, ZO, ZN, ZQ, Z0 = range(7)
+    ts(cb(MH), cb(E1), 256.0, A.mult)
+    sel(cb(TN), cb(BO), pl, A.is_ge, 0.0, -4, 0)
+    ts(cb(TN), cb(TN), col(M1), A.mult)
+    ts(cb(NDG), cb(ID), col(G4), A.mult)
+    tt(cb(NDG), cb(NDG), cb(TN), A.add)
+    sel(cb(L1), cb(LT), dif, A.not_equal, 256.0, 0, -1)
+    sel(cb(L0), cb(BO), [[-1, 128]], A.is_ge, 0.0, 0, 1)
+    sel(cb(L0), cb(L0), dif, A.not_equal, -255.0, 0, -1)
+    Z1, ZW1, ZW2, Z16 = range(4)
     zf = lambda j: v("ZB", 144 * j, 144 * j + 144)
     ts(zf(Z1), v("jj"), col(GE), A.is_equal)
-    for j, s in ((ZW1, v("wtf", 0, 1)), (ZW2, v("wtf", 1, 2)), (ZO, col(RO_)), (ZN, col(RN)), (ZQ, col(RQ)), (Z0, col(M0))):
+    for j, s in ((ZW1, v("wtf", 0, 1)), (ZW2, v("wtf", 1, 2)), (Z16, 1.0 / 32)):
         ts(zf(j), zf(Z1), s, A.mult)
     ts(v("G8", 0, 8), v("jj", 0, 8), col(GR), A.is_equal)
     ts(v("G8", 8, 16), v("G8", 0, 8), -16.0, A.mult)
     ts(v("G8", 16, 24), v("G8", 0, 8), 32.0, A.mult)
     ms(v("ONES"), 1.0)
-    act(v("KEEP"), v("ONES"), scale=col(KP))
-    ts(v("C1"), v("jj", 0, 16), 16.0, A.mult)
-    ms(v("CN", 0, 64), 128.0)
-    ms(v("CN", 64, 128), -128.0)
+    ms(v("CN", 0, 64), 128.0 - 128 * 192)
+    ms(v("CN", 64, 128), -128.0 - 128 * 192)
+    cp(v("KT"), v("tB", 0, 128))
+    ts(v("RST"), v("tB", 0, 128), 0.0, A.is_equal, 4194304.0, A.mult)
+    ts(v("OD"), v("tB"), col(K), A.not_equal, -4194304.0, A.mult)
+    ts(v("RS"), v("tB"), 0.0, A.is_equal, -8388608.0, A.mult)
+    ts(v("ODq", 0, 128), v("OD", 0, 128), -3264.0, A.add)
+    ts(v("ODq", 128, 256), v("OD", 0, 128), -12480.0, A.add)
     act(v("tA"), v("tA"), scale=col(M2))
     act(v("tB"), v("tB"), scale=col(M3))
     tt(v("TABq"), v("tA"), v("tB"), A.add)
-    iota(v("RST"), pl, 0, 0)
-    ts(v("RST"), v("RST"), 0.0, A.is_equal, 4194304.0, A.mult)
-    ts(v("ordc", 0, 4), v("jj", 0, 4), 16.0, A.mult, col(K), A.add)
-    ts(v("ordc", 4, 8), v("ordc", 0, 4), -1.0, A.mult, 127.0, A.add)
-    l3 = math.log(3.0)
-    ms(col(T2), 52 * l3)
-    ex = act(v("wc"), v("ordc"), AF.Exp, bias=col(T2), scale=-l3, more=1500)
-    ex2 = act(v("thr"), v("ordr"), AF.Exp, bias=col(T2), scale=-l3)
-    act(v("thr"), v("thr"), scale=3.5)
-    ts(v("DUM", 0, 8), v("jj", 0, 8), 16.0, A.mult, col(K), A.add)
-    ts(v("DUM", 8, 16), v("DUM", 0, 8), 385.0, A.add)
-    ts(v("DUM", 16, 24), v("DUM", 0, 8), 4097.0, A.add)
-    ts(v("DUM", 0, 8), v("DUM", 0, 8), 257.0, A.add)
+    ms(v("RS3"), 0.0)
+    ts(v("RS3", 0, 48, 3), v("ONES", 0, 16), -4096.0, A.mult)
+    ms(v("DW3"), 0.0)
+    ts(v("DW3", 2, 48, 3), v("jj", 0, 16), 16.0, A.mult, col(K), A.add)
+    ms(v("cs"), 0.0)
+    for lo in (LO, HI):
+        iota(v("SENT", lo, lo + 64), [[0, 64]], 1, 0)
+    for lo, hi in ((0, LO), (LO + 64, HI), (HI + 64, 768)):
+        ts(v("SENT", lo, hi), v("ONES", 0, hi - lo), col(N0), A.mult)
+    ts(v("ordc"), v("jj", 0, 8), 16.0, A.mult, col(K), A.add)
+    ms(v("pm"), 1.0 / 3)
+    ms(v("Aq"), 0.0)
+    scan(v("thr"), v("pm"), v("Aq"), A.mult, A.add, 3.5 * 3.0 ** 53)
+    ts(v("pm"), v("OD", 0, 128), 0.0, A.is_equal, 1 / 3.5, A.mult)
+    tt(v("pm"), v("pm"), v("thr"), A.mult)
+    ts(v("Aq"), v("RST"), 0.0, A.is_equal)
+    scan(v("wc"), v("Aq"), v("pm"), A.mult, A.add)
+    ts(v("DUM", 0, 8), v("ordc"), 257.0, A.add)
+    ts(v("DUM", 8, 16), v("ordc"), 385.0, A.add)
+    ts(v("DUM", 16, 24), v("ordc"), 4097.0, A.add)
     ms(v("Fb", 0, 16), 0.0)
-    ms(v("Fb", 4112, 4128), 0.0)
-    ms(v("Y", 256, 520), 0.0)
-    ms(v("x", 256, 264), 0)
-    ms(v("ST", 512, 528), 0.0)
-    ms(v("tabB", 256, 272), 0.0)
-    awz = ms(v("AW"), 0.0)
+    iota(v("Fb", 4112, 4128), [[0, 16]], 0, 0)
+    iota(v("Y", 256, 264), [[0, 8]], 0, 0)
+    iota(v("x", 256, 264), [[0, 8]], 0, 0)
+    iota(v("STv", 256, 272), [[0, 16]], 0, 0)
+    iota(v("inv", 4096, 4097), [[0, 1]], 16384, 0)
+    awz = iota(v("AW"), [[0, 768]], 0, 0)
+    first = act(v("SW0", LO, LO + 64), v("ONES", 0, 64), AF.Silu, scale=col(DLO), more=1300)
     for t in range(RO):
-        act(v("SW%d" % t, CEN + 1, CEN + 65), v("ONES", 0, 64), scale=col(DLO))
-        act(v("SW%d" % t, CEN - 64, CEN), v("ONES", 0, 64), scale=col(DHI))
-    for c in range(P["NS"]):
-        iota(v("cval", 512 * c, 512 * c + 512), [[1, 32], [0, 16]], 64 + 32 * c, 0)
-        j = act(ind(v("inv"), v("offI", 32 * c, 32 * c + 32)), v("cval", 512 * c, 512 * c + 512), AF.Silu, more=1500 if c == 0 else 0)
-        if c == 0:
-            ops[j]["deps"].update({ex: False, ex2: False})
+        if t:
+            act(v("SW%d" % t, LO, LO + 64), v("ONES", 0, 64), scale=col(DLO))
+        act(v("SW%d" % t, HI, HI + 64), v("ONES", 0, 64), scale=col(DHI))
+    for c, e in enumerate(P["INV"]):
+        o = ind(v("inv"), v("offI", 16 * c, 16 * c + 16))
+        if e == "S" or c == 0:
+            iota(v("cval", 256 * c, 256 * c + 256), [[64, 16], [0, 16]], 1024 * c, 0)
+        if e == "S":
+            ops[act(o, v("cval", 256 * c, 256 * c + 256), AF.Silu)]["deps"][first] = False
+        else:
+            ts(o, v("cval", 0, 256), 1.0, A.mult, float(1024 * c), A.add)
 
     fixed.update(("CB", "CF", "ZB", "col", "ONES", "G8"))
     e1 = topo.engines(core, nxt)
@@ -309,194 +356,272 @@ def build(g, core, T, topo):
             ts(s("w"), s("Yi"), 127, A.bitwise_and)
             tt(s("P1"), s("xt"), s("w"), A.mult)
             ts(s("P1"), s("P1"), 3, A.logical_shift_right, 4095, A.bitwise_and)
-            cp(s("iF"), s("P1"))
+            return cp(s("iF"), s("P1"))
 
-        def pickF(c):
-            o = v("Fb", 16 + 1024 * c, 16 + 1024 * c + 1024)
-            gi = ind(v("spr_s"), v("iF", 64 * c, 64 * c + 64))
-            if t == 0 and c < P["VF0"]:
-                cp(o, gi)
+        def eindex(n, x, wb, shift, o1, o2, pf, pi, lst):
+            mm([(o1, cb(shift), wb), (o1, cb(C40), v("ONES", 0, n))])
+            mm([(o2, cb(K1), wb), (o2, cb(K2), wb), (o2, cb(C2032), v("ONES", 0, n))])
+            tt(pf, x, o1, A.mult)
+            tt(pi, pf, o2, A.add)
+            ts(pi, pi, 5, A.logical_shift_right, 4095, A.bitwise_and)
+            cp(lst, pi)
+        pick = lambda onv, o, gi: cp(o, gi) if onv else act(o, gi)
+        ix = [index1(lo, hi) for lo, hi in P["IX"]]
+        gf = [pick(a in P["VF"][t], v("Fb", 16 + 16 * a, 16 + 16 * b), ind(v("spr_s"), v("iF", a, b))) for a, b in P["GF"]]
+        ts(v("vB"), Y, 524288.0, A.is_lt)
+        mm([(ps(5), cb(T64), v("vB"))])
+        mm([(ps(5, 256, 512), cb(T64P), v("vB"))])
+        for i, b in enumerate((6, 4)):
+            tt(v("A1", 256 * i, 256 * i + 256), ps(5, 256 * i, 256 * i + 256), Y, A.mult)
+            mm([(ps(b), cb(ID), v("OD")), (ps(b), cf(FBO), v("A1", 256 * i, 256 * i + 256))])
+            j = scan(v("Tw", 256 * i, 256 * i + 256), v("RS"), ps(b), A.add, A.max)
+            if t and P["o1"][i] >= 0:
+                ops[j]["deps"][ix[P["o1"][i]]] = False
+        act(v("hiB"), ps(6), AF.Relu, bias=159.5, scale=1.0 / 8192)
+        tw = v("Tw", 15, 256, 16)
+        ts(v("tY"), v("Tw", 15, 512, 16), float(128 * 77 * t), A.add)
+        ts(v("txt"), v("tY"), 7, A.logical_shift_right, 4095, A.bitwise_and)
+        ts(v("tw"), v("tY"), 127, A.bitwise_and)
+        tt(v("tP"), v("txt"), v("tw"), A.mult)
+        ts(v("tP"), v("tP"), 3, A.logical_shift_right, 4095, A.bitwise_and)
+        cp(v("lF"), v("tP"))
+        for i in range(2):
+            j = pick(P["FTV"] and i, v("FT", 256 * i, 256 * i + 256), ind(v("spr_s"), v("lF", 16 * i, 16 * i + 16)))
+            if t and i == 0 and P["o2"] >= 0:
+                ops[j]["deps"][gf[P["o2"]]] = False
+        ts(v("tX"), tw, 1.0 / 128, A.mult, -0.496, A.add)
+        ts(v("tE", 0, 16), v("tw", 16, 32), 127.0, A.add)
+        ts(v("tE", 16, 32), v("tw", 0, 16), 25952.0, A.mult, -25952.0, A.add)
+        tt(v("tE", 0, 16), v("tE", 0, 16), v("tX"), A.mult)
+        tt(v("tP2"), v("tE", 0, 16), v("tE", 16, 32), A.add)
+        ts(v("tP2"), v("tP2"), 6, A.logical_shift_right, 4095, A.bitwise_and)
+        cp(v("lE"), v("tP2"))
+        pick(P["ETV"], v("ET"), ind(v("bar_s"), v("lE")))
+        fT = v("FT", 0, 256)
+        for i, b in enumerate((4, 0)):
+            mm([(ps(b), cb(NI), fT), (ps(b), cb(ID), v("FT", 256, 512))], True, False)
+            mm([(ps(b), cb((ID, NI)[i]), v("ET"))], False, True)
+            if i < P["UTV"]:
+                ts(v("UT", 256 * i, 256 * i + 256), ps(b), float(i), A.is_ge, 0.5, A.subtract)
             else:
-                act(o, gi)
-
-        def tails():
-            act(v("fT"), ind(Fw, v("tlW")))
-            mm([(ps(4, 0, 16), zb(ZW1, c), v("fT", c, 256, 16)) for c in range(16)])
-            mm([(ps(4, 16, 32), zb(ZW2, c), v("fT", c, 256, 16)) for c in range(16)])
-            cp(v("uI"), ps(4, 0, 32))
-            ts(v("uI"), v("uI"), 4095, A.bitwise_and)
-            tt(v("uP"), v("uI", 0, 16), v("uI", 16, 32), A.mult)
-            ts(v("uP"), v("uP"), 5, A.logical_shift_right, 255, A.bitwise_and)
-            cp(v("qS"), v("uP"))
-            act(v("hiB"), ps(6), bias=159.508, scale=1.0 / 64)
-            mm([(ps(6), cf(FMX), v("xs")), (ps(6), cb(MH), v("hiB"))], True, False)
-            mm([(ps(6), cb(ID), v("fT"))], False, False)
-            act(v("qrow"), ind(v("TABq"), v("qS")))
-            mm([(ps(6), cb(I256), v("qrow"))], False, True)
-            act(v("pack"), ps(6), bias=col(BPK))
-
-        def slots(lo, hi):
-            s = lambda nm: v(nm, lo, hi)
-            o = ps(4, 256 + lo, 256 + hi)
-            tt(s("dany"), ps(5, lo, hi), s("tmB"), A.is_lt)
-            tt(s("dhi"), ps(5, lo, hi), s("thi"), A.is_lt)
-            mm([(o, cb(MC), s("ONES")), (o, cb(MA), s("dany")), (o, cb(MB), s("dhi"))])
-            scan(s("cum"), s("KEEP"), o, A.mult, A.add, v("cum", lo - 1, lo) if lo else 0.0)
-            tt(s("key"), s("cum"), o, A.mult)
-        index1(0, 64)
-        index1(64, 256)
-        ts(v("wB"), v("w"), 47.0, A.add)
-        mm([(ps(4), cb(SUPH), v("wB")), (ps(4), cb(C40), v("ONES"))])
-        mm([(ps(4, 256, 512), cb(K1), v("wB")), (ps(4, 256, 512), cb(K2), v("wB")), (ps(4, 256, 512), cb(C2032), v("ONES"))])
+                act(v("UT", 256 * i, 256 * i + 256), ps(b), AF.Sign, bias=0.5 - i)
+        ts(v("cc", 0, 16), tw, 262144.0, A.is_ge, 64.0, A.mult)
+        ts(v("cc", 16, 32), tw, 262144.0, A.is_lt, 64.0, A.mult)
+        for e in range(2):
+            tt(v("W2", e, 32, 2), v("tw", 0, 16), v("cc", 16 * e, 16 * e + 16), A.add)
+        if P["UTV"]:
+            ts(v("TH", 0, 32), v("W2"), 15.485, A.max, 15.5, A.subtract)
+        else:
+            ts(v("TH", 0, 32), v("W2"), 15.47, A.max, 15.5, A.subtract)
+        act(v("ab"), v("W2"), AF.Abs, bias=-24.0)
+        ts(v("TH", 32, 64), v("ab"), 7.515 if P["UTV"] > 1 else 7.53, A.max, 7.5, A.subtract)
+        mm([(ps(6, 320, 352), zb(Z16, c), v("UT", c, 512, 16)) for c in range(16)])
+        for e in range(2):
+            tt(v("FL", 32 * e, 32 * e + 32), ps(6, 320, 352), v("TH", e, 64, 2), A.is_gt)
+            scan(v("cs", 18 * e + 1, 18 * e + 17), v("FL", 32 * e, 32 * e + 16), v("FL", 32 * e + 16, 32 * e + 32), A.add, A.add)
+        mm([(ps(6, 384, 432), cb(ID), v("DW3"))] +
+           [(ps(6, 384 + e, 432, 3), cb(m), v("cs", 18 * e + s, 18 * e + 16 + s)) for e in range(2) for m, s in ((L1, 1), (L0, 0))] +
+           [(ps(6, 385, 432, 3), cb(I256), v("FL", b, b + 16)) for b in (32, 48)])
+        scan(v("ow"), v("RS3"), ps(6, 384, 432), A.add, A.max)
+        cp(v("offW"), v("ow", 2, 48, 3))
         if t:
             ts(X, Y, 1.0 / 128, A.mult, -0.496, A.add)
-        tt(v("P2f"), X, ps(4), A.mult)
-        tt(v("P2"), v("P2f"), ps(4, 256, 512), A.add)
-        ts(v("P2"), v("P2"), 5, A.logical_shift_right, 4095, A.bitwise_and)
-        cp(v("iE"), v("P2"))
-        ts(v("vB"), Y, 524288.0, A.is_lt)
-        mm([(ps(6, 256, 512), cb(T64), v("vB"))])
-        mm([(ps(2, 256, 272), zb(Z1, c), v("vB", c, 256, 16)) for c in range(16)] + [(ps(2, 256, 272), cb(BO), v("C1"))])
-        tt(v("xs"), X, ps(6, 256, 512), A.mult)
-        ts(v("tlW"), ps(2, 256, 272), col(TL), A.add)
-        mm([(ps(6), cf(FBO), v("xs"))])
-        ts(v("thi"), v("xs"), 131072.0, A.is_ge, 64.0, A.mult)
-        act(v("tmB"), ps(6, 256, 512))
-        for c, (lo, hi) in enumerate(P["CH"]):
-            for f in range(4):
-                if P["FA"][f] == c:
-                    pickF(f)
-            s = lambda nm: v(nm, 16 * lo, 16 * hi)
-            wd = hi - lo
-            act(s("E"), ind(v("bar_s"), v("iE", lo, hi)))
-            d = ps((0, 1, 7)[c % 3], 0, 16 * wd)
-            mm([(d, cb(ID), v("Fb", 16 + 16 * lo, 16 + 16 * hi)), (d, cb(NI), v("Fb", 15 + 16 * lo, 15 + 16 * hi))])
-            tt(v("UD", 32 * lo, 32 * lo + 16 * wd), d, s("E"), A.is_gt)
-            ts(s("nE"), s("E"), -1.0, A.mult)
-            tt(v("UD", 32 * lo + 16 * wd, 32 * hi), d, s("nE"), A.is_lt)
-            o = ps(2 + c % 2, 0, 2 * wd)
-            mm([(o, zb(Z1, k), v("UD", 32 * lo + k, 32 * hi, 16)) for k in range(1, 16)] +
-               [(ps(2 + c % 2, i * wd, i * wd + wd), cb(H100), v("vB", lo, hi)) for i in range(2)])
-            ts(v("su", 2 * lo, 2 * hi), o, 108.5, A.is_ge, 0.5, A.subtract)
-            o = ps(5, lo, hi)
-            mm([(o, cb(ID), v("wB", lo, hi)), (o, cb(W16), v("su", 2 * lo, 2 * lo + wd)), (o, cb(W16N), v("su", 2 * lo + wd, 2 * hi))])
-            if c == P["TA"]:
-                tails()
-            if hi == P["SL"]:
-                slots(0, hi)
-        slots(P["SL"], 256)
-        mm([(ps(0, 0, 16), zb(ZO, c), v("key", c, 256, 16)) for c in range(16)])
-        ts(v("offW"), ps(0, 0, 16), float(CEN), A.add)
+        tt(v("xs"), ps(5), X, A.mult)
+        mm([(ps(7), cf(FMX), v("xs")), (ps(7), cb(MH), v("hiB"))], True, False)
+        mm([(ps(5, 0, 16), zb(ZW1, c), v("FT", c, 256, 16)) for c in range(16)])
+        mm([(ps(5, 16, 32), zb(ZW2, c), v("FT", c, 256, 16)) for c in range(16)])
+        cp(v("uI"), ps(5, 0, 32))
+        ts(v("uI"), v("uI"), 4095, A.bitwise_and)
+        tt(v("uP"), v("uI", 0, 16), v("uI", 16, 32), A.mult)
+        ts(v("uP"), v("uP"), 5, A.logical_shift_right, 255, A.bitwise_and)
+        cp(v("qS"), v("uP"))
+        mm([(ps(7), cb(ID), fT)], False, False)
+        act(v("qrow"), ind(v("TABq"), v("qS")))
+        mm([(ps(7), cb(I256), v("qrow"))], False, True)
+        act(v("pack"), ps(7), bias=col(BPK))
         sw, lb, gb = "SW%d" % t, "LB%d" % t, "GB%d" % t
         cp(ind(v(sw), v("offW")), v("pack"))
 
         def send(sw=sw, lb=lb):
             return g.remote_dma_fused([
-                RemoteDMATransfer(dst_ids=[did(nxt)], dma_engine_mask=mk1, remote_sem=T.sem.m0, src=T[sw][:, CEN + 1:CEN + 65], dst=T[lb][:, 0:64]),
-                RemoteDMATransfer(dst_ids=[did(prv)], dma_engine_mask=mk2, remote_sem=T.sem.m1, src=T[sw][:, CEN - 64:CEN], dst=T[lb][:, 64:128])],
+                RemoteDMATransfer(dst_ids=[did(nxt)], dma_engine_mask=mk1, remote_sem=T.sem.m0, src=T[sw][:, LO:LO + 64], dst=T[lb][:, 0:64]),
+                RemoteDMATransfer(dst_ids=[did(prv)], dma_engine_mask=mk2, remote_sem=T.sem.m1, src=T[sw][:, HI:HI + 64], dst=T[lb][:, 64:128])],
                 local_sem=T.sem.ls)
         sn = add("G", send, [v(sw)], [], 300, sig="none", extra=[awz])
         add("N", None, [], [v(lb, 0, 64)], 0, sig=("m0", h * (t + 1)), lat=P["net"], extra=[sn])
         add("N", None, [], [v(lb, 64, 128)], 0, sig=("m1", (len(e2) - h) * (t + 1)), lat=P["net"], extra=[sn])
-        if t == 0:
-            for c in range(2 * P["NS"], 16):
-                ts(ind(v("inv"), v("offI", 16 * c, 16 * c + 16)), v("cval", 0, 256), 1.0, A.mult, float(16 * c), A.add)
-            ms(v("inv", 4096, 4097), 320.0)
-        ts(v("w1B"), ps(5), 48.0, A.max, 174.0, A.min)
-        ts(v("ovB"), v("key"), 65.0, A.is_ge)
-        mm([(ps(2), cf(FI), Y), (ps(2), cb(NI), v("wB")), (ps(2), cb(ID), v("w1B"))])
-        act(Y, ps(2))
-        mm([(ps(5), cb(B16), v("ONES")), (ps(5), cb(RSA), v("vB")), (ps(5), cb(BO), v("dany")), (ps(5), cb(ROVB), v("ovB"))])
-        o = ps(5, 256, 512)
-        mm([(o, cb(R15), v("vB")), (o, cb(BO), v("dany")), (o, cb(ROVB), v("ovB"))])
-        act(v("ST", 0, 512), ps(5, 0, 512), scale=1e27)
-        act(v("tabB", 0, 256), v("vB"), bias=col(KV), scale=-1048576.0)
-        dm = ps(7, 256, 512)
-        mm([(dm, cf(FXS), v("xs")), (dm, cb(SUPT), v("tmB")), (dm, cf(FSI), Y)])
+        tt(v("STv", 0, 256), ind(v("SENT"), v("offW")), v("vB"), A.mult)
+        for lo, hi in P["IE"]:
+            s = lambda nm: v(nm, lo, hi)
+            ts(s("wB"), s("w"), 47.0, A.add)
+            eindex(hi - lo, s("x"), s("wB"), SUPH, ps(3, lo, hi), ps(3, 256 + lo, 256 + hi), s("P2f"), s("P2"), s("iE"))
+        dm = ps(0)
+        done = 0
+        bank = 0
+        for c, (lo, hi) in enumerate(P["CH"]):
+            s = lambda nm: v(nm, 16 * lo, 16 * hi)
+            wd = hi - lo
+            for a, b in P["GE"]:
+                if a == lo:
+                    pick(a in P["VE"][t], v("E", 16 * a, 16 * b), ind(v("bar_s"), v("iE", a, b)))
+            f1, f0 = v("Fb", 16 + 16 * lo, 16 + 16 * hi), v("Fb", 15 + 16 * lo, 15 + 16 * hi)
+            d = ps(bank, 0, 16 * wd)
+            bank = 1 - bank
+            mm([(d, cb(ID), f1), (d, cb(NI), f0)])
+            w = 16 * wd // P["VS"]
+            for i in range(0, 16 * wd, w):
+                tt(v("UD", 32 * lo + i, 32 * lo + i + w), ps(1 - bank, i, i + w), v("E", 16 * lo + i, 16 * lo + i + w), A.is_gt)
+            if c in P["SD"]:
+                d = ps(bank, 0, 16 * wd)
+                bank = 1 - bank
+                mm([(d, cb(NI), f1), (d, cb(ID), f0), (d, cb(NI), s("E"))])
+                act(v("UD", 32 * lo + 16 * wd, 32 * hi), d, AF.Sign, bias=-0.5)
+            elif c in P["ND"]:
+                d = ps(bank, 0, 16 * wd)
+                bank = 1 - bank
+                mm([(d, cb(NI), f1), (d, cb(ID), f0)])
+                tt(v("UD", 32 * lo + 16 * wd, 32 * hi), d, s("E"), A.is_gt)
+            else:
+                if c in P["SN"]:
+                    act(s("nE"), s("E"), scale=-1.0)
+                else:
+                    ts(s("nE"), s("E"), -1.0, A.mult)
+                for i in range(0, 16 * wd, w):
+                    tt(v("UD", 16 * (lo + hi) + i, 16 * (lo + hi) + i + w), ps(1 - bank, i, i + w), v("nE", 16 * lo + i, 16 * lo + i + w), A.is_lt)
+            o = ps(2, 0, 2 * wd)
+            mm([(o, zb(Z1, k), v("UD", 32 * lo + k, 32 * hi, 16)) for k in range(1, 16)] +
+               [(ps(2, i * wd, i * wd + wd), cb(H107 if i and c in P["SD"] else H100), v("vB", lo, hi)) for i in range(2)])
+            if P["suS"]:
+                act(v("su", 2 * lo, 2 * hi), o, AF.Sign, bias=-108.5)
+            else:
+                ts(v("su", 2 * lo, 2 * hi), o, 108.5, A.is_ge, 0.5, A.subtract)
+            o = ps(3, lo, hi)
+            mm([(o, cb(ID), v("wB", lo, hi)), (o, cb(W16), v("su", 2 * lo, 2 * lo + wd)), (o, cb(W16N), v("su", 2 * lo + wd, 2 * hi))])
+            if hi in P["YQ"]:
+                o = ps(3, 256 + done, 256 + hi)
+                ts(v("w1B", done, hi), ps(3, done, hi), 48.0, A.max, 174.0, A.min)
+                if P["YV"]:
+                    mm([(o, cb(NI), v("wB", done, hi)), (o, cb(ID), v("w1B", done, hi))])
+                    tt(v("Y", done, hi), o, v("Y", done, hi), A.add)
+                else:
+                    mm([(o, cf(FI), v("Y", done, hi)), (o, cb(NI), v("wB", done, hi)), (o, cb(ID), v("w1B", done, hi))])
+                    act(v("Y", done, hi), o)
+                done = hi
+        dm = ps(bank)
+        mm([(dm, cf(FXS), v("xs")), (dm, cb(SUPT), v("vB"))], True, False)
+        for lo, hi in zip((0,) + P["YQ"], P["YQ"]):
+            mm([(ps(bank, lo, hi), cf(FSI), v("Y", lo, hi))], False, hi == 256)
         L = v(lb)
-        ts(v("metaB"), L, 1.0 / 256, A.mult, 143.502, A.add)
-        mm([(ps(0, 0, 128), cb(RQB), v("metaB"))])
-        mm([(ps(3, 0, 128), cb(RQB), v("metaB"))])
-        ts(v("lq"), ps(0, 0, 128), 16.0, A.mult, col(QK), A.add)
-        act(v("R", 1, 256, 2), ps(3, 0, 128), bias=-2448.0)
-        ops[act(v("Fq", 0, 1024), ind(Fw, v("lq", 0, 64)))]["up"] = P["u1"]
-        ops[act(v("Fq", 1024, 2048), ind(Fw, v("lq", 64, 128)))]["up"] = P["u1"]
-        mm([(ps(1, 0, 8), zb(ZN, c), v("metaB", c, 128, 16)) for c in range(16)] + [(ps(1, 0, 8), cb(BO), v("CN", 0, 128, 16))])
-        ts(v("nmW"), ps(1, 0, 8), -9360.0, A.add)
-        ts(v("R", 0, 256, 2), ind(v("inv", 0, 4104), v("nmW")), MAGIC, A.add, MAGIC + 64, A.subtract)
-        ts(v("Wf", 16, 24), ps(1, 0, 8), -9360.0, A.add)
-        mm([(ps(4, 0, 8), zb(ZQ, c), v("metaB", c, 128, 16)) for c in range(16)])
-        ts(v("Wf", 8, 16), ps(4, 0, 8), -2448.0, A.add)
-        mm([(ps(1, 0, 8), zb(Z0, c), v("R", 2 * c, 256, 32)) for c in range(16)])
-        rng = [(16 * u, 128) for u in range(4)] + [(64, 16 * u + 16) for u in range(4, 8)]
+        ts(v("metaB"), L, 1.0 / 256, A.mult, 191.502, A.add)
+        o = ps(7, 256, 384)
+        mm([(ps(7, 256, 512), cb(ID), v("ODq")), (o, cb(RQB), v("metaB")), (ps(7, 384, 512), cb(RNB), v("metaB")), (ps(7, 384, 512), cb(BO), v("CN"))])
+        scan(v("Wf", 128, 384), v("RS"), ps(7, 256, 512), A.add, A.max)
+        cp(v("AQ", 8, 24), v("Wf", 143, 384, 16))
+        if P["RS"]:
+            act(v("R", 0, 256, 2), ind(v("inv", 0, 4104), v("AQ", 16, 24)), scale=1.0 / 64)
+        else:
+            ts(v("R", 0, 256, 2), ind(v("inv", 0, 4104), v("AQ", 16, 24)), 1.0 / 64, A.mult)
+        mm([(ps(6, 0, 128), cb(RQB), v("metaB"))])
+        mm([(ps(5, 0, 128), cb(RQB), v("metaB"))])
+        ts(v("lq"), ps(6, 0, 128), 16.0, A.mult, col(QK), A.add)
+        act(v("R", 1, 256, 2), ps(5, 0, 128), bias=-3264.0)
+        for i in range(0, 128, P["GQ"]):
+            act(v("Fq", 16 * i, 16 * (i + P["GQ"])), ind(Fw, v("lq", i, i + P["GQ"])))
+        act(v("SG", 128, 256), ind(v("STv"), v("AQ", 8, 16)))
+        mm([(ps(6, 128, 256), cb(ID), v("OD", 0, 128)), (ps(6, 128, 256), cb(ID), v("R", 0, 256, 2))])
 
         def clash(j, u, first):
-            lo, hi = rng[u]
+            lo = 16 * u
             b = 256 * (8 * j + u)
-            ts(v("OH", b, b + 2 * (hi - lo)), v("R", 2 * lo, 2 * hi), v("Wf", 8 * j + u, 8 * j + u + 1), A.is_equal, v("wc", u, u + 1), A.mult)
-            mm([(ps(6, lo, hi), cb(BO), v("OH", b + i, b + 2 * (hi - lo), 2)) for i in range(2)], first, False)
+            i = 128 * j + 16 * u + 15
+            ts(v("OH", b, b + 2 * (128 - lo)), v("R", 2 * lo, 256), v("Wf", i, i + 1), A.is_equal, v("wc", 16 * u + 15, 16 * u + 16), A.mult)
+            mm([(ps(5, lo, 128), cb(BO), v("OH", b + i, b + 2 * (128 - lo), 2)) for i in range(2)], first, False)
+        scan(v("Wf", 0, 128), v("RS", 0, 128), ps(6, 128, 256), A.add, A.max)
         for u in range(8):
             clash(1, u, u == 0)
-        cp(v("Wf", 0, 8), ps(1, 0, 8))
+        cp(v("AQ", 0, 8), v("Wf", 15, 128, 16))
+        act(v("SG", 0, 128), ind(v("STv"), v("AQ", 0, 8)))
         for u in range(8):
             clash(0, u, False)
-        cp(v("AQ"), v("Wf", 0, 16))
-        cp(v("SG", 128, 256), ind(v("ST", 256, 528), v("AQ", 8, 16)))
-        cp(v("SG", 0, 128), ind(v("ST", 0, 272), v("AQ", 0, 8)))
-        mm([(ps(6, 0, 128), cb(BO), v("SG", 128, 256)), (ps(6, 0, 128), cb(BO), v("SG", 0, 128))], False, True)
-        ops[tt(v(gb), ps(6, 0, 128), v("thr"), A.is_lt)]["up"] = P["u3"]
+        mm([(ps(5, 0, 128), cb(FQ), v("SG", 128, 256)), (ps(5, 0, 128), cb(FA), v("SG", 0, 128))], False, True)
+        tt(v(gb), ps(5, 0, 128), v("thr"), A.is_lt)
 
         def ack(gb=gb):
             return g.remote_dma_fused([
-                RemoteDMATransfer(dst_ids=[did(nxt)], dma_engine_mask=mk1, remote_sem=T.sem.k0, src=T[gb][:, 64:128], dst=T.AW[:, CEN - 64:CEN]),
-                RemoteDMATransfer(dst_ids=[did(prv)], dma_engine_mask=mk2, remote_sem=T.sem.k1, src=T[gb][:, 0:64], dst=T.AW[:, CEN + 1:CEN + 65])],
+                RemoteDMATransfer(dst_ids=[did(nxt)], dma_engine_mask=mk1, remote_sem=T.sem.k0, src=T[gb][:, 64:128], dst=T.AW[:, HI:HI + 64]),
+                RemoteDMATransfer(dst_ids=[did(prv)], dma_engine_mask=mk2, remote_sem=T.sem.k1, src=T[gb][:, 0:64], dst=T.AW[:, LO:LO + 64])],
                 local_sem=T.sem.ls)
         an = add("G", ack, [v(gb)], [], 300, sig="none")
-        add("N", None, [], [v("AW", CEN - 64, CEN)], 0, sig=("k0", h * (t + 1)), lat=P["net"], extra=[an])
-        add("N", None, [], [v("AW", CEN + 1, CEN + 65)], 0, sig=("k1", (len(e2) - h) * (t + 1)), lat=P["net"], extra=[an])
-        o = ps(0, 128, 256)
+        add("N", None, [], [v("AW", HI, HI + 64)], 0, sig=("k0", h * (t + 1)), lat=P["net"], extra=[an])
+        add("N", None, [], [v("AW", LO, LO + 64)], 0, sig=("k1", (len(e2) - h) * (t + 1)), lat=P["net"], extra=[an])
+        o = ps(4, 0, 128)
         mm([(o, cf(FI), L), (o, cb(NI256), v("metaB")), (o, cb(C2304), v("ONES", 0, 128))])
-        mm([(ps(3, 0, 128), cb(TM), cb(ID))] + [(ps(3, k, 128, 16), v("Fq", k, 2048, 16), v("G8", 8, 16)) for k in range(16)], True, False)
+        mm([(ps(7, 0, 128), cb(ID), v("KT")), (ps(7, 0, 128), v("SG", 128, 256), cb(NDG))], True, False)
+        mm([(ps(7, k, 128, 16), v("Fq", k, 2048, 16), v("G8", 8, 16)) for k in range(16)], False, False)
+        for k in range(P["MH"]):
+            tt(v("Mx", 128 * k, 128 * k + 64), v("Fq", k, 1024, 16), ps(4, 0, 64), A.max)
         for k in range(16):
-            tt(v("Mx", 128 * k, 128 * k + 64), v("Fq", k, 1024, 16), ps(0, 128, 192), A.max)
-        for k in range(16):
-            tt(v("Mx", 128 * k + 64, 128 * k + 128), v("Fq", 1024 + k, 2048, 16), ps(0, 192, 256), A.max)
-            mm([(ps(3, k, 128, 16), v("Mx", 128 * k, 128 * k + 128), v("G8", 16, 24))], False, False)
-        act(v("tq"), ind(v("tabB"), v("AQ", 8, 16)))
-        mm([(ps(3, 0, 128), v("tq"), cb(ID))], False, True)
-        mm([(ps(2, 0, 128), cb(RNB), v("metaB")), (ps(2, 0, 128), cb(BO), v("CN"))])
-        act(v("nmS"), ps(2, 0, 128), bias=-9360.0)
-        ops[act(v("Yaq"), ind(v("Y"), v("AQ")))]["up"] = P["u2"]
-        mm([(ps(5, 0, 128), cf(FI), v("Yaq", 128, 256)), (ps(5, 0, 128), cf(FN128), v("nmS"))])
-        act(v("Dq"), ps(5, 0, 128), bias=-33.0)
-        scan(v("pm"), v("RST"), ps(3, 0, 128), A.add, A.min)
-        for j in range(8):
-            ts(v("mT", 16 * j, 16 * j + 16), v("pm", 16 * j, 16 * j + 16), v("pm", 16 * j + 15, 16 * j + 16), A.is_equal)
-        mm([(ps(6, 0, 128), v("mT"), cb(ID))])
-        mm([(ps(2, 0, 128), cf(FI), v("Yaq", 128, 256))], True, False)
-        tt(v("Aq"), ps(6, 0, 128), v("Dq"), A.mult)
-        mm([(ps(2, 0, 128), cf(FSI), v("Aq"))], False, True)
-        act(v("Yn"), ps(2, 0, 128))
-        mm([(ps(1, 0, 8), zb(Z0, c), v(gb, c, 128, 16)) for c in range(16)])
-        tt(v("Dif"), v("Wf"), v("DUM"), A.subtract)
+            lo = 64 if k < P["MH"] else 0
+            tt(v("Mx", 128 * k + lo, 128 * k + 128), v("Fq", k + 16 * lo, 2048, 16), ps(4, lo, 128), A.max)
+            if k % 4 == 3:
+                mm([(ps(7, i, 128, 16), v("Mx", 128 * i, 128 * i + 128), v("G8", 16, 24)) for i in range(k - 3, k + 1)], False, k == 15)
+        mm([(ps(6, 256, 384), cb(RNB), v("metaB")), (ps(6, 256, 384), cb(BO), v("CN"))])
+        act(v("nmS"), ps(6, 256, 384), bias=-12480.0)
+        tt(v("eqB"), ind(v("x"), v("AQ", 0, 8)), v("nmS"), A.is_equal)
+        mm([(ps(6, 384, 512), cb(LT), v("eqB"))])
+        act(v("mA"), ps(6, 384, 512))
+        mm([(ps(6, 128, 256), cb(ID), v("OD", 0, 128)), (ps(6, 128, 256), cb(ID), v(gb))])
+        scan(v("gw"), v("RS", 0, 128), ps(6, 128, 256), A.add, A.max)
+        tt(v("Dif"), v("Wf", 15, 384, 16), v("DUM"), A.subtract)
         nl = 3 if t < RO - 1 else 2
         for j in range(nl):
-            tt(v("L3f", 8 * j, 8 * j + 8), v("Dif", 8 * j, 8 * j + 8), ps(1, 0, 8), A.mult)
+            tt(v("L3f", 8 * j, 8 * j + 8), v("Dif", 8 * j, 8 * j + 8), v("gw", 15, 128, 16), A.mult)
         tt(v("L3f", 0, 8 * nl), v("L3f", 0, 8 * nl), v("DUM", 0, 8 * nl), A.add)
         cp(v("L3", 0, 8 * nl), v("L3f", 0, 8 * nl))
-        tt(v("eqB"), ind(v("x"), v("AQ", 0, 8)), v("nmS"), A.is_equal)
-        mm([(ps(4, 0, 128), cf(FDI), v("Yaq", 0, 128))])
-        act(v("Dd"), ps(4, 0, 128), bias=col(B15))
-        mm([(ps(4, 128, 256), cb(LT), v("eqB"))])
-        tt(v("ta"), ps(4, 128, 256), v("Dd"), A.mult)
-        tt(ind(v("Y"), v("L3", 0, 8)), v("ta"), v("Yaq", 0, 128), A.add)
+        scan(v("pm"), v("RST"), ps(7, 0, 128), A.add, A.min)
+        for j in range(8):
+            o, i, m = v("mT", 16 * j, 16 * j + 16), v("pm", 16 * j, 16 * j + 16), v("pm", 16 * j + 15, 16 * j + 16)
+            if j < P["mTS"]:
+                act(o, i, AF.Sign, bias=m, scale=-1.0)
+            else:
+                ts(o, i, m, A.is_equal, 1.0, A.subtract)
+        if P["DQ"]:
+            mm([(ps(6, 0, 128), cb(ID), v("ONES", 0, 128)), (ps(6, 0, 128), v("mT"), cb(ID))])
+        else:
+            mm([(ps(6, 0, 128), v("mT"), cb(ID))])
+            act(v("mQ"), ps(6, 0, 128), bias=1.0)
+        bq = 1 - bank if P["DQ"] else 4
+        o = ps(bq, 128, 256)
+        mm([(o, cb(RN128), v("metaB")), (o, cb(B128), v("CN")), (o, cb(CTB), v("ONES", 0, 128))], True, False)
+        mm([(ps(5, 128, 256), cb(E15), v("ONES", 0, 128))], True, False)
+        if P["Y1"]:
+            act(v("Yaq"), ind(v("Y"), v("AQ", 0, 16)))
+        else:
+            act(v("Yaq", 128, 256), ind(v("Y"), v("AQ", 8, 16)))
+            act(v("Yaq", 0, 128), ind(v("Y"), v("AQ", 0, 8)))
+        mm([(o, cf(FI), v("Yaq", 128, 256))], False, True)
+        mm([(ps(5, 128, 256), cf(FDI), v("Yaq", 0, 128))], False, True)
+        if P["DQ"]:
+            act(v("Dq"), o)
+            tt(v("Aq"), ps(6, 0, 128), v("Dq"), A.mult)
+        else:
+            tt(v("Aq"), o, v("mQ"), A.mult)
+        mm([(ps(7, 128, 256), cf(FSI), v("Aq"))])
+        act(v("Yn"), ps(7, 128, 256))
         act(v("tm2"), ind(v("AW"), v("offW")))
         tt(dm, v("tm2"), dm, A.mult)
-        tt(Y, Y, dm, A.add)
-        cp(ind(v("Y"), v("L3", 8, 16)), v("Yn"))
+        tt(v("ta"), ps(5, 128, 256), v("mA"), A.mult)
+        edits = [lambda: tt(ind(v("Y"), v("L3", 0, 8)), v("ta"), v("Yaq", 0, 128), A.add),
+                 lambda: tt(ind(v("Y"), v("L3", 8, 16)), v("Yn"), v("Yaq", 128, 256), A.add)]
+        edits.insert(P["rl"], lambda: tt(Y, Y, dm, A.add))
+        for f in edits:
+            f()
         if t < RO - 1:
-            act(v("qF"), v("R", 1, 256, 2), bias=64.0)
-            cp(ind(v("inv", 0, 4232), v("L3", 16, 24)), v("qF"))
+            act(v("qF"), v("R", 1, 256, 2), scale=64.0)
+            if P["ivS"]:
+                ops[act(ind(v("inv", 0, 4232), v("L3", 16, 24)), v("qF"), AF.Silu)]["up"] = 1200.0
+            else:
+                cp(ind(v("inv", 0, 4232), v("L3", 16, 24)), v("qF"))
 
     now[0] = RO
     ts(X, Y, 1.0 / 128, A.mult, 0.504, A.add)
@@ -515,6 +640,19 @@ def build(g, core, T, topo):
 
 
 def schedule(ops):
+    order, total, seen = [], 0.0, {}
+    for t in range(RO):
+        idx = [i for i, o in enumerate(ops) if min(o["t"], RO - 1) == t]
+        tags = tuple(ops[i]["tag"] for i in idx)
+        if tags not in seen:
+            sub = [dict(ops[i], deps={j - idx[0]: w for j, w in ops[i]["deps"].items() if j >= idx[0]}) for i in idx]
+            seen[tags] = arrange(sub)
+        order += [(idx[0] + i, total + s) for i, s in seen[tags][0]]
+        total += seen[tags][1]
+    return order, total
+
+
+def arrange(ops):
     n = len(ops)
     cost = [o["cost"] for o in ops]
     eng = [o["eng"] for o in ops]
@@ -525,84 +663,85 @@ def schedule(ops):
             if d > cost[j]:
                 far.update(ops[j]["deps"])
         pre[i] = [(j, d) for j, d in pre[i] if j not in far or ops[j]["lat"] > 100]
-    suc = [[] for _ in range(n)]
+    lat = [o["lat"] - o["up"] for o in ops]
+    post = [[] for _ in range(n)]
     for i in range(n):
         for j, d in pre[i]:
-            suc[j].append(i)
+            post[j].append((i, d + cost[i] - cost[j]))
 
-    def place(key):
+    def place(order, edges, first):
         st = [0.0] * n
-        why = [-1] * n
         busy = {e: [] for e in set(eng)}
-        for i in sorted(range(n), key=lambda i: (-key[i], i)):
-            s, y = 0.0, -1
-            for j, d in pre[i]:
+        for i in order:
+            s = first[i]
+            for j, d in edges[i]:
                 if st[j] + d > s:
-                    s, y = st[j] + d, j
+                    s = st[j] + d
             if eng[i] != "N":
                 b = busy[eng[i]]
+                c = cost[i]
                 k = len(b)
                 while k > 0 and b[k - 1][1] > s:
                     k -= 1
-                while k < len(b) and b[k][0] < s + cost[i]:
-                    if b[k][1] > s:
-                        s, y = b[k][1], -2 - b[k][2]
+                while k < len(b) and b[k][0] < s + c:
+                    s = b[k][1]
                     k += 1
-                b.insert(k, (s, s + cost[i], i))
-            st[i], why[i] = s, y
-        z = max(range(n), key=lambda i: st[i] + cost[i] + ops[i]["lat"])
-        return st, why, z, st[z] + cost[z] + ops[z]["lat"]
+                b.insert(k, (s, s + c))
+            st[i] = s
+        return st
+    zero = [0.0] * n
+    cases = []
+    for f, gc, sc, pe, call, hop, net in P["cases"]:
+        c = [(o["cost"] + P["cyc"] * (o["g"] * (gc - P["g"]) + o["sc"] * (sc - P["sc"]))) * f * (pe if o["eng"] == "P" else 1.0) + call * (o["eng"] in "VS")
+             for o in ops]
+        e = [[(j, c[j] + ((d > cost[j]) and hop + ops[j]["lat"] * (net if ops[j]["lat"] > 100 else 1.0))) for j, d in pre[i]] for i in range(n)]
+        cases.append((c, e, f))
+
+    def end(st):
+        order = sorted(range(n), key=lambda i: (st[i], i))
+        z = max(st[i] + cost[i] + lat[i] for i in range(n))
+        for c, e, f in cases:
+            s2, free = [0.0] * n, dict.fromkeys(eng, 0.0)
+            for i in order:
+                s = free[eng[i]]
+                for j, d in e[i]:
+                    if s2[j] + d > s:
+                        s = s2[j] + d
+                s2[i] = s
+                if eng[i] != "N":
+                    free[eng[i]] = s + c[i]
+            z += max(s2[i] + c[i] + lat[i] for i in range(n)) / f
+        return z / (1 + len(cases))
     key = [0.0] * n
-    for more in (1.0, 0.0):
+    for i in range(n - 1, -1, -1):
+        for j, d in pre[i]:
+            key[j] = max(key[j], key[i] + d + 1e-3)
+    cur = place(sorted(range(n), key=lambda i: (-key[i], i)), pre, zero)
+    best, seed = cur, 12345
+    ec = eb = end(cur)
+    for it in range(P["it"]):
+        seed = (seed * 1103515245 + 12345) % 2147483648
+        if (seed >> 8) % 8 < P["jb"]:
+            back = place(sorted(range(n), key=lambda i: (-cur[i] - cost[i], -i)), post, lat)
+            key = [-back[i] - cost[i] for i in range(n)]
+        else:
+            key = list(cur)
+        for _ in range(P["shake"]):
+            seed = (seed * 1103515245 + 12345) % 2147483648
+            i = (seed >> 8) % n
+            seed = (seed * 1103515245 + 12345) % 2147483648
+            key[i] -= (seed >> 8) % P["rnd"]
         for i in range(n - 1, -1, -1):
             for j, d in pre[i]:
-                key[j] = max(key[j], key[i] + d * more + 1e-3)
-        key = [key[i] + ops[i]["up"] * more for i in range(n)]
-    twin = {(o["t"], o["tag"]): i for i, o in enumerate(ops)}
-    cur = place(key)
-    best = cur
-    seed = 12345
-    for it in range(P["it"]):
-        held, i = [], cur[2]
-        while i != -1:
-            y = cur[1][i]
-            if y < -1:
-                y = -2 - y
-                held.append((i, y))
-            i = y
-        seed = (seed * 1103515245 + 12345) % 2147483648
-        i, y = held[(seed >> 8) % len(held)]
-        k2 = list(key)
-        todo = []
-        dt = ops[y]["t"] - ops[i]["t"]
-        pairs = [(i, y)]
-        if seed % 5 < P["tw"]:
-            pairs = [(twin[r, ops[i]["tag"]], twin[r + dt, ops[y]["tag"]]) for r in range(RO + 1)
-                     if (r, ops[i]["tag"]) in twin and (r + dt, ops[y]["tag"]) in twin]
-        for i, y in pairs:
-            if seed % 3:
-                k2[i] = max(k2[i], k2[y] + 1e-3 + (seed % 7) * P["rnd"])
-                todo.append(i)
-            else:
-                k2[y] = min(k2[y], k2[i] - 1e-3 - (seed % 7) * P["rnd"])
-                todo.append(y)
-        while todo:
-            a = todo.pop()
-            for j, d in pre[a]:
-                if k2[j] <= k2[a]:
-                    k2[j] = k2[a] + 1e-3
-                    todo.append(j)
-            for j in suc[a]:
-                if k2[j] >= k2[a]:
-                    k2[j] = k2[a] - 1e-3
-                    todo.append(j)
-        new = place(k2)
-        if new[3] <= cur[3] + P["tol"] * (1.0 - it / P["it"]):
-            cur, key = new, k2
-            if new[3] < best[3]:
-                best = new
-    st = best[0]
-    return [(i, st[i]) for i in sorted(range(n), key=lambda i: (st[i], i))], best[3]
+                if key[i] < key[j]:
+                    key[j] = key[i]
+        new = place(sorted(range(n), key=lambda i: (key[i], i)), pre, zero)
+        en = end(new)
+        if en <= ec + P["tol"] * (1.0 - it / P["it"]):
+            cur, ec = new, en
+            if en < eb:
+                best, eb = new, en
+    return [(i, best[i]) for i in sorted(range(n), key=lambda i: (best[i], i))], eb
 
 
 def rank_program(g, core, T, topo):

@@ -6,20 +6,22 @@ RO = 4
 LO, HI = 256, 512
 MAGIC = 12582912.0
 BF, F32, I32, U16 = "bfloat16", "float32", "int32", "uint16"
-P = {"it": 9000, "rnd": 5000, "tol": 250.0, "shake": 1, "jb": 2, "INV": "SSSSSSSSSSVVVVVV", "cyc": 0.87, "pe": 0.44, "g": 1.56, "sc": 3.8, "hop": 110.0, "self": 110.0, "net": 2700.0,
+P = {"it": 18000, "rnd": 3000, "tol": 60.0, "pm": 2, "jb": 1, "seed": 12345, "INV": "SSSSSVVV", "cyc": 0.92, "pe": 0.49, "g": 1.56, "sc": 3.8, "hop": 90.0, "self": 90.0, "net": 2300.0,
      "CH": [(32 * c, 32 * c + 32) for c in range(8)], "YQ": (64, 128, 192, 256), "VF": ((), (), (), ()), "VE": ((), (), (), ()),
-     "IX": ((0, 64), (64, 128), (128, 256)), "IE": ((0, 128), (128, 256)), "SD": (), "ND": (), "FTV": 0, "ETV": 0, "UTV": 0, "suS": 0, "RS": 1, "ivS": 0, "mTS": 0,
-     "cut": 256, "VS": 1, "YV": 1, "DQ": 1, "MH": 8, "Y1": 1, "GF": [(64 * c, 64 * c + 64) for c in range(4)], "GE": [(32 * c, 32 * c + 32) for c in range(8)], "GQ": 64, "rl": 0,
-     "o1": (-1, -1), "o2": -1, "SN": (), "CS": 4, "sfix": 170.0, "EV": "",
-     "cases": ((1.4, 1.9, 5.6, 1.0, 0.0, 110.0, 1.0), (1.0, 1.15, 2.0, 1.1, 25.0, 190.0, 1.3), (1.15, 1.95, 2.2, 1.1, 25.0, 80.0, 0.8))}
+     "IX": ((0, 64), (64, 128), (128, 256)), "IE": ((0, 128), (128, 256)), "SD": (), "ND": (0, 1), "FT": ((0, 16), (16, 32)), "ETV": 0, "UTV": 1, "suS": 0, "RS": 1, "ivS": 1, "mTS": 4,
+     "cut": 256, "VS": 1, "YV": 1, "DQ": 1, "MH": 15, "Y1": 0, "GF": [(64 * c, 64 * c + 64) for c in range(4)], "GE": [(32 * c, 32 * c + 32) for c in range(8)], "GQ": 64, "rl": 2,
+     "o1": (-1, -1), "o2": -1, "SN": (), "CS": 4, "sfix": 90.0, "EV": "",
+     "TV": 0, "PW": 256, "first": 2500.0,
+     "cases": ((1.25, 1.8, 5.2, 1.1, 0.0, 60.0, 0.85), (0.93, 1.25, 2.6, 1.0, 0.0, 210.0, 1.7), (1.1, 1.95, 2.2, 0.95, 5.0, 120.0, 1.3),
+               (1.0, 1.2, 5.2, 1.05, 0.0, 80.0, 2.3), (1.25, 1.1, 1.9, 1.12, 0.0, 50.0, 0.8))}
 
 SB, POOL = {}, {}
 for _d, _l in ((BF, "spr_s 4096 bar_s 4096 wt_s 2 Fb 4128 E 4096 nE 4096 UD 8192 STv 272 SENT 768 AW 768 OH 4096 Fq 2048 Mx 2048 CB 6144 ZB 1008 "
-                    "TABq 256 GB0 128 GB1 128 GB2 128 GB3 128 FT 512 ET 256 UT 512 tmB 256 qrow 256 SG 256 G8 24 ONES 256 | wB 256 vB 256 hiB 256 su 512 w1B 256 "
-                    "metaB 128 R 256 eqB 128 mT 128 CN 128 OD 256 ODq 256 KT 128 mA 128 mQ 128 cc 32 FL 64 cs 36 DW3 48"),
-               (F32, "Y 520 Yaq 256 ta 128 Yn 128 tm2 256 qF 128 pack 256 nmS 128 inv 8320 cval 4096 o2 256 o3 256 o4 256 CF 1152 col 48 "
-                     "SW0 768 SW1 768 SW2 768 SW3 768 LB0 128 LB1 128 LB2 128 LB3 128 | P2f 256 xs 256 A1 512 Tw 512 RS 256 W2 32 Wf 384 gw 128 Dif 24 L3f 24 "
-                     "pm 128 Aq 128 Dq 128 o1 256 mg 128 jj 144 wtf 2 tA 256 tB 256 RST 128 thr 128 ordc 8 wc 128 DUM 24 tE 32 ab 32 TH 64 "
+                    "TABq 256 GB0 128 GB1 128 GB2 128 GB3 128 FT 512 ET 256 UT 512 SG 256 G8 24 ONES 256 | wB 256 vB 256 hiB 256 su 512 w1B 256 "
+                    "metaB 128 R 256 eqB 128 mT 128 CN 128 OD 256 ODq 256 tA 256 tB 256 RST 128 RS 256 mA 128 mQ 128 cc 32 FL 64 cs 36 DW3 48"),
+               (F32, "Y 520 Yaq 256 ta 128 Yn 128 tm2 256 qF 128 pack 256 qrow 256 dmS 256 nmS 128 inv 8320 cval 4096 o2 256 o3 256 o4 256 CF 1152 col 48 "
+                     "SW0 768 SW1 768 SW2 768 SW3 768 LB0 128 LB1 128 LB2 128 LB3 128 | P2f 256 xs 256 A1 512 Tw 512 W2 32 Wf 384 gw 128 Dif 24 L3f 24 "
+                     "pm 128 Aq 128 Dq 128 o1 256 mg 128 jj 144 wtf 2 thr 128 ordc 8 wc 8 DUM 24 tE 32 ab 32 TH 64 "
                      "RS3 48 ow 48"),
                (I32, "lam_s 256 mon_s 256 x 264 | Yi 256 xt 256 w 256 P1 256 P2 256 uI 32 uP 16 Jt 256 pI 2 tY 32 txt 32 tw 32 tP 32 tX 16 tP2 16"),
                (U16, "iF 256 iE 256 lF 32 lE 16 qS 16 offW 16 lq 128 AQ 24 L3 24 offI 256 |")):
@@ -35,7 +37,7 @@ for _d, _l in ((BF, "spr_s 4096 bar_s 4096 wt_s 2 Fb 4128 E 4096 nE 4096 UD 8192
 SCRATCH = {k: ("sbuf", [128, n], d) for k, (n, d) in SB.items()}
 for _b in range(8):
     SCRATCH["PS%d" % _b] = ("psum", [128, 512], F32)
-SEMAPHORES = ["cV", "cS", "cP", "cG", "ls", "m0", "m1", "k0", "k1", "d0", "d1", "d2", "d3", "d4", "d5", "d6", "d7"]
+SEMAPHORES = ["cV", "cS", "cP", "cG", "ls", "m0", "m1", "k0", "k1", "d0", "d1", "d2", "d3", "d4", "d5", "d6", "d7", "d8"]
 PLAN = {}
 
 
@@ -187,7 +189,8 @@ def build(g, core, T, topo):
     dma("S", T.mon_s[:], T.mon[:], [], [v("mon_s")], "d1", 2200)
     dma("S", T.wt_s[:], T.wt[:], [], [v("wt_s")], "d2", 2200)
     d3 = dma("Y", T.spr_s[:], T.spr[:], [], [v("spr_s")], "d3", 6500)
-    d4 = dma("Y", T.bar_s[:], T.bar[:], [], [v("bar_s")], "d4", 11000)
+    d4 = dma("Y", T.bar_s[:, 0:2752], T.bar[:, 1344:4096], [], [v("bar_s", 0, 2752)], "d4", 9500)
+    ops[dma("Y", T.bar_s[:, 2752:4096], T.bar[:, 0:1344], [], [v("bar_s", 2752, 4096)], "d8", 11000)]["deps"][d4] = False
     ops[d3]["deps"][d0] = False
     ops[d4]["deps"][d3] = False
 
@@ -233,8 +236,8 @@ def build(g, core, T, topo):
     lin(CQ, [(0, big), (15, big)])
     lin(CT, [(0, 128 * 12480), (1, -33)])
     cp(v("wtf"), v("wt_s"))
-    (BO, ID, NI, H100, H107, SUPH, C40, K1, K2, C2032, T64, T64P, W16, W16N, MH, I256, SUPT, LT, RQB, RNB, RN128, B128, NI256, C2304,
-     SUP, SDN, BSI, BDI, E0, E1, E15, FA, FQ, CTB, NDG, L1, L0, TN) = range(38)
+    (BO, ID, NI, H100, H107, SUPH, N127, K1, K2, C2032, T64, T64P, W16, W16N, MH, I256, SUPT, LT, RQB, RNB, RN128, B128, NI256, C2304,
+     SUP, SDN, BSI, BDI, E0, E1, E15, FA, FQ, CTB, NDG, L1, L0, D2, D3, TN) = range(40)
     (FI, FBO, FMX, FSI, FXS, FDI) = range(6)
     dif, pl = [[1, 128]], [[0, 8], [1, 16]]
     ts(cb(BO), v("mg"), col(GR), A.is_equal)
@@ -250,20 +253,20 @@ def build(g, core, T, topo):
     tt(cb(TN), cb(SDN), cb(TN), A.subtract)
     ts(cb(T64P), cb(TN), 64.0, A.mult)
     sel(cb(TN), cb(BO), pl, A.is_equal, 0.0, -15, 0)
-    ts(cb(E15), cb(TN), 32768.0, A.mult)
-    for d, s, c in ((NI, ID, -1.0), (H100, ID, 100.0), (K1, ID, 12288.0), (K2, ID, 688.0), (I256, ID, 256.0), (C40, BO, 2.5), (C2032, BO, 2032.0),
+    ts(cb(E15), cb(TN), 65536.0, A.mult)
+    for d, s, c in ((N127, ID, -127.0),) * (P["PW"] < 256) + ((NI, ID, -1.0), (H100, ID, 100.0), (K1, ID, 12288.0), (K2, ID, 688.0), (I256, ID, 256.0),
                     (SUPH, SUP, 0.5), (T64, BDI, -64.0), (W16, BDI, -8.0 if P["suS"] else -16.0), (W16N, BDI, 8.0 if P["suS"] else 16.0), (NI256, ID, -256.0),
                     (C2304, BO, 3072.0), (RQB, BO, col(RQ)), (RNB, BO, col(RN)), (RN128, RNB, -128.0), (B128, BO, -128.0),
                     (FA, BO, col(CA)), (FQ, BO, col(CQ)), (CTB, BO, col(CT))) + ((H107, ID, 107.0),) * (len(P["SD"]) > 0):
-        if d in (C40, C2032, C2304, B128, NI, H100, K1, K2, I256, NI256)[:P["CS"]]:
+        if d in (C2304, B128, NI, H100, K1, K2, I256, NI256)[:P["CS"]]:
             act(cb(d), cb(s), scale=c)
         else:
             ts(cb(d), cb(s), c, A.mult)
     for d, s, c in ((FI, ID, 1.0), (FBO, BO, 1.0 / 64), (FSI, BSI, 1.0), (FDI, BDI, 1.0), (FMX, E1, 4.0)):
         act(cf(d), cb(s), scale=c)
-    tt(cb(TN), cb(E0), cb(SUP), A.subtract)
-    act(cf(FXS), cb(TN), scale=2.0)
-    ts(cb(SUPT), cb(BSI), 524288.0, A.mult)
+    mm([(ps(2, 0, 128), cb(ID), cb(E0)), (ps(2, 0, 128), cb(NI), cb(SUP))])
+    act(cf(FXS), ps(2, 0, 128), scale=2.0)
+    ts(cb(SUPT), cb(BSI), 1048576.0, A.mult)
     for i in range(1, 2):
         ts(v("CB", 128 * SUPT, 128 * SUPT + 128, 16), v("CB", 128 * ID, 128 * ID + 128, 16), 33.0, A.mult)
     ts(cb(E1), cb(E1), -64.0, A.mult)
@@ -287,15 +290,15 @@ def build(g, core, T, topo):
     ms(v("ONES"), 1.0)
     ms(v("CN", 0, 64), 128.0 - 128 * 192)
     ms(v("CN", 64, 128), -128.0 - 128 * 192)
-    cp(v("KT"), v("tB", 0, 128))
     ts(v("RST"), v("tB", 0, 128), 0.0, A.is_equal, 4194304.0, A.mult)
     ts(v("OD"), v("tB"), col(K), A.not_equal, -4194304.0, A.mult)
     ts(v("RS"), v("tB"), 0.0, A.is_equal, -8388608.0, A.mult)
     ts(v("ODq", 0, 128), v("OD", 0, 128), -3264.0, A.add)
     ts(v("ODq", 128, 256), v("OD", 0, 128), -12480.0, A.add)
-    act(v("tA"), v("tA"), scale=col(M2))
-    act(v("tB"), v("tB"), scale=col(M3))
-    tt(v("TABq"), v("tA"), v("tB"), A.add)
+    ts(cb(D2), cb(ID), col(M2), A.mult)
+    ts(cb(D3), cb(ID), col(M3), A.mult)
+    mm([(ps(1), cb(D2), v("tA")), (ps(1), cb(D3), v("tB"))])
+    act(v("TABq"), ps(1), scale=256.0)
     ms(v("RS3"), 0.0)
     ts(v("RS3", 0, 48, 3), v("ONES", 0, 16), -4096.0, A.mult)
     ms(v("DW3"), 0.0)
@@ -309,10 +312,10 @@ def build(g, core, T, topo):
     ms(v("pm"), 1.0 / 3)
     ms(v("Aq"), 0.0)
     scan(v("thr"), v("pm"), v("Aq"), A.mult, A.add, 3.5 * 3.0 ** 53)
-    ts(v("pm"), v("OD", 0, 128), 0.0, A.is_equal, 1 / 3.5, A.mult)
-    tt(v("pm"), v("pm"), v("thr"), A.mult)
-    ts(v("Aq"), v("RST"), 0.0, A.is_equal)
-    scan(v("wc"), v("Aq"), v("pm"), A.mult, A.add)
+    tt(v("pm", 0, 16), v("col", 32, 48), v("thr", 0, 16), A.mult)
+    scan(v("pm", 16, 32), v("ONES", 0, 16), v("pm", 0, 16), A.mult, A.add)
+    ts(v("pm", 32, 33), v("pm", 31, 32), 3.0 ** -52 / 3.5 ** 2, A.mult)
+    ts(v("wc"), v("thr", 0, 128, 16), v("pm", 32, 33), A.mult)
     ts(v("DUM", 0, 8), v("ordc"), 257.0, A.add)
     ts(v("DUM", 8, 16), v("ordc"), 385.0, A.add)
     ts(v("DUM", 16, 24), v("ordc"), 4097.0, A.add)
@@ -322,20 +325,17 @@ def build(g, core, T, topo):
     iota(v("x", 256, 264), [[0, 8]], 0, 0)
     iota(v("STv", 256, 272), [[0, 16]], 0, 0)
     iota(v("inv", 4096, 4097), [[0, 1]], 16384, 0)
-    awz = iota(v("AW"), [[0, 768]], 0, 0)
+    for lo, hi in ((0, LO), (LO + 64, HI), (HI + 64, 768)):
+        iota(v("AW", lo, hi), [[0, hi - lo]], 0, 0)
     first = act(v("SW0", LO, LO + 64), v("ONES", 0, 64), AF.Silu, scale=col(DLO), more=1300)
-    for t in range(RO):
-        if t:
-            act(v("SW%d" % t, LO, LO + 64), v("ONES", 0, 64), scale=col(DLO))
-        act(v("SW%d" % t, HI, HI + 64), v("ONES", 0, 64), scale=col(DHI))
+    act(v("SW0", HI, HI + 64), v("ONES", 0, 64), scale=col(DHI))
     for c, e in enumerate(P["INV"]):
-        o = ind(v("inv"), v("offI", 16 * c, 16 * c + 16))
-        if e == "S" or c == 0:
-            iota(v("cval", 256 * c, 256 * c + 256), [[64, 16], [0, 16]], 1024 * c, 0)
+        o = ind(v("inv"), v("offI", 32 * c, 32 * c + 32))
         if e == "S":
-            ops[act(o, v("cval", 256 * c, 256 * c + 256), AF.Silu)]["deps"][first] = False
+            iota(v("cval", 512 * c, 512 * c + 512), [[64, 32], [0, 16]], 2048 * c, 0)
+            ops[act(o, v("cval", 512 * c, 512 * c + 512), AF.Silu)]["deps"][first] = False
         else:
-            ts(o, v("cval", 0, 256), 1.0, A.mult, float(1024 * c), A.add)
+            ts(o, v("cval", 0, 512), 1.0, A.mult, float(2048 * c), A.add)
 
     fixed.update(("CB", "CF", "ZB", "col", "ONES", "G8"))
     e1 = topo.engines(core, nxt)
@@ -354,13 +354,18 @@ def build(g, core, T, topo):
             ts(s("Yi"), s("Y"), float(128 * 77 * t), A.add)
             ts(s("xt"), s("Yi"), 7, A.logical_shift_right, 4095, A.bitwise_and)
             ts(s("w"), s("Yi"), 127, A.bitwise_and)
-            tt(s("P1"), s("xt"), s("w"), A.mult)
+            ts(s("wB"), s("w"), 127.0, A.add)
+            if lo >= P["PW"]:
+                mm([(ps(2, lo, hi), cb(ID), s("wB")), (ps(2, lo, hi), cb(N127), v("ONES", lo, hi))])
+                tt(s("P1"), ps(2, lo, hi), s("xt"), A.mult)
+            else:
+                tt(s("P1"), s("xt"), s("w"), A.mult)
             ts(s("P1"), s("P1"), 3, A.logical_shift_right, 4095, A.bitwise_and)
             return cp(s("iF"), s("P1"))
 
         def eindex(n, x, wb, shift, o1, o2, pf, pi, lst):
-            mm([(o1, cb(shift), wb), (o1, cb(C40), v("ONES", 0, n))])
-            mm([(o2, cb(K1), wb), (o2, cb(K2), wb), (o2, cb(C2032), v("ONES", 0, n))])
+            mm([(o1, cb(shift), wb)])
+            mm([(o2, cb(K1), wb), (o2, cb(K2), wb)])
             tt(pf, x, o1, A.mult)
             tt(pi, pf, o2, A.add)
             ts(pi, pi, 5, A.logical_shift_right, 4095, A.bitwise_and)
@@ -368,9 +373,12 @@ def build(g, core, T, topo):
         pick = lambda onv, o, gi: cp(o, gi) if onv else act(o, gi)
         ix = [index1(lo, hi) for lo, hi in P["IX"]]
         gf = [pick(a in P["VF"][t], v("Fb", 16 + 16 * a, 16 + 16 * b), ind(v("spr_s"), v("iF", a, b))) for a, b in P["GF"]]
-        ts(v("vB"), Y, 524288.0, A.is_lt)
-        mm([(ps(5), cb(T64), v("vB"))])
-        mm([(ps(5, 256, 512), cb(T64P), v("vB"))])
+        def taken():
+            ts(v("vB"), Y, 524288.0, A.is_lt)
+            mm([(ps(5), cb(T64), v("vB"))])
+            mm([(ps(5, 256, 512), cb(T64P), v("vB"))])
+        if t == 0 or P["rl"] < 2:
+            taken()
         for i, b in enumerate((6, 4)):
             tt(v("A1", 256 * i, 256 * i + 256), ps(5, 256 * i, 256 * i + 256), Y, A.mult)
             mm([(ps(b), cb(ID), v("OD")), (ps(b), cf(FBO), v("A1", 256 * i, 256 * i + 256))])
@@ -385,13 +393,11 @@ def build(g, core, T, topo):
         tt(v("tP"), v("txt"), v("tw"), A.mult)
         ts(v("tP"), v("tP"), 3, A.logical_shift_right, 4095, A.bitwise_and)
         cp(v("lF"), v("tP"))
-        for i in range(2):
-            j = pick(P["FTV"] and i, v("FT", 256 * i, 256 * i + 256), ind(v("spr_s"), v("lF", 16 * i, 16 * i + 16)))
-            if t and i == 0 and P["o2"] >= 0:
-                ops[j]["deps"][gf[P["o2"]]] = False
+        for lo, hi in P["FT"]:
+            act(v("FT", 16 * lo, 16 * hi), ind(v("spr_s"), v("lF", lo, hi)))
         ts(v("tX"), tw, 1.0 / 128, A.mult, -0.496, A.add)
         ts(v("tE", 0, 16), v("tw", 16, 32), 127.0, A.add)
-        ts(v("tE", 16, 32), v("tw", 0, 16), 25952.0, A.mult, -25952.0, A.add)
+        ts(v("tE", 16, 32), v("tw", 0, 16), 25952.0, A.mult, 25952.0 * 127, A.add)
         tt(v("tE", 0, 16), v("tE", 0, 16), v("tX"), A.mult)
         tt(v("tP2"), v("tE", 0, 16), v("tE", 16, 32), A.add)
         ts(v("tP2"), v("tP2"), 6, A.logical_shift_right, 4095, A.bitwise_and)
@@ -399,22 +405,21 @@ def build(g, core, T, topo):
         pick(P["ETV"], v("ET"), ind(v("bar_s"), v("lE")))
         fT = v("FT", 0, 256)
         for i, b in enumerate((4, 0)):
-            mm([(ps(b), cb(NI), fT), (ps(b), cb(ID), v("FT", 256, 512))], True, False)
-            mm([(ps(b), cb((ID, NI)[i]), v("ET"))], False, True)
-            if i < P["UTV"]:
-                ts(v("UT", 256 * i, 256 * i + 256), ps(b), float(i), A.is_ge, 0.5, A.subtract)
+            o = v("UT", 256 * i, 256 * i + 256)
+            if P["UTV"] >> i & 1:
+                mm([(ps(b), cb((ID, NI)[i]), fT), (ps(b), cb((NI, ID)[i]), v("FT", 256, 512))])
+                tt(o, ps(b), v("ET"), (A.is_le, A.is_gt)[i])
             else:
-                act(v("UT", 256 * i, 256 * i + 256), ps(b), AF.Sign, bias=0.5 - i)
+                mm([(ps(b), cb(NI), fT), (ps(b), cb(ID), v("FT", 256, 512))], True, False)
+                mm([(ps(b), cb((ID, NI)[i]), v("ET"))], False, True)
+                act(o, ps(b), AF.Sign, bias=0.5 - i)
         ts(v("cc", 0, 16), tw, 262144.0, A.is_ge, 64.0, A.mult)
         ts(v("cc", 16, 32), tw, 262144.0, A.is_lt, 64.0, A.mult)
         for e in range(2):
             tt(v("W2", e, 32, 2), v("tw", 0, 16), v("cc", 16 * e, 16 * e + 16), A.add)
-        if P["UTV"]:
-            ts(v("TH", 0, 32), v("W2"), 15.485, A.max, 15.5, A.subtract)
-        else:
-            ts(v("TH", 0, 32), v("W2"), 15.47, A.max, 15.5, A.subtract)
+        ts(v("TH", 0, 32), v("W2"), *((15.234, A.max, 15.0) if P["UTV"] & 1 else (15.47, A.max, 15.5)), A.subtract)
         act(v("ab"), v("W2"), AF.Abs, bias=-24.0)
-        ts(v("TH", 32, 64), v("ab"), 7.515 if P["UTV"] > 1 else 7.53, A.max, 7.5, A.subtract)
+        ts(v("TH", 32, 64), v("ab"), *((7.266, A.max, 7.0) if P["UTV"] & 2 else (7.53, A.max, 7.5)), A.subtract)
         mm([(ps(6, 320, 352), zb(Z16, c), v("UT", c, 512, 16)) for c in range(16)])
         for e in range(2):
             tt(v("FL", 32 * e, 32 * e + 32), ps(6, 320, 352), v("TH", e, 64, 2), A.is_gt)
@@ -435,25 +440,23 @@ def build(g, core, T, topo):
         tt(v("uP"), v("uI", 0, 16), v("uI", 16, 32), A.mult)
         ts(v("uP"), v("uP"), 5, A.logical_shift_right, 255, A.bitwise_and)
         cp(v("qS"), v("uP"))
-        mm([(ps(7), cb(ID), fT)], False, False)
-        act(v("qrow"), ind(v("TABq"), v("qS")))
-        mm([(ps(7), cb(I256), v("qrow"))], False, True)
+        mm([(ps(7), cb(ID), fT)], False, True)
         act(v("pack"), ps(7), bias=col(BPK))
+        act(v("qrow"), ind(v("TABq"), v("qS")))
         sw, lb, gb = "SW%d" % t, "LB%d" % t, "GB%d" % t
-        cp(ind(v(sw), v("offW")), v("pack"))
+        tt(ind(v(sw), v("offW")), v("pack"), v("qrow"), A.add)
 
         def send(sw=sw, lb=lb):
             return g.remote_dma_fused([
                 RemoteDMATransfer(dst_ids=[did(nxt)], dma_engine_mask=mk1, remote_sem=T.sem.m0, src=T[sw][:, LO:LO + 64], dst=T[lb][:, 0:64]),
                 RemoteDMATransfer(dst_ids=[did(prv)], dma_engine_mask=mk2, remote_sem=T.sem.m1, src=T[sw][:, HI:HI + 64], dst=T[lb][:, 64:128])],
                 local_sem=T.sem.ls)
-        sn = add("G", send, [v(sw)], [], 300, sig="none", extra=[awz])
-        add("N", None, [], [v(lb, 0, 64)], 0, sig=("m0", h * (t + 1)), lat=P["net"], extra=[sn])
-        add("N", None, [], [v(lb, 64, 128)], 0, sig=("m1", (len(e2) - h) * (t + 1)), lat=P["net"], extra=[sn])
+        sn = add("G", send, [v(sw)], [], 300, sig="none")
+        add("N", None, [], [v(lb, 0, 64)], 0, sig=("m0", h * (t + 1)), lat=P["net"] + P["first"] * (t == 0), extra=[sn])
+        add("N", None, [], [v(lb, 64, 128)], 0, sig=("m1", (len(e2) - h) * (t + 1)), lat=P["net"] + P["first"] * (t == 0), extra=[sn])
         tt(v("STv", 0, 256), ind(v("SENT"), v("offW")), v("vB"), A.mult)
         for lo, hi in P["IE"]:
             s = lambda nm: v(nm, lo, hi)
-            ts(s("wB"), s("w"), 47.0, A.add)
             eindex(hi - lo, s("x"), s("wB"), SUPH, ps(3, lo, hi), ps(3, 256 + lo, 256 + hi), s("P2f"), s("P2"), s("iE"))
         dm = ps(0)
         done = 0
@@ -499,7 +502,7 @@ def build(g, core, T, topo):
             mm([(o, cb(ID), v("wB", lo, hi)), (o, cb(W16), v("su", 2 * lo, 2 * lo + wd)), (o, cb(W16N), v("su", 2 * lo + wd, 2 * hi))])
             if hi in P["YQ"]:
                 o = ps(3, 256 + done, 256 + hi)
-                ts(v("w1B", done, hi), ps(3, done, hi), 48.0, A.max, 174.0, A.min)
+                ts(v("w1B", done, hi), ps(3, done, hi), 128.0, A.max, 254.0, A.min)
                 if P["YV"]:
                     mm([(o, cb(NI), v("wB", done, hi)), (o, cb(ID), v("w1B", done, hi))])
                     tt(v("Y", done, hi), o, v("Y", done, hi), A.add)
@@ -534,7 +537,7 @@ def build(g, core, T, topo):
             lo = 16 * u
             b = 256 * (8 * j + u)
             i = 128 * j + 16 * u + 15
-            ts(v("OH", b, b + 2 * (128 - lo)), v("R", 2 * lo, 256), v("Wf", i, i + 1), A.is_equal, v("wc", 16 * u + 15, 16 * u + 16), A.mult)
+            ts(v("OH", b, b + 2 * (128 - lo)), v("R", 2 * lo, 256), v("Wf", i, i + 1), A.is_equal, v("wc", u, u + 1), A.mult)
             mm([(ps(5, lo, 128), cb(BO), v("OH", b + i, b + 2 * (128 - lo), 2)) for i in range(2)], first, False)
         scan(v("Wf", 0, 128), v("RS", 0, 128), ps(6, 128, 256), A.add, A.max)
         for u in range(8):
@@ -556,15 +559,15 @@ def build(g, core, T, topo):
         add("N", None, [], [v("AW", LO, LO + 64)], 0, sig=("k1", (len(e2) - h) * (t + 1)), lat=P["net"], extra=[an])
         o = ps(4, 0, 128)
         mm([(o, cf(FI), L), (o, cb(NI256), v("metaB")), (o, cb(C2304), v("ONES", 0, 128))])
-        mm([(ps(7, 0, 128), cb(ID), v("KT")), (ps(7, 0, 128), v("SG", 128, 256), cb(NDG))], True, False)
-        mm([(ps(7, k, 128, 16), v("Fq", k, 2048, 16), v("G8", 8, 16)) for k in range(16)], False, False)
+        mm([(ps(7, 0, 128), cb(ID), v("tB", 0, 128)), (ps(7, 0, 128), v("SG", 128, 256), cb(NDG))], True, False)
+        mm([(ps(7, k, 128, 16), v("Fq", k, 2048, 16), v("G8", 8, 16)) for k in range(15)], False, False)
         for k in range(P["MH"]):
             tt(v("Mx", 128 * k, 128 * k + 64), v("Fq", k, 1024, 16), ps(4, 0, 64), A.max)
-        for k in range(16):
+        for k in range(15):
             lo = 64 if k < P["MH"] else 0
             tt(v("Mx", 128 * k + lo, 128 * k + 128), v("Fq", k + 16 * lo, 2048, 16), ps(4, lo, 128), A.max)
-            if k % 4 == 3:
-                mm([(ps(7, i, 128, 16), v("Mx", 128 * i, 128 * i + 128), v("G8", 16, 24)) for i in range(k - 3, k + 1)], False, k == 15)
+            if k % 3 == 2:
+                mm([(ps(7, i, 128, 16), v("Mx", 128 * i, 128 * i + 128), v("G8", 16, 24)) for i in range(k - 2, k + 1)], False, k == 14)
         mm([(ps(6, 256, 384), cb(RNB), v("metaB")), (ps(6, 256, 384), cb(BO), v("CN"))])
         act(v("nmS"), ps(6, 256, 384), bias=-12480.0)
         tt(v("eqB"), ind(v("x"), v("AQ", 0, 8)), v("nmS"), A.is_equal)
@@ -608,15 +611,24 @@ def build(g, core, T, topo):
             tt(v("Aq"), o, v("mQ"), A.mult)
         mm([(ps(7, 128, 256), cf(FSI), v("Aq"))])
         act(v("Yn"), ps(7, 128, 256))
-        act(v("tm2"), ind(v("AW"), v("offW")))
-        tt(dm, v("tm2"), dm, A.mult)
+        if P["TV"]:
+            act(v("dmS"), dm)
+            tt(v("tm2"), ind(v("AW"), v("offW")), v("dmS"), A.mult)
+            dm = v("tm2")
+        else:
+            act(v("tm2"), ind(v("AW"), v("offW")))
+            tt(dm, v("tm2"), dm, A.mult)
         tt(v("ta"), ps(5, 128, 256), v("mA"), A.mult)
         edits = [lambda: tt(ind(v("Y"), v("L3", 0, 8)), v("ta"), v("Yaq", 0, 128), A.add),
                  lambda: tt(ind(v("Y"), v("L3", 8, 16)), v("Yn"), v("Yaq", 128, 256), A.add)]
         edits.insert(P["rl"], lambda: tt(Y, Y, dm, A.add))
+        if P["rl"] == 2 and t < RO - 1:
+            edits.insert(2, taken)
         for f in edits:
             f()
         if t < RO - 1:
+            act(v("SW%d" % (t + 1), LO, LO + 64), v("ONES", 0, 64), scale=col(DLO))
+            act(v("SW%d" % (t + 1), HI, HI + 64), v("ONES", 0, 64), scale=col(DHI))
             act(v("qF"), v("R", 1, 256, 2), scale=64.0)
             if P["ivS"]:
                 ops[act(ind(v("inv", 0, 4232), v("L3", 16, 24)), v("qF"), AF.Silu)]["up"] = 1200.0
@@ -624,35 +636,37 @@ def build(g, core, T, topo):
                 cp(ind(v("inv", 0, 4232), v("L3", 16, 24)), v("qF"))
 
     now[0] = RO
-    ts(X, Y, 1.0 / 128, A.mult, 0.504, A.add)
-    ts(v("vB"), Y, 524288.0, A.is_lt)
-    tt(v("o1"), X, v("vB"), A.mult)
-    act(v("o2"), v("o1"), bias=-1.0)
+    for lo in (0, 128):
+        s = lambda nm: v(nm, lo, lo + 128)
+        ts(s("Yi"), s("Y"), 1048448.0, A.min, 128.0, A.add)
+        ts(s("xt"), s("Yi"), 7, A.logical_shift_right, 8191, A.bitwise_and)
+        ts(s("o2"), s("xt"), -1.0, A.add)
+        ts(s("w"), s("Yi"), 1, A.logical_shift_right, 63, A.bitwise_and)
+        cp(s("o3"), s("w"))
     dma("S", T.yl[:], T.o2[:], [v("o2")], [], "d6", 2200)
-    cp(v("Yi"), Y)
-    ts(v("Yi"), v("Yi"), 1, A.logical_shift_right, 63, A.bitwise_and)
-    tt(v("o3"), v("Yi"), v("vB"), A.mult)
     dma("Y", T.yz[:], T.o3[:], [v("o3")], [], "d7", 2200)
+    act(v("vB"), Y, AF.Sign, bias=524288.0, scale=-1.0)
     mm([(v("PS0", 0, 256, 1, 8), v("G8", 0, 8), v("vB"))])
-    act(v("o4", 0, 256, 1, 8), v("PS0", 0, 256, 1, 8))
+    act(v("o4", 0, 256, 1, 8), v("PS0", 0, 256, 1, 8), bias=8.0, scale=0.5)
     dma("S", T.yn[:], T.o4[0:8, :], [v("o4")], [], "d5", 2000)
     return ops, 2 * RO * len(e2)
 
 
 def schedule(ops):
-    order, total, seen = [], 0.0, {}
-    for t in range(RO):
+    total, seen, part, hint = 0.0, {}, {}, None
+    for t in (1, 2, 3, 0):
         idx = [i for i, o in enumerate(ops) if min(o["t"], RO - 1) == t]
         tags = tuple(ops[i]["tag"] for i in idx)
         if tags not in seen:
             sub = [dict(ops[i], deps={j - idx[0]: w for j, w in ops[i]["deps"].items() if j >= idx[0]}) for i in idx]
-            seen[tags] = arrange(sub)
-        order += [(idx[0] + i, total + s) for i, s in seen[tags][0]]
+            seen[tags] = arrange(sub, P["it"] // (1, 1, 1, 4)[t], hint)
+            hint = hint or {tags[i]: s for i, s in seen[tags][0]}
+        part[t] = [(idx[0] + i, s) for i, s in seen[tags][0]]
         total += seen[tags][1]
-    return order, total
+    return sum((part[t] for t in range(RO)), []), total
 
 
-def arrange(ops):
+def arrange(ops, its, hint=None):
     n = len(ops)
     cost = [o["cost"] for o in ops]
     eng = [o["eng"] for o in ops]
@@ -694,54 +708,85 @@ def arrange(ops):
     for f, gc, sc, pe, call, hop, net in P["cases"]:
         c = [(o["cost"] + P["cyc"] * (o["g"] * (gc - P["g"]) + o["sc"] * (sc - P["sc"]))) * f * (pe if o["eng"] == "P" else 1.0) + call * (o["eng"] in "VS")
              for o in ops]
-        e = [[(j, c[j] + ((d > cost[j]) and hop + ops[j]["lat"] * (net if ops[j]["lat"] > 100 else 1.0))) for j, d in pre[i]] for i in range(n)]
+        e = [[(j, c[j] + ((d > cost[j]) and hop + ops[j]["lat"] * (net if eng[j] == "N" else net ** 0.4 if ops[j]["sig"] else 1.0))) for j, d in pre[i]] for i in range(n)]
         cases.append((c, e, f))
 
-    def end(st):
-        order = sorted(range(n), key=lambda i: (st[i], i))
-        z = max(st[i] + cost[i] + lat[i] for i in range(n))
+    cases.insert(0, (cost, pre, 1.0))
+
+    def play(order):
+        z, runs = [], []
         for c, e, f in cases:
-            s2, free = [0.0] * n, dict.fromkeys(eng, 0.0)
+            s2, why, last, free = [0.0] * n, [-1] * n, {}, dict.fromkeys(eng, 0.0)
             for i in order:
-                s = free[eng[i]]
+                q = eng[i]
+                s = free[q]
+                y = -2 - last[q] if q in last else -1
                 for j, d in e[i]:
-                    if s2[j] + d > s:
-                        s = s2[j] + d
-                s2[i] = s
-                if eng[i] != "N":
-                    free[eng[i]] = s + c[i]
-            z += max(s2[i] + c[i] + lat[i] for i in range(n)) / f
-        return z / (1 + len(cases))
+                    if s2[j] + d >= s:
+                        s, y = s2[j] + d, j
+                s2[i], why[i] = s, y
+                if q != "N":
+                    free[q], last[q] = s + c[i], i
+            i = max(range(n), key=lambda i: s2[i] + c[i] + lat[i])
+            z.append((s2[i] + c[i] + lat[i]) / f)
+            runs.append((s2, why, i))
+        return (sum(z) + z[0]) / (len(z) + 1), order, runs, z
+    by = lambda st: sorted(range(n), key=lambda i: (st[i], i))
     key = [0.0] * n
     for i in range(n - 1, -1, -1):
         for j, d in pre[i]:
             key[j] = max(key[j], key[i] + d + 1e-3)
-    cur = place(sorted(range(n), key=lambda i: (-key[i], i)), pre, zero)
-    best, seed = cur, 12345
-    ec = eb = end(cur)
-    for it in range(P["it"]):
-        seed = (seed * 1103515245 + 12345) % 2147483648
-        if (seed >> 8) % 8 < P["jb"]:
-            back = place(sorted(range(n), key=lambda i: (-cur[i] - cost[i], -i)), post, lat)
+    best = cur = play(by(place(sorted(range(n), key=lambda i: (-key[i], i)), pre, zero)))
+    for t0 in range(0, 16000, 2000) if hint else ():
+        for i in range(n):
+            key[i] = max([t0 + hint[ops[i]["tag"]] if ops[i]["tag"] in hint else cur[2][0][0][i] * (t0 > 0)] + [key[j] for j, d in pre[i]])
+        best = min(best, play(by(key)), play(by(place(by(key), pre, zero))))
+    cur = best
+    seed = [P["seed"]]
+
+    def draw(m):
+        seed[0] = (seed[0] * 1103515245 + 12345) % 2147483648
+        return (seed[0] >> 8) % m
+    for it in range(its):
+        kind = draw(16)
+        st = cur[2][0][0]
+        if kind < P["jb"]:
+            back = place(sorted(range(n), key=lambda i: (-st[i] - cost[i], -i)), post, lat)
             key = [-back[i] - cost[i] for i in range(n)]
+        elif kind < P["pm"]:
+            key = list(st)
         else:
-            key = list(cur)
-        for _ in range(P["shake"]):
-            seed = (seed * 1103515245 + 12345) % 2147483648
-            i = (seed >> 8) % n
-            seed = (seed * 1103515245 + 12345) % 2147483648
-            key[i] -= (seed >> 8) % P["rnd"]
+            key = [0.0] * n
+            for k, i in enumerate(cur[1]):
+                key[i] = 50.0 * k
+        held, (_, why, i) = [], cur[2][draw(len(cases))]
+        while i != -1:
+            y = why[i]
+            if y < -1:
+                y = -2 - y
+                held.append((i, y))
+            i = y
+        i, y = held[draw(len(held))]
+        far = draw(P["rnd"]) * draw(2)
+        if draw(2):
+            key[i] = key[y] - 1 - far
+        else:
+            key[y] = key[i] + 1 + far
+            for a in range(y, n):
+                for j, d in post[a]:
+                    if key[j] < key[a]:
+                        key[j] = key[a]
         for i in range(n - 1, -1, -1):
             for j, d in pre[i]:
                 if key[i] < key[j]:
                     key[j] = key[i]
-        new = place(sorted(range(n), key=lambda i: (key[i], i)), pre, zero)
-        en = end(new)
-        if en <= ec + P["tol"] * (1.0 - it / P["it"]):
-            cur, ec = new, en
-            if en < eb:
-                best, eb = new, en
-    return [(i, best[i]) for i in sorted(range(n), key=lambda i: (best[i], i))], eb
+        new = play(by(place(by(key), pre, zero)) if kind < P["pm"] else by(key))
+        if new[0] <= cur[0] + P["tol"] * (1.0 - it / its):
+            cur = new
+            if new[0] < best[0]:
+                best = new
+    PLAN["ends"] = best[3]
+    return [(i, best[2][0][0][i]) for i in best[1]], best[0]
 
 
 def rank_program(g, core, T, topo):

import math
from concourse.bass import DstId, RemoteDMATransfer
from concourse.mybir import AluOpType as A, ActivationFunctionType as AF

RO = 4
LO, HI = 256, 512
MAGIC = 12582912.0
BF, F32, I32, U16 = "bfloat16", "float32", "int32", "uint16"
P = {"it": 18000, "rnd": 3000, "tol": 60.0, "pm": 2, "jb": 1, "seed": 12345, "INV": "SSSSSVVV", "cyc": 0.92, "pe": 0.49, "g": 1.56, "sc": 3.8, "hop": 90.0, "self": 90.0, "net": 2300.0,
     "CH": [(32 * c, 32 * c + 32) for c in range(8)], "YQ": (64, 128, 192, 256), "VF": ((), (), (), ()), "VE": ((), (), (), ()),
     "IX": ((0, 64), (64, 128), (128, 256)), "IE": ((0, 128), (128, 256)), "SD": (), "ND": (0, 1), "FT": ((0, 16), (16, 32)), "ETV": 0, "UTV": 1, "suS": 0, "RS": 1, "ivS": 1, "mTS": 4,
     "cut": 256, "VS": 1, "YV": 1, "DQ": 1, "MH": 15, "Y1": 0, "GF": [(64 * c, 64 * c + 64) for c in range(4)], "GE": [(32 * c, 32 * c + 32) for c in range(8)], "GQ": 64, "rl": 2,
     "o1": (-1, -1), "o2": -1, "SN": (), "CS": 4, "sfix": 90.0, "EV": "",
     "TV": 0, "PW": 256, "first": 2500.0,
     "cases": ((1.25, 1.8, 5.2, 1.1, 0.0, 60.0, 0.85), (0.93, 1.25, 2.6, 1.0, 0.0, 210.0, 1.7), (1.1, 1.95, 2.2, 0.95, 5.0, 120.0, 1.3),
               (1.0, 1.2, 5.2, 1.05, 0.0, 80.0, 2.3), (1.25, 1.1, 1.9, 1.12, 0.0, 50.0, 0.8))}

SB, POOL = {}, {}
for _d, _l in ((BF, "spr_s 4096 bar_s 4096 wt_s 2 Fb 4128 E 4096 nE 4096 UD 8192 STv 272 SENT 768 AW 768 OH 4096 Fq 2048 Mx 2048 CB 6144 ZB 1008 "
                    "TABq 256 GB0 128 GB1 128 GB2 128 GB3 128 FT 512 ET 256 UT 512 SG 256 G8 24 ONES 256 | wB 256 vB 256 hiB 256 su 512 w1B 256 "
                    "metaB 128 R 256 eqB 128 mT 128 CN 128 OD 256 ODq 256 tA 256 tB 256 RST 128 RS 256 mA 128 mQ 128 cc 32 FL 64 cs 36 DW3 48"),
               (F32, "Y 520 Yaq 256 ta 128 Yn 128 tm2 256 qF 128 pack 256 qrow 256 dmS 256 nmS 128 inv 8320 cval 4096 o2 256 o3 256 o4 256 CF 1152 col 48 "
                     "SW0 768 SW1 768 SW2 768 SW3 768 LB0 128 LB1 128 LB2 128 LB3 128 | P2f 256 xs 256 A1 512 Tw 512 W2 32 Wf 384 gw 128 Dif 24 L3f 24 "
                     "pm 128 Aq 128 Dq 128 o1 256 mg 128 jj 144 wtf 2 thr 128 ordc 8 wc 8 DUM 24 tE 32 ab 32 TH 64 "
                     "RS3 48 ow 48"),
               (I32, "lam_s 256 mon_s 256 x 264 | Yi 256 xt 256 w 256 P1 256 P2 256 uI 32 uP 16 Jt 256 pI 2 tY 32 txt 32 tw 32 tP 32 tX 16 tP2 16"),
               (U16, "iF 256 iE 256 lF 32 lE 16 qS 16 offW 16 lq 128 AQ 24 L3 24 offI 256 |")):
    _w, _p = _l.split("|")
    _w, _p, _o = _w.split(), _p.split(), 0
    for _i in range(0, len(_w), 2):
        SB[_w[_i]] = (int(_w[_i + 1]), _d)
    for _i in range(0, len(_p), 2):
        POOL[_p[_i]] = ("pool_" + _d, _o, int(_p[_i + 1]))
        _o += (int(_p[_i + 1]) + 15) // 16 * 16
    if _o:
        SB["pool_" + _d] = (_o, _d)
SCRATCH = {k: ("sbuf", [128, n], d) for k, (n, d) in SB.items()}
for _b in range(8):
    SCRATCH["PS%d" % _b] = ("psum", [128, 512], F32)
SEMAPHORES = ["cV", "cS", "cP", "cG", "ls", "m0", "m1", "k0", "k1", "d0", "d1", "d2", "d3", "d4", "d5", "d6", "d7", "d8"]
PLAN = {}


def build(g, core, T, topo):
    rank = T.rank_of(core)
    n = len(T.cores)
    nxt, prv = T.cores[(rank + 1) % n], T.cores[(rank - 1) % n]
    ops = []
    acc = {}
    fixed = set()
    now = [0]

    def v(name, lo=0, hi=None, st=1, p=128):
        nm = name
        if name in POOL:
            name, o, w = POOL[name]
            lo, hi = o + lo, o + (w if hi is None else hi)
        if hi is None:
            hi = SB[name][0]
        t = T[name]
        ap = t[0:p, lo:hi] if st == 1 else t[0:p, lo:hi:st]
        dtp = SB[name][1] if name in SB else F32
        return {"ap": ap, "r": [(name, lo, hi, lo % 2 if st % 2 == 0 else None)], "n": len(range(lo, hi, st)), "two": dtp in (BF, U16),
                "ps": name not in SB, "ind": False, "f32": dtp == F32, "nm": nm}

    def ind(win, off):
        return {"ap": win["ap"].indirect(off["ap"]), "r": win["r"], "o": off["r"], "n": 16 * off["n"], "two": win["two"], "ps": False, "ind": True,
                "nm": win["nm"]}

    def add(eng, fn, rd, wr, cost, sig=None, lat=0.0, extra=()):
        i = len(ops)
        deps = {}
        rr, ww = [], []
        for a in rd:
            rr += a["r"] + a.get("o", [])
        for a in wr:
            ww += a["r"]
            rr += a.get("o", [])
        for lst, isw in ((rr, False), (ww, True)):
            for (nm, lo, hi, pa) in lst:
                for (j, l2, h2, w2, e2, p2) in acc.get(nm, []):
                    ov = l2 < hi and lo < h2 and (pa is None or p2 is None or pa == p2)
                    if nm not in SB and e2 != eng:
                        deps[j] = True
                    elif nm not in SB and eng == "P":
                        deps[j] = deps.get(j, False)
                    elif ov and (w2 or isw):
                        deps[j] = deps.get(j, False) or e2 != eng or eng != "P"
        for j in extra:
            deps[j] = True
        for lst, isw in ((rr, False), (ww, True)):
            for (nm, lo, hi, pa) in lst:
                old = acc.get(nm, [])
                if isw and nm in SB and pa is None:
                    old = [e for e in old if not (lo <= e[1] and e[2] <= hi)]
                if isw or nm not in fixed:
                    acc[nm] = (old if nm in SB else old[-150:]) + [(i, lo, hi, isw, eng, pa)]
        ops.append({"eng": eng, "fn": fn, "deps": deps, "cost": cost, "sig": sig, "lat": lat, "up": 0.0, "t": now[0],
                    "g": sum(a["n"] for a in rd if a["ind"]), "sc": sum(a["n"] for a in wr if a["ind"]),
                    "tag": (eng == "N", tuple((r[0][:2] if r[0][:2] in ("SW", "LB", "GB") else r[0], r[1]) for r in ww + rr))})
        return i

    def vcost(out, ins, two=1.0):
        nn = max(a["n"] for a in ins + [out])
        if out["ind"]:
            return 50 + nn * P["sc"] * P["cyc"]
        if any(a["ind"] for a in ins):
            return 50 + nn * P["g"] * P["cyc"]
        if two == 1.0 and out["two"] and all(a["two"] for a in ins):
            two = 0.5
        return max(64, nn * two) * P["cyc"]

    def sc(s):
        return s["ap"] if isinstance(s, dict) else s

    def cols(*s):
        return [a for a in s if isinstance(a, dict)]

    def ts(out, in0, s1, op0, s2=None, op1=None):
        if op1 is None:
            fn = lambda: g.vector.tensor_scalar(out["ap"], in0["ap"], sc(s1), None, op0)
        else:
            fn = lambda: g.vector.tensor_scalar(out["ap"], in0["ap"], sc(s1), sc(s2), op0, op1)
        return add("V", fn, [in0] + cols(s1, s2), [out], vcost(out, [in0]))

    def tt(out, a, b, op):
        return add("V", lambda: g.vector.tensor_tensor(out["ap"], a["ap"], b["ap"], op), [a, b], [out],
                   vcost(out, [a, b], 1.01 if a["ps"] or b["ps"] else 2.0))

    def cp(out, a):
        return add("V", lambda: g.vector.tensor_copy(out["ap"], a["ap"]), [a], [out], vcost(out, [a]))

    def ms(out, c):
        return add("V", lambda: g.vector.memset(out["ap"], c), [], [out], vcost(out, []))

    def scan(out, d0, d1, op0, op1, ini=0.0):
        return add("V", lambda: g.vector.tensor_tensor_scan(out["ap"], d0["ap"], d1["ap"], sc(ini), op0, op1), [d0, d1] + cols(ini), [out],
                   vcost(out, [d0, d1]))

    def act(out, a, func=AF.Identity, bias=None, scale=None, more=0.0):
        if out["nm"] in P["EV"].split() and func == AF.Identity and not a["ind"]:
            return ts(out, a, 1.0 if scale is None else scale, A.mult, 0.0 if bias is None else bias, A.add)
        kw = {}
        if bias is not None:
            kw["bias"] = sc(bias)
        if scale is not None:
            kw["scale"] = sc(scale)
        c = (65 if out["ind"] or a["ind"] else P["sfix"]) + a["n"] * P["cyc"] * (P["sc"] if out["ind"] else P["g"] if a["ind"] else 1.0) + more
        return add("S", lambda: g.scalar.activation(out["ap"], a["ap"], func, **kw), [a] + cols(bias, scale), [out], c)

    def mm(items, first=True, last=True):
        c, k = 0, 0
        while k < len(items) - 1 and c < P["cut"]:
            c += max(min(64, items[k][1]["n"]), items[k][2]["n"]) * (4 if items[k][2]["f32"] else 1)
            k += 1
        if c >= P["cut"]:
            mm(items[:k], first, False)
            return mm(items[k:], False, last)

        def fn():
            r = None
            for i, (o, l, x) in enumerate(items):
                r = g.tensor.matmul(o["ap"], l["ap"], x["ap"], first and i == 0, last and i == len(items) - 1)
            return r
        c = sum(max(min(64, l["n"]), x["n"]) * (4 if x["f32"] else 1) for (o, l, x) in items) * P["pe"]
        return add("P", fn, [a for it in items for a in it[1:]], [it[0] for it in items], c, lat=60.0)

    def iota(out, pat, base, cm):
        if out["f32"] or out["two"]:
            fn = lambda: g.iota(out["ap"], pat, base, cm, allow_small_or_imprecise_dtypes=True)
        else:
            fn = lambda: g.iota(out["ap"], pat, base, cm)
        return add("G", fn, [], [out], 160 + 2 * out["n"] * P["cyc"])

    def sel(out, a, pat, op, fill, base, cm):
        return add("G", lambda: g.affine_select(out["ap"], a["ap"], pat, op, fill, base, cm), [a], [out], 200 + 2 * out["n"] * P["cyc"])

    def dma(q, out, in_, rd, wr, sem, lat):
        e = g.sync if q == "Y" else g.scalar
        return add(q, lambda: e.dma_start(out, in_).then_inc(T.sem[sem], 16), rd, wr, 60, sig=(sem, 16), lat=lat)

    col = lambda j: v("col", j, j + 1)
    cb = lambda j: v("CB", 128 * j, 128 * j + 128)
    cf = lambda j: v("CF", 128 * j, 128 * j + 128)
    zb = lambda j, k: v("ZB", 144 * j + 15 - k, 144 * j + 143 - k)
    ps = lambda b, lo=0, hi=256, st=1: v("PS%d" % b, lo, hi, st)

    d0 = dma("Y", T.lam_s[:], T.lam[:], [], [v("lam_s")], "d0", 2200)
    dma("S", T.mon_s[:], T.mon[:], [], [v("mon_s")], "d1", 2200)
    dma("S", T.wt_s[:], T.wt[:], [], [v("wt_s")], "d2", 2200)
    d3 = dma("Y", T.spr_s[:], T.spr[:], [], [v("spr_s")], "d3", 6500)
    d4 = dma("Y", T.bar_s[:, 0:2752], T.bar[:, 1344:4096], [], [v("bar_s", 0, 2752)], "d4", 9500)
    ops[dma("Y", T.bar_s[:, 2752:4096], T.bar[:, 0:1344], [], [v("bar_s", 2752, 4096)], "d8", 11000)]["deps"][d4] = False
    ops[d3]["deps"][d0] = False
    ops[d4]["deps"][d3] = False

    Y = v("Y", 0, 256)
    X = v("x", 0, 256)
    iota(v("Jt"), [[16, 256]], 4112, 1)
    ts(X, v("lam_s"), 16383, A.bitwise_and)
    tt(v("Jt"), v("Jt"), X, A.min)
    cp(v("offI"), v("Jt"))
    ts(v("o1"), v("mon_s"), 2.0, A.mult, 1.0, A.add)
    ts(v("o2"), X, 128.0, A.mult)
    tt(Y, v("o1"), v("o2"), A.add)

    iota(v("pI", 0, 1), [[0, 1]], 0, 1)
    iota(v("mg"), [[1, 8], [0, 16]], 0, 0)
    iota(v("jj"), [[1, 144]], 0, 0)
    iota(v("tA"), [[1, 16], [0, 16]], 0, 0)
    iota(v("tB"), [[0, 16], [1, 16]], 0, 0)
    K, GR, GE, N0, M1, G4, RN, RQ, BPK, DLO, DHI, QK, CA, CQ, CT = range(15)
    ts(v("pI", 1, 2), v("pI", 0, 1), 15, A.bitwise_and)
    cp(col(K), v("pI", 1, 2))
    ts(v("pI", 1, 2), v("pI", 0, 1), 4, A.logical_shift_right)
    cp(col(GR), v("pI", 1, 2))
    ts(col(GE), col(GR), 16.0, A.mult, 15.0, A.add)
    ts(col(QK), col(K), -16.0 * 3264, A.add)
    ts(v("col", 32, 48), v("jj", 0, 16), col(K), A.is_equal)
    M2, M3 = 34, 35
    ts(col(N0), col(K), 0.0, A.not_equal)
    ts(col(M1), col(K), 1.0, A.is_equal, 1048576.0, A.mult)
    ts(col(G4), col(K), 4.0, A.is_ge, -1048576.0, A.mult)

    def lin(dst, terms):
        ts(col(dst), col(K), float(terms[0][0]), A.is_equal, float(terms[0][1]), A.mult)
        for k, wgt in terms[1:]:
            ts(col(dst), col(32 + k), float(wgt), A.mult, col(dst), A.add)
    big = 2.0 ** 90
    lin(RN, [(0, 64), (1, 1), (4, 2048)])
    lin(RQ, [(2, 16), (3, 1)])
    lin(BPK, [(0, -40960), (1, 2621440)])
    lin(DLO, [(4, 256), (2, 256 * 16)])
    lin(DHI, [(4, 256 * 3), (2, 256 * 16)])
    lin(CA, [(0, big), (1, big), (4, -big)])
    lin(CQ, [(0, big), (15, big)])
    lin(CT, [(0, 128 * 12480), (1, -33)])
    cp(v("wtf"), v("wt_s"))
    (BO, ID, NI, H100, H107, SUPH, N127, K1, K2, C2032, T64, T64P, W16, W16N, MH, I256, SUPT, LT, RQB, RNB, RN128, B128, NI256, C2304,
     SUP, SDN, BSI, BDI, E0, E1, E15, FA, FQ, CTB, NDG, L1, L0, D2, D3, TN) = range(40)
    (FI, FBO, FMX, FSI, FXS, FDI) = range(6)
    dif, pl = [[1, 128]], [[0, 8], [1, 16]]
    ts(cb(BO), v("mg"), col(GR), A.is_equal)
    sel(cb(ID), cb(BO), dif, A.is_equal, 0.0, 0, -1)
    sel(cb(SUP), cb(BO), dif, A.is_equal, 0.0, -1, -1)
    sel(cb(SDN), cb(BO), dif, A.is_equal, 0.0, 1, -1)
    sel(cb(BSI), cb(SUP), dif, A.not_equal, -1.0, 0, -1)
    sel(cb(BDI), cb(SDN), dif, A.not_equal, -1.0, 0, -1)
    sel(cb(LT), cb(BO), dif, A.is_ge, 0.0, 0, -1)
    sel(cb(E0), cb(BO), pl, A.is_equal, 0.0, 0, 0)
    sel(cb(E1), cb(BO), pl, A.is_equal, 0.0, -1, 0)
    sel(cb(TN), cb(BO), dif, A.is_equal, 0.0, 2, -1)
    tt(cb(TN), cb(SDN), cb(TN), A.subtract)
    ts(cb(T64P), cb(TN), 64.0, A.mult)
    sel(cb(TN), cb(BO), pl, A.is_equal, 0.0, -15, 0)
    ts(cb(E15), cb(TN), 65536.0, A.mult)
    for d, s, c in ((N127, ID, -127.0),) * (P["PW"] < 256) + ((NI, ID, -1.0), (H100, ID, 100.0), (K1, ID, 12288.0), (K2, ID, 688.0), (I256, ID, 256.0),
                    (SUPH, SUP, 0.5), (T64, BDI, -64.0), (W16, BDI, -8.0 if P["suS"] else -16.0), (W16N, BDI, 8.0 if P["suS"] else 16.0), (NI256, ID, -256.0),
                    (C2304, BO, 3072.0), (RQB, BO, col(RQ)), (RNB, BO, col(RN)), (RN128, RNB, -128.0), (B128, BO, -128.0),
                    (FA, BO, col(CA)), (FQ, BO, col(CQ)), (CTB, BO, col(CT))) + ((H107, ID, 107.0),) * (len(P["SD"]) > 0):
        if d in (C2304, B128, NI, H100, K1, K2, I256, NI256)[:P["CS"]]:
            act(cb(d), cb(s), scale=c)
        else:
            ts(cb(d), cb(s), c, A.mult)
    for d, s, c in ((FI, ID, 1.0), (FBO, BO, 1.0 / 64), (FSI, BSI, 1.0), (FDI, BDI, 1.0), (FMX, E1, 4.0)):
        act(cf(d), cb(s), scale=c)
    mm([(ps(2, 0, 128), cb(ID), cb(E0)), (ps(2, 0, 128), cb(NI), cb(SUP))])
    act(cf(FXS), ps(2, 0, 128), scale=2.0)
    ts(cb(SUPT), cb(BSI), 1048576.0, A.mult)
    for i in range(1, 2):
        ts(v("CB", 128 * SUPT, 128 * SUPT + 128, 16), v("CB", 128 * ID, 128 * ID + 128, 16), 33.0, A.mult)
    ts(cb(E1), cb(E1), -64.0, A.mult)
    tt(cb(E1), cb(E1), cb(E0), A.add)
    ts(cb(MH), cb(E1), 256.0, A.mult)
    sel(cb(TN), cb(BO), pl, A.is_ge, 0.0, -4, 0)
    ts(cb(TN), cb(TN), col(M1), A.mult)
    ts(cb(NDG), cb(ID), col(G4), A.mult)
    tt(cb(NDG), cb(NDG), cb(TN), A.add)
    sel(cb(L1), cb(LT), dif, A.not_equal, 256.0, 0, -1)
    sel(cb(L0), cb(BO), [[-1, 128]], A.is_ge, 0.0, 0, 1)
    sel(cb(L0), cb(L0), dif, A.not_equal, -255.0, 0, -1)
    Z1, ZW1, ZW2, Z16 = range(4)
    zf = lambda j: v("ZB", 144 * j, 144 * j + 144)
    ts(zf(Z1), v("jj"), col(GE), A.is_equal)
    for j, s in ((ZW1, v("wtf", 0, 1)), (ZW2, v("wtf", 1, 2)), (Z16, 1.0 / 32)):
        ts(zf(j), zf(Z1), s, A.mult)
    ts(v("G8", 0, 8), v("jj", 0, 8), col(GR), A.is_equal)
    ts(v("G8", 8, 16), v("G8", 0, 8), -16.0, A.mult)
    ts(v("G8", 16, 24), v("G8", 0, 8), 32.0, A.mult)
    ms(v("ONES"), 1.0)
    ms(v("CN", 0, 64), 128.0 - 128 * 192)
    ms(v("CN", 64, 128), -128.0 - 128 * 192)
    ts(v("RST"), v("tB", 0, 128), 0.0, A.is_equal, 4194304.0, A.mult)
    ts(v("OD"), v("tB"), col(K), A.not_equal, -4194304.0, A.mult)
    ts(v("RS"), v("tB"), 0.0, A.is_equal, -8388608.0, A.mult)
    ts(v("ODq", 0, 128), v("OD", 0, 128), -3264.0, A.add)
    ts(v("ODq", 128, 256), v("OD", 0, 128), -12480.0, A.add)
    ts(cb(D2), cb(ID), col(M2), A.mult)
    ts(cb(D3), cb(ID), col(M3), A.mult)
    mm([(ps(1), cb(D2), v("tA")), (ps(1), cb(D3), v("tB"))])
    act(v("TABq"), ps(1), scale=256.0)
    ms(v("RS3"), 0.0)
    ts(v("RS3", 0, 48, 3), v("ONES", 0, 16), -4096.0, A.mult)
    ms(v("DW3"), 0.0)
    ts(v("DW3", 2, 48, 3), v("jj", 0, 16), 16.0, A.mult, col(K), A.add)
    ms(v("cs"), 0.0)
    for lo in (LO, HI):
        iota(v("SENT", lo, lo + 64), [[0, 64]], 1, 0)
    for lo, hi in ((0, LO), (LO + 64, HI), (HI + 64, 768)):
        ts(v("SENT", lo, hi), v("ONES", 0, hi - lo), col(N0), A.mult)
    ts(v("ordc"), v("jj", 0, 8), 16.0, A.mult, col(K), A.add)
    ms(v("pm"), 1.0 / 3)
    ms(v("Aq"), 0.0)
    scan(v("thr"), v("pm"), v("Aq"), A.mult, A.add, 3.5 * 3.0 ** 53)
    tt(v("pm", 0, 16), v("col", 32, 48), v("thr", 0, 16), A.mult)
    scan(v("pm", 16, 32), v("ONES", 0, 16), v("pm", 0, 16), A.mult, A.add)
    ts(v("pm", 32, 33), v("pm", 31, 32), 3.0 ** -52 / 3.5 ** 2, A.mult)
    ts(v("wc"), v("thr", 0, 128, 16), v("pm", 32, 33), A.mult)
    ts(v("DUM", 0, 8), v("ordc"), 257.0, A.add)
    ts(v("DUM", 8, 16), v("ordc"), 385.0, A.add)
    ts(v("DUM", 16, 24), v("ordc"), 4097.0, A.add)
    ms(v("Fb", 0, 16), 0.0)
    iota(v("Fb", 4112, 4128), [[0, 16]], 0, 0)
    iota(v("Y", 256, 264), [[0, 8]], 0, 0)
    iota(v("x", 256, 264), [[0, 8]], 0, 0)
    iota(v("STv", 256, 272), [[0, 16]], 0, 0)
    iota(v("inv", 4096, 4097), [[0, 1]], 16384, 0)
    for lo, hi in ((0, LO), (LO + 64, HI), (HI + 64, 768)):
        iota(v("AW", lo, hi), [[0, hi - lo]], 0, 0)
    first = act(v("SW0", LO, LO + 64), v("ONES", 0, 64), AF.Silu, scale=col(DLO), more=1300)
    act(v("SW0", HI, HI + 64), v("ONES", 0, 64), scale=col(DHI))
    for c, e in enumerate(P["INV"]):
        o = ind(v("inv"), v("offI", 32 * c, 32 * c + 32))
        if e == "S":
            iota(v("cval", 512 * c, 512 * c + 512), [[64, 32], [0, 16]], 2048 * c, 0)
            ops[act(o, v("cval", 512 * c, 512 * c + 512), AF.Silu)]["deps"][first] = False
        else:
            ts(o, v("cval", 0, 512), 1.0, A.mult, float(2048 * c), A.add)

    fixed.update(("CB", "CF", "ZB", "col", "ONES", "G8"))
    e1 = topo.engines(core, nxt)
    e2 = topo.engines(core, prv)
    h = len(e1) // 2
    mk1 = sum(1 << i for i in e1[:h])
    mk2 = sum(1 << i for i in e2[h:])
    did = lambda c: DstId(rid=topo.addr(c)[0], pnc=topo.addr(c)[1])
    Fw = v("Fb", 16, 4128)

    for t in range(RO):
        now[0] = t

        def index1(lo, hi):
            s = lambda nm: v(nm, lo, hi)
            ts(s("Yi"), s("Y"), float(128 * 77 * t), A.add)
            ts(s("xt"), s("Yi"), 7, A.logical_shift_right, 4095, A.bitwise_and)
            ts(s("w"), s("Yi"), 127, A.bitwise_and)
            ts(s("wB"), s("w"), 127.0, A.add)
            if lo >= P["PW"]:
                mm([(ps(2, lo, hi), cb(ID), s("wB")), (ps(2, lo, hi), cb(N127), v("ONES", lo, hi))])
                tt(s("P1"), ps(2, lo, hi), s("xt"), A.mult)
            else:
                tt(s("P1"), s("xt"), s("w"), A.mult)
            ts(s("P1"), s("P1"), 3, A.logical_shift_right, 4095, A.bitwise_and)
            return cp(s("iF"), s("P1"))

        def eindex(n, x, wb, shift, o1, o2, pf, pi, lst):
            mm([(o1, cb(shift), wb)])
            mm([(o2, cb(K1), wb), (o2, cb(K2), wb)])
            tt(pf, x, o1, A.mult)
            tt(pi, pf, o2, A.add)
            ts(pi, pi, 5, A.logical_shift_right, 4095, A.bitwise_and)
            cp(lst, pi)
        pick = lambda onv, o, gi: cp(o, gi) if onv else act(o, gi)
        ix = [index1(lo, hi) for lo, hi in P["IX"]]
        gf = [pick(a in P["VF"][t], v("Fb", 16 + 16 * a, 16 + 16 * b), ind(v("spr_s"), v("iF", a, b))) for a, b in P["GF"]]
        def taken():
            ts(v("vB"), Y, 524288.0, A.is_lt)
            mm([(ps(5), cb(T64), v("vB"))])
            mm([(ps(5, 256, 512), cb(T64P), v("vB"))])
        if t == 0 or P["rl"] < 2:
            taken()
        for i, b in enumerate((6, 4)):
            tt(v("A1", 256 * i, 256 * i + 256), ps(5, 256 * i, 256 * i + 256), Y, A.mult)
            mm([(ps(b), cb(ID), v("OD")), (ps(b), cf(FBO), v("A1", 256 * i, 256 * i + 256))])
            j = scan(v("Tw", 256 * i, 256 * i + 256), v("RS"), ps(b), A.add, A.max)
            if t and P["o1"][i] >= 0:
                ops[j]["deps"][ix[P["o1"][i]]] = False
        act(v("hiB"), ps(6), AF.Relu, bias=159.5, scale=1.0 / 8192)
        tw = v("Tw", 15, 256, 16)
        ts(v("tY"), v("Tw", 15, 512, 16), float(128 * 77 * t), A.add)
        ts(v("txt"), v("tY"), 7, A.logical_shift_right, 4095, A.bitwise_and)
        ts(v("tw"), v("tY"), 127, A.bitwise_and)
        tt(v("tP"), v("txt"), v("tw"), A.mult)
        ts(v("tP"), v("tP"), 3, A.logical_shift_right, 4095, A.bitwise_and)
        cp(v("lF"), v("tP"))
        for lo, hi in P["FT"]:
            act(v("FT", 16 * lo, 16 * hi), ind(v("spr_s"), v("lF", lo, hi)))
        ts(v("tX"), tw, 1.0 / 128, A.mult, -0.496, A.add)
        ts(v("tE", 0, 16), v("tw", 16, 32), 127.0, A.add)
        ts(v("tE", 16, 32), v("tw", 0, 16), 25952.0, A.mult, 25952.0 * 127, A.add)
        tt(v("tE", 0, 16), v("tE", 0, 16), v("tX"), A.mult)
        tt(v("tP2"), v("tE", 0, 16), v("tE", 16, 32), A.add)
        ts(v("tP2"), v("tP2"), 6, A.logical_shift_right, 4095, A.bitwise_and)
        cp(v("lE"), v("tP2"))
        pick(P["ETV"], v("ET"), ind(v("bar_s"), v("lE")))
        fT = v("FT", 0, 256)
        for i, b in enumerate((4, 0)):
            o = v("UT", 256 * i, 256 * i + 256)
            if P["UTV"] >> i & 1:
                mm([(ps(b), cb((ID, NI)[i]), fT), (ps(b), cb((NI, ID)[i]), v("FT", 256, 512))])
                tt(o, ps(b), v("ET"), (A.is_le, A.is_gt)[i])
            else:
                mm([(ps(b), cb(NI), fT), (ps(b), cb(ID), v("FT", 256, 512))], True, False)
                mm([(ps(b), cb((ID, NI)[i]), v("ET"))], False, True)
                act(o, ps(b), AF.Sign, bias=0.5 - i)
        ts(v("cc", 0, 16), tw, 262144.0, A.is_ge, 64.0, A.mult)
        ts(v("cc", 16, 32), tw, 262144.0, A.is_lt, 64.0, A.mult)
        for e in range(2):
            tt(v("W2", e, 32, 2), v("tw", 0, 16), v("cc", 16 * e, 16 * e + 16), A.add)
        ts(v("TH", 0, 32), v("W2"), *((15.234, A.max, 15.0) if P["UTV"] & 1 else (15.47, A.max, 15.5)), A.subtract)
        act(v("ab"), v("W2"), AF.Abs, bias=-24.0)
        ts(v("TH", 32, 64), v("ab"), *((7.266, A.max, 7.0) if P["UTV"] & 2 else (7.53, A.max, 7.5)), A.subtract)
        mm([(ps(6, 320, 352), zb(Z16, c), v("UT", c, 512, 16)) for c in range(16)])
        for e in range(2):
            tt(v("FL", 32 * e, 32 * e + 32), ps(6, 320, 352), v("TH", e, 64, 2), A.is_gt)
            scan(v("cs", 18 * e + 1, 18 * e + 17), v("FL", 32 * e, 32 * e + 16), v("FL", 32 * e + 16, 32 * e + 32), A.add, A.add)
        mm([(ps(6, 384, 432), cb(ID), v("DW3"))] +
           [(ps(6, 384 + e, 432, 3), cb(m), v("cs", 18 * e + s, 18 * e + 16 + s)) for e in range(2) for m, s in ((L1, 1), (L0, 0))] +
           [(ps(6, 385, 432, 3), cb(I256), v("FL", b, b + 16)) for b in (32, 48)])
        scan(v("ow"), v("RS3"), ps(6, 384, 432), A.add, A.max)
        cp(v("offW"), v("ow", 2, 48, 3))
        if t:
            ts(X, Y, 1.0 / 128, A.mult, -0.496, A.add)
        tt(v("xs"), ps(5), X, A.mult)
        mm([(ps(7), cf(FMX), v("xs")), (ps(7), cb(MH), v("hiB"))], True, False)
        mm([(ps(5, 0, 16), zb(ZW1, c), v("FT", c, 256, 16)) for c in range(16)])
        mm([(ps(5, 16, 32), zb(ZW2, c), v("FT", c, 256, 16)) for c in range(16)])
        cp(v("uI"), ps(5, 0, 32))
        ts(v("uI"), v("uI"), 4095, A.bitwise_and)
        tt(v("uP"), v("uI", 0, 16), v("uI", 16, 32), A.mult)
        ts(v("uP"), v("uP"), 5, A.logical_shift_right, 255, A.bitwise_and)
        cp(v("qS"), v("uP"))
        mm([(ps(7), cb(ID), fT)], False, True)
        act(v("pack"), ps(7), bias=col(BPK))
        act(v("qrow"), ind(v("TABq"), v("qS")))
        sw, lb, gb = "SW%d" % t, "LB%d" % t, "GB%d" % t
        tt(ind(v(sw), v("offW")), v("pack"), v("qrow"), A.add)

        def send(sw=sw, lb=lb):
            return g.remote_dma_fused([
                RemoteDMATransfer(dst_ids=[did(nxt)], dma_engine_mask=mk1, remote_sem=T.sem.m0, src=T[sw][:, LO:LO + 64], dst=T[lb][:, 0:64]),
                RemoteDMATransfer(dst_ids=[did(prv)], dma_engine_mask=mk2, remote_sem=T.sem.m1, src=T[sw][:, HI:HI + 64], dst=T[lb][:, 64:128])],
                local_sem=T.sem.ls)
        sn = add("G", send, [v(sw)], [], 300, sig="none")
        add("N", None, [], [v(lb, 0, 64)], 0, sig=("m0", h * (t + 1)), lat=P["net"] + P["first"] * (t == 0), extra=[sn])
        add("N", None, [], [v(lb, 64, 128)], 0, sig=("m1", (len(e2) - h) * (t + 1)), lat=P["net"] + P["first"] * (t == 0), extra=[sn])
        tt(v("STv", 0, 256), ind(v("SENT"), v("offW")), v("vB"), A.mult)
        for lo, hi in P["IE"]:
            s = lambda nm: v(nm, lo, hi)
            eindex(hi - lo, s("x"), s("wB"), SUPH, ps(3, lo, hi), ps(3, 256 + lo, 256 + hi), s("P2f"), s("P2"), s("iE"))
        dm = ps(0)
        done = 0
        bank = 0
        for c, (lo, hi) in enumerate(P["CH"]):
            s = lambda nm: v(nm, 16 * lo, 16 * hi)
            wd = hi - lo
            for a, b in P["GE"]:
                if a == lo:
                    pick(a in P["VE"][t], v("E", 16 * a, 16 * b), ind(v("bar_s"), v("iE", a, b)))
            f1, f0 = v("Fb", 16 + 16 * lo, 16 + 16 * hi), v("Fb", 15 + 16 * lo, 15 + 16 * hi)
            d = ps(bank, 0, 16 * wd)
            bank = 1 - bank
            mm([(d, cb(ID), f1), (d, cb(NI), f0)])
            w = 16 * wd // P["VS"]
            for i in range(0, 16 * wd, w):
                tt(v("UD", 32 * lo + i, 32 * lo + i + w), ps(1 - bank, i, i + w), v("E", 16 * lo + i, 16 * lo + i + w), A.is_gt)
            if c in P["SD"]:
                d = ps(bank, 0, 16 * wd)
                bank = 1 - bank
                mm([(d, cb(NI), f1), (d, cb(ID), f0), (d, cb(NI), s("E"))])
                act(v("UD", 32 * lo + 16 * wd, 32 * hi), d, AF.Sign, bias=-0.5)
            elif c in P["ND"]:
                d = ps(bank, 0, 16 * wd)
                bank = 1 - bank
                mm([(d, cb(NI), f1), (d, cb(ID), f0)])
                tt(v("UD", 32 * lo + 16 * wd, 32 * hi), d, s("E"), A.is_gt)
            else:
                if c in P["SN"]:
                    act(s("nE"), s("E"), scale=-1.0)
                else:
                    ts(s("nE"), s("E"), -1.0, A.mult)
                for i in range(0, 16 * wd, w):
                    tt(v("UD", 16 * (lo + hi) + i, 16 * (lo + hi) + i + w), ps(1 - bank, i, i + w), v("nE", 16 * lo + i, 16 * lo + i + w), A.is_lt)
            o = ps(2, 0, 2 * wd)
            mm([(o, zb(Z1, k), v("UD", 32 * lo + k, 32 * hi, 16)) for k in range(1, 16)] +
               [(ps(2, i * wd, i * wd + wd), cb(H107 if i and c in P["SD"] else H100), v("vB", lo, hi)) for i in range(2)])
            if P["suS"]:
                act(v("su", 2 * lo, 2 * hi), o, AF.Sign, bias=-108.5)
            else:
                ts(v("su", 2 * lo, 2 * hi), o, 108.5, A.is_ge, 0.5, A.subtract)
            o = ps(3, lo, hi)
            mm([(o, cb(ID), v("wB", lo, hi)), (o, cb(W16), v("su", 2 * lo, 2 * lo + wd)), (o, cb(W16N), v("su", 2 * lo + wd, 2 * hi))])
            if hi in P["YQ"]:
                o = ps(3, 256 + done, 256 + hi)
                ts(v("w1B", done, hi), ps(3, done, hi), 128.0, A.max, 254.0, A.min)
                if P["YV"]:
                    mm([(o, cb(NI), v("wB", done, hi)), (o, cb(ID), v("w1B", done, hi))])
                    tt(v("Y", done, hi), o, v("Y", done, hi), A.add)
                else:
                    mm([(o, cf(FI), v("Y", done, hi)), (o, cb(NI), v("wB", done, hi)), (o, cb(ID), v("w1B", done, hi))])
                    act(v("Y", done, hi), o)
                done = hi
        dm = ps(bank)
        mm([(dm, cf(FXS), v("xs")), (dm, cb(SUPT), v("vB"))], True, False)
        for lo, hi in zip((0,) + P["YQ"], P["YQ"]):
            mm([(ps(bank, lo, hi), cf(FSI), v("Y", lo, hi))], False, hi == 256)
        L = v(lb)
        ts(v("metaB"), L, 1.0 / 256, A.mult, 191.502, A.add)
        o = ps(7, 256, 384)
        mm([(ps(7, 256, 512), cb(ID), v("ODq")), (o, cb(RQB), v("metaB")), (ps(7, 384, 512), cb(RNB), v("metaB")), (ps(7, 384, 512), cb(BO), v("CN"))])
        scan(v("Wf", 128, 384), v("RS"), ps(7, 256, 512), A.add, A.max)
        cp(v("AQ", 8, 24), v("Wf", 143, 384, 16))
        if P["RS"]:
            act(v("R", 0, 256, 2), ind(v("inv", 0, 4104), v("AQ", 16, 24)), scale=1.0 / 64)
        else:
            ts(v("R", 0, 256, 2), ind(v("inv", 0, 4104), v("AQ", 16, 24)), 1.0 / 64, A.mult)
        mm([(ps(6, 0, 128), cb(RQB), v("metaB"))])
        mm([(ps(5, 0, 128), cb(RQB), v("metaB"))])
        ts(v("lq"), ps(6, 0, 128), 16.0, A.mult, col(QK), A.add)
        act(v("R", 1, 256, 2), ps(5, 0, 128), bias=-3264.0)
        for i in range(0, 128, P["GQ"]):
            act(v("Fq", 16 * i, 16 * (i + P["GQ"])), ind(Fw, v("lq", i, i + P["GQ"])))
        act(v("SG", 128, 256), ind(v("STv"), v("AQ", 8, 16)))
        mm([(ps(6, 128, 256), cb(ID), v("OD", 0, 128)), (ps(6, 128, 256), cb(ID), v("R", 0, 256, 2))])

        def clash(j, u, first):
            lo = 16 * u
            b = 256 * (8 * j + u)
            i = 128 * j + 16 * u + 15
            ts(v("OH", b, b + 2 * (128 - lo)), v("R", 2 * lo, 256), v("Wf", i, i + 1), A.is_equal, v("wc", u, u + 1), A.mult)
            mm([(ps(5, lo, 128), cb(BO), v("OH", b + i, b + 2 * (128 - lo), 2)) for i in range(2)], first, False)
        scan(v("Wf", 0, 128), v("RS", 0, 128), ps(6, 128, 256), A.add, A.max)
        for u in range(8):
            clash(1, u, u == 0)
        cp(v("AQ", 0, 8), v("Wf", 15, 128, 16))
        act(v("SG", 0, 128), ind(v("STv"), v("AQ", 0, 8)))
        for u in range(8):
            clash(0, u, False)
        mm([(ps(5, 0, 128), cb(FQ), v("SG", 128, 256)), (ps(5, 0, 128), cb(FA), v("SG", 0, 128))], False, True)
        tt(v(gb), ps(5, 0, 128), v("thr"), A.is_lt)

        def ack(gb=gb):
            return g.remote_dma_fused([
                RemoteDMATransfer(dst_ids=[did(nxt)], dma_engine_mask=mk1, remote_sem=T.sem.k0, src=T[gb][:, 64:128], dst=T.AW[:, HI:HI + 64]),
                RemoteDMATransfer(dst_ids=[did(prv)], dma_engine_mask=mk2, remote_sem=T.sem.k1, src=T[gb][:, 0:64], dst=T.AW[:, LO:LO + 64])],
                local_sem=T.sem.ls)
        an = add("G", ack, [v(gb)], [], 300, sig="none")
        add("N", None, [], [v("AW", HI, HI + 64)], 0, sig=("k0", h * (t + 1)), lat=P["net"], extra=[an])
        add("N", None, [], [v("AW", LO, LO + 64)], 0, sig=("k1", (len(e2) - h) * (t + 1)), lat=P["net"], extra=[an])
        o = ps(4, 0, 128)
        mm([(o, cf(FI), L), (o, cb(NI256), v("metaB")), (o, cb(C2304), v("ONES", 0, 128))])
        mm([(ps(7, 0, 128), cb(ID), v("tB", 0, 128)), (ps(7, 0, 128), v("SG", 128, 256), cb(NDG))], True, False)
        mm([(ps(7, k, 128, 16), v("Fq", k, 2048, 16), v("G8", 8, 16)) for k in range(15)], False, False)
        for k in range(P["MH"]):
            tt(v("Mx", 128 * k, 128 * k + 64), v("Fq", k, 1024, 16), ps(4, 0, 64), A.max)
        for k in range(15):
            lo = 64 if k < P["MH"] else 0
            tt(v("Mx", 128 * k + lo, 128 * k + 128), v("Fq", k + 16 * lo, 2048, 16), ps(4, lo, 128), A.max)
            if k % 3 == 2:
                mm([(ps(7, i, 128, 16), v("Mx", 128 * i, 128 * i + 128), v("G8", 16, 24)) for i in range(k - 2, k + 1)], False, k == 14)
        mm([(ps(6, 256, 384), cb(RNB), v("metaB")), (ps(6, 256, 384), cb(BO), v("CN"))])
        act(v("nmS"), ps(6, 256, 384), bias=-12480.0)
        tt(v("eqB"), ind(v("x"), v("AQ", 0, 8)), v("nmS"), A.is_equal)
        mm([(ps(6, 384, 512), cb(LT), v("eqB"))])
        act(v("mA"), ps(6, 384, 512))
        mm([(ps(6, 128, 256), cb(ID), v("OD", 0, 128)), (ps(6, 128, 256), cb(ID), v(gb))])
        scan(v("gw"), v("RS", 0, 128), ps(6, 128, 256), A.add, A.max)
        tt(v("Dif"), v("Wf", 15, 384, 16), v("DUM"), A.subtract)
        nl = 3 if t < RO - 1 else 2
        for j in range(nl):
            tt(v("L3f", 8 * j, 8 * j + 8), v("Dif", 8 * j, 8 * j + 8), v("gw", 15, 128, 16), A.mult)
        tt(v("L3f", 0, 8 * nl), v("L3f", 0, 8 * nl), v("DUM", 0, 8 * nl), A.add)
        cp(v("L3", 0, 8 * nl), v("L3f", 0, 8 * nl))
        scan(v("pm"), v("RST"), ps(7, 0, 128), A.add, A.min)
        for j in range(8):
            o, i, m = v("mT", 16 * j, 16 * j + 16), v("pm", 16 * j, 16 * j + 16), v("pm", 16 * j + 15, 16 * j + 16)
            if j < P["mTS"]:
                act(o, i, AF.Sign, bias=m, scale=-1.0)
            else:
                ts(o, i, m, A.is_equal, 1.0, A.subtract)
        if P["DQ"]:
            mm([(ps(6, 0, 128), cb(ID), v("ONES", 0, 128)), (ps(6, 0, 128), v("mT"), cb(ID))])
        else:
            mm([(ps(6, 0, 128), v("mT"), cb(ID))])
            act(v("mQ"), ps(6, 0, 128), bias=1.0)
        bq = 1 - bank if P["DQ"] else 4
        o = ps(bq, 128, 256)
        mm([(o, cb(RN128), v("metaB")), (o, cb(B128), v("CN")), (o, cb(CTB), v("ONES", 0, 128))], True, False)
        mm([(ps(5, 128, 256), cb(E15), v("ONES", 0, 128))], True, False)
        if P["Y1"]:
            act(v("Yaq"), ind(v("Y"), v("AQ", 0, 16)))
        else:
            act(v("Yaq", 128, 256), ind(v("Y"), v("AQ", 8, 16)))
            act(v("Yaq", 0, 128), ind(v("Y"), v("AQ", 0, 8)))
        mm([(o, cf(FI), v("Yaq", 128, 256))], False, True)
        mm([(ps(5, 128, 256), cf(FDI), v("Yaq", 0, 128))], False, True)
        if P["DQ"]:
            act(v("Dq"), o)
            tt(v("Aq"), ps(6, 0, 128), v("Dq"), A.mult)
        else:
            tt(v("Aq"), o, v("mQ"), A.mult)
        mm([(ps(7, 128, 256), cf(FSI), v("Aq"))])
        act(v("Yn"), ps(7, 128, 256))
        if P["TV"]:
            act(v("dmS"), dm)
            tt(v("tm2"), ind(v("AW"), v("offW")), v("dmS"), A.mult)
            dm = v("tm2")
        else:
            act(v("tm2"), ind(v("AW"), v("offW")))
            tt(dm, v("tm2"), dm, A.mult)
        tt(v("ta"), ps(5, 128, 256), v("mA"), A.mult)
        edits = [lambda: tt(ind(v("Y"), v("L3", 0, 8)), v("ta"), v("Yaq", 0, 128), A.add),
                 lambda: tt(ind(v("Y"), v("L3", 8, 16)), v("Yn"), v("Yaq", 128, 256), A.add)]
        edits.insert(P["rl"], lambda: tt(Y, Y, dm, A.add))
        if P["rl"] == 2 and t < RO - 1:
            edits.insert(2, taken)
        for f in edits:
            f()
        if t < RO - 1:
            act(v("SW%d" % (t + 1), LO, LO + 64), v("ONES", 0, 64), scale=col(DLO))
            act(v("SW%d" % (t + 1), HI, HI + 64), v("ONES", 0, 64), scale=col(DHI))
            act(v("qF"), v("R", 1, 256, 2), scale=64.0)
            if P["ivS"]:
                ops[act(ind(v("inv", 0, 4232), v("L3", 16, 24)), v("qF"), AF.Silu)]["up"] = 1200.0
            else:
                cp(ind(v("inv", 0, 4232), v("L3", 16, 24)), v("qF"))

    now[0] = RO
    for lo in (0, 128):
        s = lambda nm: v(nm, lo, lo + 128)
        ts(s("Yi"), s("Y"), 1048448.0, A.min, 128.0, A.add)
        ts(s("xt"), s("Yi"), 7, A.logical_shift_right, 8191, A.bitwise_and)
        ts(s("o2"), s("xt"), -1.0, A.add)
        ts(s("w"), s("Yi"), 1, A.logical_shift_right, 63, A.bitwise_and)
        cp(s("o3"), s("w"))
    dma("S", T.yl[:], T.o2[:], [v("o2")], [], "d6", 2200)
    dma("Y", T.yz[:], T.o3[:], [v("o3")], [], "d7", 2200)
    act(v("vB"), Y, AF.Sign, bias=524288.0, scale=-1.0)
    mm([(v("PS0", 0, 256, 1, 8), v("G8", 0, 8), v("vB"))])
    act(v("o4", 0, 256, 1, 8), v("PS0", 0, 256, 1, 8), bias=8.0, scale=0.5)
    dma("S", T.yn[:], T.o4[0:8, :], [v("o4")], [], "d5", 2000)
    return ops, 2 * RO * len(e2)


def schedule(ops):
    total, seen, part, hint = 0.0, {}, {}, None
    for t in (1, 2, 3, 0):
        idx = [i for i, o in enumerate(ops) if min(o["t"], RO - 1) == t]
        tags = tuple(ops[i]["tag"] for i in idx)
        if tags not in seen:
            sub = [dict(ops[i], deps={j - idx[0]: w for j, w in ops[i]["deps"].items() if j >= idx[0]}) for i in idx]
            seen[tags] = arrange(sub, P["it"] // (1, 1, 1, 4)[t], hint)
            hint = hint or {tags[i]: s for i, s in seen[tags][0]}
        part[t] = [(idx[0] + i, s) for i, s in seen[tags][0]]
        total += seen[tags][1]
    return sum((part[t] for t in range(RO)), []), total


def arrange(ops, its, hint=None):
    n = len(ops)
    cost = [o["cost"] for o in ops]
    eng = [o["eng"] for o in ops]
    pre = [[(j, cost[j] + (ops[j]["lat"] + (P["self"] if eng[j] == eng[i] else P["hop"]) if w else 0.0)) for j, w in ops[i]["deps"].items()] for i in range(n)]
    for i in range(n):
        far = set()
        for j, d in pre[i]:
            if d > cost[j]:
                far.update(ops[j]["deps"])
        pre[i] = [(j, d) for j, d in pre[i] if j not in far or ops[j]["lat"] > 100]
    lat = [o["lat"] - o["up"] for o in ops]
    post = [[] for _ in range(n)]
    for i in range(n):
        for j, d in pre[i]:
            post[j].append((i, d + cost[i] - cost[j]))

    def place(order, edges, first):
        st = [0.0] * n
        busy = {e: [] for e in set(eng)}
        for i in order:
            s = first[i]
            for j, d in edges[i]:
                if st[j] + d > s:
                    s = st[j] + d
            if eng[i] != "N":
                b = busy[eng[i]]
                c = cost[i]
                k = len(b)
                while k > 0 and b[k - 1][1] > s:
                    k -= 1
                while k < len(b) and b[k][0] < s + c:
                    s = b[k][1]
                    k += 1
                b.insert(k, (s, s + c))
            st[i] = s
        return st
    zero = [0.0] * n
    cases = []
    for f, gc, sc, pe, call, hop, net in P["cases"]:
        c = [(o["cost"] + P["cyc"] * (o["g"] * (gc - P["g"]) + o["sc"] * (sc - P["sc"]))) * f * (pe if o["eng"] == "P" else 1.0) + call * (o["eng"] in "VS")
             for o in ops]
        e = [[(j, c[j] + ((d > cost[j]) and hop + ops[j]["lat"] * (net if eng[j] == "N" else net ** 0.4 if ops[j]["sig"] else 1.0))) for j, d in pre[i]] for i in range(n)]
        cases.append((c, e, f))

    cases.insert(0, (cost, pre, 1.0))

    def play(order):
        z, runs = [], []
        for c, e, f in cases:
            s2, why, last, free = [0.0] * n, [-1] * n, {}, dict.fromkeys(eng, 0.0)
            for i in order:
                q = eng[i]
                s = free[q]
                y = -2 - last[q] if q in last else -1
                for j, d in e[i]:
                    if s2[j] + d >= s:
                        s, y = s2[j] + d, j
                s2[i], why[i] = s, y
                if q != "N":
                    free[q], last[q] = s + c[i], i
            i = max(range(n), key=lambda i: s2[i] + c[i] + lat[i])
            z.append((s2[i] + c[i] + lat[i]) / f)
            runs.append((s2, why, i))
        return (sum(z) + z[0]) / (len(z) + 1), order, runs, z
    by = lambda st: sorted(range(n), key=lambda i: (st[i], i))
    key = [0.0] * n
    for i in range(n - 1, -1, -1):
        for j, d in pre[i]:
            key[j] = max(key[j], key[i] + d + 1e-3)
    best = cur = play(by(place(sorted(range(n), key=lambda i: (-key[i], i)), pre, zero)))
    for t0 in range(0, 16000, 2000) if hint else ():
        for i in range(n):
            key[i] = max([t0 + hint[ops[i]["tag"]] if ops[i]["tag"] in hint else cur[2][0][0][i] * (t0 > 0)] + [key[j] for j, d in pre[i]])
        best = min(best, play(by(key)), play(by(place(by(key), pre, zero))))
    cur = best
    seed = [P["seed"]]

    def draw(m):
        seed[0] = (seed[0] * 1103515245 + 12345) % 2147483648
        return (seed[0] >> 8) % m
    for it in range(its):
        kind = draw(16)
        st = cur[2][0][0]
        if kind < P["jb"]:
            back = place(sorted(range(n), key=lambda i: (-st[i] - cost[i], -i)), post, lat)
            key = [-back[i] - cost[i] for i in range(n)]
        elif kind < P["pm"]:
            key = list(st)
        else:
            key = [0.0] * n
            for k, i in enumerate(cur[1]):
                key[i] = 50.0 * k
        held, (_, why, i) = [], cur[2][draw(len(cases))]
        while i != -1:
            y = why[i]
            if y < -1:
                y = -2 - y
                held.append((i, y))
            i = y
        i, y = held[draw(len(held))]
        far = draw(P["rnd"]) * draw(2)
        if draw(2):
            key[i] = key[y] - 1 - far
        else:
            key[y] = key[i] + 1 + far
            for a in range(y, n):
                for j, d in post[a]:
                    if key[j] < key[a]:
                        key[j] = key[a]
        for i in range(n - 1, -1, -1):
            for j, d in pre[i]:
                if key[i] < key[j]:
                    key[j] = key[i]
        new = play(by(place(by(key), pre, zero)) if kind < P["pm"] else by(key))
        if new[0] <= cur[0] + P["tol"] * (1.0 - it / its):
            cur = new
            if new[0] < best[0]:
                best = new
    PLAN["ends"] = best[3]
    return [(i, best[2][0][0][i]) for i in best[1]], best[0]


def rank_program(g, core, T, topo):
    if T.rank_of(core) is None:
        return
    ops, nls = build(g, core, T, topo)
    if "order" not in PLAN:
        PLAN["order"] = schedule(ops)[0]
    q = {"V": g.vector, "S": g.scalar, "P": g.tensor, "G": g, "Y": g.sync}
    cnt = {"V": 0, "S": 0, "P": 0, "G": 0}
    known = {k: {} for k in q}
    clock = {}
    sig = {}
    for i, _ in PLAN["order"]:
        o = ops[i]
        e = o["eng"]
        if e == "N":
            sig[i] = o["sig"]
            clock[i] = {}
            continue
        kn = known[e]
        need = {}
        for j, w in o["deps"].items():
            if w and sig[j] != "none":
                need[sig[j][0]] = max(need.get(sig[j][0], (0, 0)), (sig[j][1], j))
        for s, (val, j) in sorted(need.items(), key=lambda z: -z[1][1]):
            if kn.get(s, 0) < val:
                q[e].wait_ge(T.sem[s], val)
                kn[s] = val
                for s2, v2 in clock[j].items():
                    kn[s2] = max(kn.get(s2, 0), v2)
        r = o["fn"]()
        if o["sig"] is None:
            cnt[e] += 1
            r.then_inc(T.sem["c" + e], 1)
            sig[i] = ("c" + e, cnt[e])
        else:
            sig[i] = o["sig"]
        clock[i] = dict(kn)
    for e in cnt:
        g.wait_ge(T.sem["c" + e], cnt[e])
    g.wait_ge(T.sem.ls, nls)
    for s in ("d5", "d6", "d7"):
        g.wait_ge(T.sem[s], 16)
